import numpy as np
import ml_dtypes


def mxq(x, axis, fmt="e4m3"):
    dtype, down = {"e4m3": (ml_dtypes.float8_e4m3fn, 7), "e5m2": (ml_dtypes.float8_e5m2, 14)}[fmt]
    v = np.moveaxis(np.asarray(x, np.float32).astype(ml_dtypes.bfloat16).astype(np.float64), axis, -1)
    blocks = v.reshape(v.shape[:-1] + (-1, 32))
    amax = np.abs(blocks).max(-1, keepdims=True)
    byte = np.maximum(np.where(amax > 0, np.frexp(amax)[1] - 1 + 127, 0) - down, 1)
    scale = np.exp2(byte - 127.0)
    codes = (blocks / scale).astype(np.float32).astype(dtype).astype(np.float64)
    return np.moveaxis((codes * scale).reshape(v.shape), -1, axis)


WIDE = False


def mx_kscale(k):
    if not WIDE:
        return np.ones(k)
    levels = np.array([10, -10, 5, -5, 0])
    if k % 512:
        return np.exp2(np.random.permutation(np.resize(levels, k // 32))).repeat(32)
    a = np.empty((k // 512, 16))
    for p in range(k // 512):
        a[p, :8] = np.random.permutation(np.resize(levels, 8))
        for g in range(8):
            far = levels[np.abs(levels - a[p, g]) >= 10]
            a[p, g + 8] = far[np.random.randint(len(far))]
    return np.exp2(a.ravel()).repeat(32)


BF16 = ml_dtypes.bfloat16


def bf(x):
    return np.asarray(x, np.float32).astype(BF16)


def f64(x):
    return np.asarray(x).astype(np.float64)


T, D, F = 4096, 1024, 256


def erf(u):
    c = np.clip(u, -6.0, 6.0)
    q = 2.0 * c * c
    term = np.array(c)
    total = np.array(c)
    for n in range(1, 151):
        term *= q / (2 * n + 1)
        total += term
    return np.where(np.abs(u) > 6.0, np.sign(u), 2.0 / np.sqrt(np.pi) * np.exp(-c * c) * total)


def gelu_erf_grad(a):
    cdf = 0.5 * (1.0 + erf(a / np.sqrt(2.0)))
    pdf_term = a * np.exp(-np.square(a) / 2.0) / np.sqrt(2.0 * np.pi)
    return cdf + pdf_term


def frobenius(z):
    return np.sqrt(np.sum(np.square(z), axis=(0, 1)))


def draw0():
    s, t = mx_kscale(D), mx_kscale(T)
    return {
        "x": bf(np.random.standard_normal((T, D)) / t[:, None]),
        "a": bf(np.random.standard_normal((T, F))),
        "dy": bf(np.random.standard_normal((T, D)) * s[None, :] * t[:, None]),
        "w2": bf(np.random.standard_normal((F, D)) / np.sqrt(D) / s[None, :]),
        "w1": bf(np.random.standard_normal((D, F))),
        "m": bf(np.random.standard_normal((D, F)) * 0.3),
        "v": bf(np.random.uniform(0.2, 1.0, (D, F))),
    }


def core(x, a, dy, w2, w1, m, v):
    x, a, dy, w2, w1, m, v = f64(x), f64(a), f64(dy), f64(w2), f64(w1), f64(m), f64(v)
    tokens = x.shape[0]
    dh = mxq(dy, 1, "e4m3") @ mxq(w2, 1, "e4m3").T
    da = dh * gelu_erf_grad(a)
    g = (mxq(x, 0, "e4m3").T @ mxq(da, 0, "e4m3")) / np.sqrt(tokens)
    m_new = 0.6 * m + 0.4 * g
    v_new = 0.6 * v + 0.4 * np.square(g)
    r = m_new / np.sqrt(v_new) + 0.1 * w1
    trust = frobenius(w1) / frobenius(r)
    return w1 - 0.5 * trust * r


def e4m3fn_bytes(y):
    return np.clip(np.asarray(y, np.float64), -448.0, 448.0).astype(np.float32).astype(ml_dtypes.float8_e4m3fn).view(np.uint8)


def e4m3fn_values(b):
    return np.asarray(b, np.uint8).view(ml_dtypes.float8_e4m3fn).astype(np.float64)


def setup_inputs():
    d = draw0()
    x0 = np.asarray(d['x']).astype(np.float64)
    s = (np.max(np.abs(x0), axis=(1,), keepdims=True) / 448.0).astype(np.float32)
    out = {}
    for k, v in d.items():
        if k == 'x':
            out['x_bytes'] = e4m3fn_bytes(x0 / s.astype(np.float64))
            out['x_scale'] = s
        else:
            out[k] = v
    return out


def reference(x_bytes, x_scale, a, dy, w2, w1, m, v):
    return core(e4m3fn_values(x_bytes) * x_scale.astype(np.float64), a, dy, w2, w1, m, v)

@@ -1,0 +1,420 @@
+from contextlib import ExitStack
+
+import concourse.mybir as mybir
+from concourse.masks import make_identity
+
+F32 = mybir.dt.float32
+BF16 = mybir.dt.bfloat16
+U32 = mybir.dt.uint32
+U8 = mybir.dt.uint8
+FP8 = mybir.dt.float8_e4m3fn
+FP8X4 = mybir.dt.float8_e4m3fn_x4
+MULT = mybir.AluOpType.mult
+ADD = mybir.AluOpType.add
+SUB = mybir.AluOpType.subtract
+MAX = mybir.AluOpType.max
+MIN = mybir.AluOpType.min
+ACT = mybir.ActivationFunctionType
+
+T, D, F = 4096, 1024, 256
+FLOPS = 4 * T * D * F
+
+P = 128
+NG = T // 512
+NC = D // 512
+NJ = D // P
+H = 1.5 * 2.0 ** -11
+LIVE = 3
+
+
+VC = 768
+
+
+def tile_lambmlpbackwardstep_t_kernel(tc, x_bytes, x_scale, a, dy, w2, w1, m, v, out):
+    nc = tc.nc
+    with ExitStack() as ctx:
+        keep = ctx.enter_context(tc.tile_pool(name="keep", bufs=1))
+        pool = ctx.enter_context(tc.tile_pool(name="work", bufs=2))
+        psum = ctx.enter_context(tc.psum_pool(name="psum", bufs=1))
+        ctx.enter_context(tc.manual_schedule())
+
+        ident = keep.tile([P, P], F32, name="ident")
+        ones = keep.tile([P, P], F32, name="ones")
+        ident_h = keep.tile([P, P], BF16, name="ident_h")
+        offs = keep.tile([P, 4], F32, name="offs")
+        warm = keep.tile([P, 2], F32, name="warm")
+        xs = keep.tile([P, NG, 4], F32, name="xs")
+        xq = keep.tile([P, NG, D], U32, name="xq", align_bytes=64)
+        xqs = keep.tile([P, NG, D], U8, name="xqs", align_bytes=64)
+        daq = keep.tile([P, NG, F], U32, name="daq", align_bytes=64)
+        daqs = keep.tile([P, NG, F], U8, name="daqs", align_bytes=64)
+        w2r = keep.tile([P, 2, D], BF16, name="w2r", align_bytes=64)
+        w2g = keep.tile([P, NC * F * 4], BF16, name="w2g", align_bytes=64)
+        w2q = keep.tile([P, NC, F], U32, name="w2q", align_bytes=64)
+        w2qs = keep.tile([P, NC, F], U8, name="w2qs", align_bytes=64)
+        w1t = keep.tile([P, NJ, F], BF16, name="w1t")
+        mt = keep.tile([P, NJ, F], BF16, name="mt")
+        vt = keep.tile([P, NJ, F], BF16, name="vt")
+        sq = keep.tile([P, NJ, F], F32, name="sq")
+        mn = keep.tile([P, NJ, F], F32, name="mn")
+        stats = keep.tile([P, 8], F32, name="stats")
+        small = keep.tile([P, 8], F32, name="small")
+        wsum = keep.tile([P, 8], F32, name="wsum")
+        junk = keep.tile([P, 2, F], BF16, name="junk")
+
+        gbank = [psum.tile([P, 512], F32, name=f"g{j}", tag=f"g{j}", bufs=1) for j in range(LIVE)]
+
+        a_v = a.rearrange("(g p t) f -> g p t f", p=P, t=4)
+        dy_v = dy.rearrange("(g p t) d -> g p t d", p=P, t=4)
+        x_v = x_bytes.rearrange("(g p t) d -> g p t d", p=P, t=4)
+
+        at, dyt, x8, ac, g3, g6, g2, dyg, dyq, dyqs, dh, da, xp, xi, tp, xw, wb = ({} for k in range(17))
+
+        def load_a(i):
+            at[i] = pool.tile([P, 4 * F], BF16, name=f"a{i}", tag="a", bufs=3)
+            nc.sync.dma_start(out=at[i][:].rearrange("p (t f) -> p t f", t=4), in_=a_v[i])
+
+        def load_dy(i):
+            dyt[i] = pool.tile([P, 4, D], BF16, name=f"dy{i}", tag="dy", bufs=3)
+            nc.sync.dma_start(out=dyt[i][:], in_=dy_v[i])
+
+        def load_x(i):
+            x8[i] = pool.tile([P, 4, D], U8, name=f"x8_{i}", tag="x8", bufs=3)
+            nc.sync.dma_start(out=x8[i][:], in_=x_v[i])
+
+        def clamp(i):
+            ac[i] = pool.tile([P, 4 * F], BF16, name=f"ac{i}", tag="ac", bufs=2)
+            nc.vector.tensor_scalar(out=ac[i][:], in0=at[i][:], scalar1=7.0, scalar2=-7.0, op0=MIN, op1=MAX)
+
+        def gelu(i, nodes):
+            for n in nodes:
+                d, tag, k = ((g2, "g2", 0), (g3, "g3", 1), (g6, "g6", 2))[n]
+                d[i] = pool.tile([P, 4 * F], F32, name=f"{tag}_{i}", tag=tag, bufs=2)
+                nc.scalar.activation(out=d[i][:], in_=ac[i][:], func=ACT.Gelu, bias=offs[:, k : k + 1])
+
+        def fd1(i):
+            nc.vector.scalar_tensor_tensor(out=g3[i][:], in0=g2[i][:], scalar=-27.0 / 32, in1=g3[i][:], op0=MULT, op1=ADD)
+
+        def fd2(i):
+            nc.vector.scalar_tensor_tensor(out=g6[i][:], in0=g6[i][:], scalar=-5.0 / 32, in1=g3[i][:], op0=MULT, op1=ADD)
+
+        def transposes_pe(i, t):
+            tp[i, t] = psum.tile([P, NC, 2, P], F32, name=f"tp{i}_{t}", tag="tp", bufs=2)
+            words = dyt[i][:, t, :].bitcast(F32)
+            for c in range(NC):
+                for u in range(2):
+                    nc.tensor.transpose(tp[i, t][:, c, u, :], words[:, 256 * c + u : 256 * (c + 1) : 2], ident[:])
+
+        def copy_t(i, t):
+            if t == 0:
+                dyg[i] = pool.tile([P, 4, D], BF16, name=f"dyg{i}", tag="dyg", bufs=2, align_bytes=64)
+            dst = dyg[i][:, t, :].bitcast(F32).rearrange("q (c r u) -> q c r u", c=NC, u=2)
+            nc.scalar.copy(out=dst, in_=tp[i, t][:].rearrange("q c u r -> q c r u"))
+
+        def q_dy(i):
+            dyq[i] = pool.tile([P, 4, NC, P], U32, name=f"dyq{i}", tag="dyq", bufs=2, align_bytes=64)
+            dyqs[i] = pool.tile([P, 4, NC, P], U8, name=f"dyqs{i}", tag="dyqs", bufs=2, align_bytes=64)
+            for h in range(2):
+                s = slice(2 * h, 2 * h + 2)
+                nc.vector.quantize_mx(
+                    out=dyq[i][:, s].rearrange("p t c r -> p (t c r)").bitcast(FP8X4),
+                    scales=dyqs[i][:, s].rearrange("p t c r -> p (t c r)"),
+                    in_=dyg[i][:, s].rearrange("p t k -> p (t k)"),
+                )
+
+        def mm1(i, h):
+            dh[i, h] = psum.tile([P, 4, P], F32, name=f"dh{i}_{h}", tag="dh", bufs=2)
+            for t in range(4):
+                for c in range(NC):
+                    nc.tensor.matmul_mx(
+                        out=dh[i, h][:, t, :],
+                        lhsT=dyq[i][:, t, c, :].bitcast(FP8X4),
+                        lhsT_scale=dyqs[i][:, t, c, :],
+                        rhs=w2q[:, c, P * h : P * (h + 1)].bitcast(FP8X4),
+                        rhs_scale=w2qs[:, c, P * h : P * (h + 1)],
+                        start=(c == 0),
+                        stop=(c == NC - 1),
+                    )
+
+        def make_da(i, h):
+            if h == 0:
+                da[i] = pool.tile([P, F, 4], BF16, name=f"da{i}", tag="da", bufs=2, align_bytes=64)
+            s = slice(128 * h, 128 * (h + 1))
+            nc.vector.scalar_tensor_tensor(
+                out=da[i][:, s, :],
+                in0=g6[i][:].rearrange("p (t f) -> p f t", t=4)[:, s, :],
+                scalar=4.0 / (15.0 * H),
+                in1=dh[i, h][:].rearrange("p t f -> p f t"),
+                op0=MULT,
+                op1=MULT,
+            )
+
+        def q_da(i):
+            nc.vector.quantize_mx(
+                out=daq[:, i, :].bitcast(FP8X4), scales=daqs[:, i, :], in_=da[i][:].rearrange("p f t -> p (f t)")
+            )
+
+        def widen(i, t):
+            if t == 0:
+                xp[i] = pool.tile([P, 2, VC, 2], BF16, name=f"xp{i}", tag="xp", bufs=2)
+            nc.vector.tensor_scalar(
+                out=xp[i][:, t // 2, :, t % 2],
+                in0=x8[i][:, t, 0:VC].bitcast(FP8),
+                scalar1=xs[:, i, t : t + 1],
+                scalar2=None,
+                op0=MULT,
+            )
+
+        def widen_s(i, t):
+            if t == 0:
+                xw[i] = pool.tile([P, 4, D - VC], BF16, name=f"xw{i}", tag="xw", bufs=2)
+            nc.scalar.activation(out=xw[i][:, t, :], in_=x8[i][:, t, VC:D].bitcast(FP8), func=ACT.Copy, scale=xs[:, i, t : t + 1])
+
+        def pair_up(i, h):
+            if h == 0:
+                xi[i] = pool.tile([P, D * 4], BF16, name=f"xi{i}", tag="xi", bufs=2, align_bytes=64)
+            src = xp[i][:].rearrange("p a d e -> p (a d e)").bitcast(F32).rearrange("p (a d) -> p d a", a=2)
+            dst = xi[i][:].bitcast(F32).rearrange("p (d a) -> p d a", a=2)
+            s = slice(512 * h, min(512 * (h + 1), VC))
+            nc.scalar.copy(out=dst[:, s, :], in_=src[:, s, :])
+
+        def weave(i, c):
+            half = (D - VC) // 2
+            wb[i, c] = psum.tile([P, 4 * half], BF16, name=f"wb{i}_{c}", tag="wb", bufs=1)
+            step = half if half <= 128 else half // 2
+            for d in range(0, half, step):
+                col = half * c + d
+                nc.tensor.matmul(
+                    wb[i, c][:, 4 * d : 4 * (d + step)],
+                    lhsT=ident_h[:],
+                    rhs=xw[i][:, :, col : col + step].rearrange("p t d -> p d t"),
+                    start=True,
+                    stop=True,
+                )
+
+        def plane_up(i, c):
+            half = (D - VC) // 2
+            nc.scalar.copy(out=xi[i][:, 4 * (VC + half * c) : 4 * (VC + half * (c + 1))], in_=wb[i, c][:])
+
+        def q_x(i, h):
+            s = slice(512 * h, 512 * (h + 1))
+            nc.vector.quantize_mx(
+                out=xq[:, i, s].bitcast(FP8X4), scales=xqs[:, i, s], in_=xi[i][:, 2048 * h : 2048 * (h + 1)]
+            )
+
+        def mm2(i, js):
+            for j in js:
+                nc.tensor.matmul_mx(
+                    out=gbank[j][:, 0:F],
+                    lhsT=xq[:, i, P * j : P * (j + 1)].bitcast(FP8X4),
+                    lhsT_scale=xqs[:, i, P * j : P * (j + 1)],
+                    rhs=daq[:, i, :].bitcast(FP8X4),
+                    rhs_scale=daqs[:, i, :],
+                    start=(i == 0),
+                    stop=(i == NG - 1),
+                )
+
+        load_a(0)
+        nc.scalar.dma_start(out=xs[:], in_=x_scale.rearrange("(g p t) o -> p g (t o)", p=P, t=4))
+        load_x(0)
+        nc.sync.dma_start(out=w2r[:], in_=w2.rearrange("(h p) d -> p h d", p=P))
+        load_dy(0)
+        load_a(1)
+        load_x(1)
+        load_dy(1)
+        nc.vector.memset(warm[:], 1.0)
+        for k, n in enumerate((-2.0, 3.0, 6.0)):
+            nc.vector.memset(offs[:, k : k + 1], n * H)
+        nc.vector.memset(ones[:], 1.0)
+        nc.scalar.activation(out=warm[:, 0:1], in_=warm[:, 1:2], func=ACT.Gelu, bias=offs[:, 0:1])
+        make_identity(nc, ident[:])
+        nc.vector.tensor_copy(out=ident_h[:], in_=ident[:])
+        clamp(0)
+
+        def w2_transposes(h):
+            bank = psum.tile([P, NC, 2, P], F32, name=f"w2_{h}", tag="dh", bufs=2)
+            words = w2r[:, h, :].bitcast(F32)
+            for c in range(NC):
+                for u in range(2):
+                    nc.tensor.transpose(bank[:, c, u, :], words[:, 256 * c + u : 256 * (c + 1) : 2], ident[:])
+            return bank
+
+        def prep_w2(banks):
+            dst = w2g[:].bitcast(F32).rearrange("q (c f u) -> q c f u", c=NC, u=2)
+            for h in range(2):
+                nc.vector.tensor_copy(out=dst[:, :, P * h : P * (h + 1), :], in_=banks[h][:].rearrange("q c u r -> q c r u"))
+            nc.vector.quantize_mx(
+                out=w2q[:].rearrange("p c f -> p (c f)").bitcast(FP8X4), scales=w2qs[:].rearrange("p c f -> p (c f)"), in_=w2g[:]
+            )
+
+        def w1_norm(b):
+            s = slice(2 * b, 2 * b + 2)
+            nc.scalar.activation(out=junk[:], in_=w1t[:, s, :], func=ACT.Square, scale=0.5, accum_out=stats[:, b : b + 1])
+
+        for s in range(NG + 1):
+            if s + 2 < NG:
+                load_a(s + 2)
+                load_x(s + 2)
+                load_dy(s + 2)
+            if s == 2:
+                nc.sync.dma_start(out=w1t[:], in_=w1.rearrange("(j p) f -> p j f", p=P))
+            if s == 4:
+                nc.sync.dma_start(out=mt[:], in_=m.rearrange("(j p) f -> p j f", p=P))
+                nc.sync.dma_start(out=vt[:], in_=v.rearrange("(j p) f -> p j f", p=P))
+            if s == 0:
+                w2_banks = [w2_transposes(h) for h in range(2)]
+            if s == 0:
+                gelu(0, range(3))
+            if s < NG:
+                widen(s, 0)
+            if s < NG:
+                widen(s, 3)
+            if 2 <= s and s - 2 < NG - 1:
+                q_da(s - 2)
+            if 1 <= s:
+                fd1(s - 1)
+            if s < NG:
+                widen(s, 2)
+            if s < NG:
+                widen_s(s, 0)
+            if s < NG:
+                widen_s(s, 3)
+            if 0 < s < NG:
+                gelu(s, [1])
+            if s < NG:
+                widen_s(s, 1)
+            if 2 <= s and s - 2 < NG - 1:
+                mm2(s - 2, range(LIVE))
+            if s < NG:
+                transposes_pe(s, 0)
+            if 1 <= s:
+                q_dy(s - 1)
+            if 1 <= s:
+                mm1(s - 1, 0)
+            if 1 <= s:
+                mm1(s - 1, 1)
+            if s < NG:
+                widen_s(s, 2)
+            if s < NG:
+                weave(s, 0)
+            if s < NG:
+                copy_t(s, 0)
+            if s < NG:
+                widen(s, 1)
+            if s == 0:
+                prep_w2(w2_banks)
+            if 0 < s < NG:
+                gelu(s, [0])
+            if s < NG:
+                transposes_pe(s, 2)
+            if s < NG:
+                pair_up(s, 0)
+            if s < NG:
+                copy_t(s, 2)
+            if 1 <= s:
+                fd2(s - 1)
+            if s < NG:
+                transposes_pe(s, 1)
+            if s + 1 < NG:
+                clamp(s + 1)
+            if 1 <= s:
+                q_x(s - 1, 1)
+            if s < NG:
+                plane_up(s, 0)
+            if s < NG:
+                pair_up(s, 1)
+            if 1 <= s:
+                make_da(s - 1, 0)
+            if 1 <= s:
+                make_da(s - 1, 1)
+            if s < NG:
+                copy_t(s, 1)
+            if s < NG:
+                transposes_pe(s, 3)
+            if s < NG:
+                copy_t(s, 3)
+            if s < NG:
+                weave(s, 1)
+            if 0 < s < NG:
+                gelu(s, [2])
+            if s < NG:
+                plane_up(s, 1)
+            if 1 <= s:
+                q_x(s - 1, 0)
+            if s == NG - 1:
+                for b in range(4):
+                    w1_norm(b)
+                nc.scalar.activation(out=warm[:, 0:1], in_=warm[:, 1:2], func=ACT.Abs_reciprocal_sqrt)
+            if s == NG:
+                for j, tag in ((3, "wb"), (4, "tp"), (5, "tp")):
+                    gbank.append(psum.tile([P, 512], F32, name=f"g{j}", tag=tag, bufs=1 if tag == "wb" else 2))
+                    for i in range(NG - 1):
+                        mm2(i, [j])
+        q_da(NG - 1)
+        mm2(NG - 1, range(6))
+        for j in (6, 7):
+            gbank.append(psum.tile([P, 512], F32, name=f"g{j}", tag="dh", bufs=2))
+            for i in range(NG):
+                mm2(i, [j])
+        def moments(b):
+            for js, jv in ((2 * b, 2 * b + 1), (2 * b + 1, 2 * b)):
+                nc.scalar.activation(
+                    out=sq[:, js, :], in_=gbank[js][:, 0:F], func=ACT.Square, scale=(2.0 / 3.0) ** 0.5 / 64.0
+                )
+                nc.vector.scalar_tensor_tensor(
+                    out=mn[:, jv, :], in0=gbank[jv][:, 0:F], scalar=-2.0 / 3.0 / 64.0, in1=mt[:, jv, :], op0=MULT, op1=SUB
+                )
+            s = slice(2 * b, 2 * b + 2)
+            nc.gpsimd.tensor_tensor(out=sq[:, s, :], in0=sq[:, s, :], in1=vt[:, s, :], op=ADD)
+
+        def inv_root(b):
+            s = slice(2 * b, 2 * b + 2)
+            nc.scalar.activation(out=sq[:, s, :], in_=sq[:, s, :], func=ACT.Abs_reciprocal_sqrt, scale=1.0 / 0.6)
+
+        def ratio(b):
+            s = slice(2 * b, 2 * b + 2)
+            nc.vector.tensor_tensor(out=mn[:, s, :], in0=mn[:, s, :], in1=sq[:, s, :], op=MULT)
+
+        def decay(b):
+            s = slice(2 * b, 2 * b + 2)
+            nc.vector.scalar_tensor_tensor(out=mn[:, s, :], in0=w1t[:, s, :], scalar=-0.1, in1=mn[:, s, :], op0=MULT, op1=ADD)
+
+        def r_norm(b):
+            s = slice(2 * b, 2 * b + 2)
+            nc.scalar.activation(out=sq[:, s, :], in_=mn[:, s, :], func=ACT.Square, accum_out=stats[:, 4 + b : 5 + b])
+
+        moments(0)
+        moments(1)
+        tot = psum.tile([P, 8], F32, name="tot", tag="g0", bufs=1)
+        for b in range(4):
+            nc.tensor.matmul(tot[:, 1:2], lhsT=ones[:], rhs=stats[:, b : b + 1], start=(b == 0), stop=(b == 3))
+        moments(2)
+        inv_root(0)
+        moments(3)
+        inv_root(1)
+        ratio(0)
+        inv_root(2)
+        ratio(1)
+        decay(0)
+        r_norm(0)
+        inv_root(3)
+        ratio(2)
+        nc.vector.reciprocal(out=wsum[:, 0:1], in_=tot[:, 1:2])
+        decay(1)
+        r_norm(1)
+        ratio(3)
+        decay(2)
+        r_norm(2)
+        decay(3)
+        r_norm(3)
+        for b in range(4):
+            nc.tensor.matmul(tot[:, 0:1], lhsT=ones[:], rhs=stats[:, 4 + b : 5 + b], start=(b == 0), stop=(b == 3))
+        nc.scalar.activation(out=small[:, 0:1], in_=tot[:, 0:1], func=ACT.Abs_reciprocal_sqrt, scale=wsum[:, 0:1])
+        out_v = out.rearrange("(j p) f -> p j f", p=P)
+        for b in range(4):
+            s = slice(2 * b, 2 * b + 2)
+            res = pool.tile([P, 2, F], F32, name=f"res{b}", tag="res", bufs=4)
+            nc.vector.scalar_tensor_tensor(
+                out=res[:], in0=mn[:, s, :], scalar=small[:, 0:1], in1=w1t[:, s, :], op0=MULT, op1=ADD
+            )
+            nc.sync.dma_start(out=out_v[:, s, :], in_=res[:])

@@ -23,11 +23,13 @@ P = 128
 NG = T // 512
 NC = D // 512
 NJ = D // P
+NB = NJ // 2
 H = 1.5 * 2.0 ** -11
 LIVE = 3
-
-
-VC = 768
+WC = 384
+VC = D - WC
+WS = 3
+WN = 1
 
 
 def tile_lambmlpbackwardstep_t_kernel(tc, x_bytes, x_scale, a, dy, w2, w1, m, v, out):
@@ -42,7 +44,6 @@ def tile_lambmlpbackwardstep_t_kernel(tc, x_bytes, x_scale, a, dy, w2, w1, m, v,
         ones = keep.tile([P, P], F32, name="ones")
         ident_h = keep.tile([P, P], BF16, name="ident_h")
         offs = keep.tile([P, 4], F32, name="offs")
-        warm = keep.tile([P, 2], F32, name="warm")
         xs = keep.tile([P, NG, 4], F32, name="xs")
         xq = keep.tile([P, NG, D], U32, name="xq", align_bytes=64)
         xqs = keep.tile([P, NG, D], U8, name="xqs", align_bytes=64)
@@ -52,75 +53,92 @@ def tile_lambmlpbackwardstep_t_kernel(tc, x_bytes, x_scale, a, dy, w2, w1, m, v,
         w2g = keep.tile([P, NC * F * 4], BF16, name="w2g", align_bytes=64)
         w2q = keep.tile([P, NC, F], U32, name="w2q", align_bytes=64)
         w2qs = keep.tile([P, NC, F], U8, name="w2qs", align_bytes=64)
-        w1t = keep.tile([P, NJ, F], BF16, name="w1t")
-        mt = keep.tile([P, NJ, F], BF16, name="mt")
-        vt = keep.tile([P, NJ, F], BF16, name="vt")
-        sq = keep.tile([P, NJ, F], F32, name="sq")
-        mn = keep.tile([P, NJ, F], F32, name="mn")
-        stats = keep.tile([P, 8], F32, name="stats")
-        small = keep.tile([P, 8], F32, name="small")
+        w1t = keep.tile([P, NJ * F], BF16, name="w1t")
+        mt = keep.tile([P, NJ * F], BF16, name="mt")
+        vt = keep.tile([P, NJ * F], BF16, name="vt")
+        sq = keep.tile([P, NJ * F], F32, name="sq")
+        mn = keep.tile([P, NJ * F], F32, name="mn")
+        rsum = keep.tile([P, 8], F32, name="rsum")
         wsum = keep.tile([P, 8], F32, name="wsum")
-        junk = keep.tile([P, 2, F], BF16, name="junk")
+        winv = keep.tile([P, 8], F32, name="winv")
+        winv2 = keep.tile([P, 8], F32, name="winv2")
+        step = keep.tile([P, 8], F32, name="step")
 
-        gbank = [psum.tile([P, 512], F32, name=f"g{j}", tag=f"g{j}", bufs=1) for j in range(LIVE)]
+        gbank = []
 
         a_v = a.rearrange("(g p t) f -> g p t f", p=P, t=4)
         dy_v = dy.rearrange("(g p t) d -> g p t d", p=P, t=4)
         x_v = x_bytes.rearrange("(g p t) d -> g p t d", p=P, t=4)
 
-        at, dyt, x8, ac, g3, g6, g2, dyg, dyq, dyqs, dh, da, xp, xi, tp, xw, wb = ({} for k in range(17))
+        at, dyt, x8, ac, ge, dyg, dyq, dyqs, dh, da, xp, xi, tp, xw, wb = ({} for k in range(15))
 
         def load_a(i):
-            at[i] = pool.tile([P, 4 * F], BF16, name=f"a{i}", tag="a", bufs=3)
-            nc.sync.dma_start(out=at[i][:].rearrange("p (t f) -> p t f", t=4), in_=a_v[i])
+            at[i] = pool.tile([P, 4, F], BF16, name=f"a{i}", tag="a", bufs=3)
+            nc.sync.dma_start(out=at[i][:], in_=a_v[i])
 
-        def load_dy(i):
-            dyt[i] = pool.tile([P, 4, D], BF16, name=f"dy{i}", tag="dy", bufs=3)
-            nc.sync.dma_start(out=dyt[i][:], in_=dy_v[i])
+        def load_dy(i, u):
+            dyt[i, u] = pool.tile([P, 2, D], BF16, name=f"dy{i}_{u}", tag="dy", bufs=6)
+            nc.sync.dma_start(out=dyt[i, u][:], in_=dy_v[i][:, 2 * u : 2 * u + 2, :])
 
         def load_x(i):
             x8[i] = pool.tile([P, 4, D], U8, name=f"x8_{i}", tag="x8", bufs=3)
             nc.sync.dma_start(out=x8[i][:], in_=x_v[i])
 
+        def load_rows(dst, src):
+            nc.sync.dma_start(out=dst[:].rearrange("p (j f) -> p j f", f=F), in_=src.rearrange("(j p) f -> p j f", p=P))
+
+        def move(on_vector, dst, src):
+            if on_vector:
+                nc.vector.tensor_copy(out=dst, in_=src)
+            else:
+                nc.scalar.copy(out=dst, in_=src)
+
         def clamp(i):
-            ac[i] = pool.tile([P, 4 * F], BF16, name=f"ac{i}", tag="ac", bufs=2)
-            nc.vector.tensor_scalar(out=ac[i][:], in0=at[i][:], scalar1=7.0, scalar2=-7.0, op0=MIN, op1=MAX)
+            ac[i] = pool.tile([P, F, 4], BF16, name=f"ac{i}", tag="ac", bufs=2)
+            nc.vector.tensor_scalar(
+                out=ac[i][:].rearrange("p (c e) t -> p c t e", e=4),
+                in0=at[i][:].rearrange("p t (c e) -> p c t e", e=4),
+                scalar1=7.0,
+                scalar2=-7.0,
+                op0=MIN,
+                op1=MAX,
+            )
 
-        def gelu(i, nodes):
-            for n in nodes:
-                d, tag, k = ((g2, "g2", 0), (g3, "g3", 1), (g6, "g6", 2))[n]
-                d[i] = pool.tile([P, 4 * F], F32, name=f"{tag}_{i}", tag=tag, bufs=2)
-                nc.scalar.activation(out=d[i][:], in_=ac[i][:], func=ACT.Gelu, bias=offs[:, k : k + 1])
+        def gelu(i, k):
+            ge[i, k] = pool.tile([P, 4 * F], F32, name=f"ge{i}_{k}", tag=f"ge{k}", bufs=2)
+            nc.scalar.activation(
+                out=ge[i, k][:], in_=ac[i][:].rearrange("p f t -> p (f t)"), func=ACT.Gelu, bias=offs[:, k : k + 1]
+            )
 
-        def fd1(i):
-            nc.vector.scalar_tensor_tensor(out=g3[i][:], in0=g2[i][:], scalar=-27.0 / 32, in1=g3[i][:], op0=MULT, op1=ADD)
+        def diff(i, k, lo=0, hi=4 * F):
+            src, weight = ((0, -27.0 / 32), (2, -5.0 / 32))[k]
+            nc.vector.scalar_tensor_tensor(
+                out=ge[i, 1][:, lo:hi], in0=ge[i, src][:, lo:hi], scalar=weight, in1=ge[i, 1][:, lo:hi], op0=MULT, op1=ADD
+            )
 
-        def fd2(i):
-            nc.vector.scalar_tensor_tensor(out=g6[i][:], in0=g6[i][:], scalar=-5.0 / 32, in1=g3[i][:], op0=MULT, op1=ADD)
-
-        def transposes_pe(i, t):
-            tp[i, t] = psum.tile([P, NC, 2, P], F32, name=f"tp{i}_{t}", tag="tp", bufs=2)
-            words = dyt[i][:, t, :].bitcast(F32)
+        def turn(i, t, tag="tp", bufs=2):
+            tp[i, t] = psum.tile([P, NC, 2, P], F32, name=f"tp{i}_{t}", tag=tag, bufs=bufs)
+            words = dyt[i, t // 2][:, t % 2, :].bitcast(F32)
             for c in range(NC):
                 for u in range(2):
                     nc.tensor.transpose(tp[i, t][:, c, u, :], words[:, 256 * c + u : 256 * (c + 1) : 2], ident[:])
 
-        def copy_t(i, t):
+        def empty(i, t, on_vector=False):
             if t == 0:
                 dyg[i] = pool.tile([P, 4, D], BF16, name=f"dyg{i}", tag="dyg", bufs=2, align_bytes=64)
             dst = dyg[i][:, t, :].bitcast(F32).rearrange("q (c r u) -> q c r u", c=NC, u=2)
-            nc.scalar.copy(out=dst, in_=tp[i, t][:].rearrange("q c u r -> q c r u"))
+            move(on_vector, dst, tp[i, t][:].rearrange("q c u r -> q c r u"))
 
-        def q_dy(i):
-            dyq[i] = pool.tile([P, 4, NC, P], U32, name=f"dyq{i}", tag="dyq", bufs=2, align_bytes=64)
-            dyqs[i] = pool.tile([P, 4, NC, P], U8, name=f"dyqs{i}", tag="dyqs", bufs=2, align_bytes=64)
-            for h in range(2):
-                s = slice(2 * h, 2 * h + 2)
-                nc.vector.quantize_mx(
-                    out=dyq[i][:, s].rearrange("p t c r -> p (t c r)").bitcast(FP8X4),
-                    scales=dyqs[i][:, s].rearrange("p t c r -> p (t c r)"),
-                    in_=dyg[i][:, s].rearrange("p t k -> p (t k)"),
-                )
+        def q_dy(i, u):
+            if u == 0:
+                dyq[i] = pool.tile([P, 4, NC, P], U32, name=f"dyq{i}", tag="dyq", bufs=2, align_bytes=64)
+                dyqs[i] = pool.tile([P, 4, NC, P], U8, name=f"dyqs{i}", tag="dyqs", bufs=2, align_bytes=64)
+            s = slice(2 * u, 2 * u + 2)
+            nc.vector.quantize_mx(
+                out=dyq[i][:, s].rearrange("p t c r -> p (t c r)").bitcast(FP8X4),
+                scales=dyqs[i][:, s].rearrange("p t c r -> p (t c r)"),
+                in_=dyg[i][:, s].rearrange("p t k -> p (t k)"),
+            )
 
         def mm1(i, h):
             dh[i, h] = psum.tile([P, 4, P], F32, name=f"dh{i}_{h}", tag="dh", bufs=2)
@@ -138,11 +156,11 @@ def tile_lambmlpbackwardstep_t_kernel(tc, x_bytes, x_scale, a, dy, w2, w1, m, v,
 
         def make_da(i, h):
             if h == 0:
-                da[i] = pool.tile([P, F, 4], BF16, name=f"da{i}", tag="da", bufs=2, align_bytes=64)
-            s = slice(128 * h, 128 * (h + 1))
+                da[i] = pool.tile([P, 4 * F], BF16, name=f"da{i}", tag="da", bufs=2, align_bytes=64)
+            s = slice(512 * h, 512 * (h + 1))
             nc.vector.scalar_tensor_tensor(
-                out=da[i][:, s, :],
-                in0=g6[i][:].rearrange("p (t f) -> p f t", t=4)[:, s, :],
+                out=da[i][:, s].rearrange("p (f t) -> p f t", t=4),
+                in0=ge[i, 1][:, s].rearrange("p (f t) -> p f t", t=4),
                 scalar=4.0 / (15.0 * H),
                 in1=dh[i, h][:].rearrange("p t f -> p f t"),
                 op0=MULT,
@@ -150,11 +168,9 @@ def tile_lambmlpbackwardstep_t_kernel(tc, x_bytes, x_scale, a, dy, w2, w1, m, v,
             )
 
         def q_da(i):
-            nc.vector.quantize_mx(
-                out=daq[:, i, :].bitcast(FP8X4), scales=daqs[:, i, :], in_=da[i][:].rearrange("p f t -> p (f t)")
-            )
+            nc.vector.quantize_mx(out=daq[:, i, :].bitcast(FP8X4), scales=daqs[:, i, :], in_=da[i][:])
 
-        def widen(i, t):
+        def widen_pairs(i, t):
             if t == 0:
                 xp[i] = pool.tile([P, 2, VC, 2], BF16, name=f"xp{i}", tag="xp", bufs=2)
             nc.vector.tensor_scalar(
@@ -165,73 +181,59 @@ def tile_lambmlpbackwardstep_t_kernel(tc, x_bytes, x_scale, a, dy, w2, w1, m, v,
                 op0=MULT,
             )
 
-        def widen_s(i, t):
+        def widen_rows(i, t, on_vector=False):
             if t == 0:
-                xw[i] = pool.tile([P, 4, D - VC], BF16, name=f"xw{i}", tag="xw", bufs=2)
-            nc.scalar.activation(out=xw[i][:, t, :], in_=x8[i][:, t, VC:D].bitcast(FP8), func=ACT.Copy, scale=xs[:, i, t : t + 1])
+                xw[i] = pool.tile([P, 4, WC], BF16, name=f"xw{i}", tag="xw", bufs=2)
+            src = x8[i][:, t, VC:D].bitcast(FP8)
+            if on_vector:
+                nc.vector.tensor_scalar(out=xw[i][:, t, :], in0=src, scalar1=xs[:, i, t : t + 1], scalar2=None, op0=MULT)
+            else:
+                nc.scalar.activation(out=xw[i][:, t, :], in_=src, func=ACT.Copy, scale=xs[:, i, t : t + 1])
 
-        def pair_up(i, h):
-            if h == 0:
-                xi[i] = pool.tile([P, D * 4], BF16, name=f"xi{i}", tag="xi", bufs=2, align_bytes=64)
+        def new_xi(i):
+            xi[i] = pool.tile([P, D * 4], BF16, name=f"xi{i}", tag="xi", bufs=2, align_bytes=64)
+
+        def join_pairs(i, lo, hi, on_vector=False):
             src = xp[i][:].rearrange("p a d e -> p (a d e)").bitcast(F32).rearrange("p (a d) -> p d a", a=2)
-            dst = xi[i][:].bitcast(F32).rearrange("p (d a) -> p d a", a=2)
-            s = slice(512 * h, min(512 * (h + 1), VC))
-            nc.scalar.copy(out=dst[:, s, :], in_=src[:, s, :])
+            dst = xi[i][:, 0 : 4 * VC].bitcast(F32).rearrange("p (d a) -> p d a", a=2)
+            move(on_vector, dst[:, lo:hi, :], src[:, lo:hi, :])
 
-        def weave(i, c):
-            half = (D - VC) // 2
-            wb[i, c] = psum.tile([P, 4 * half], BF16, name=f"wb{i}_{c}", tag="wb", bufs=1)
-            step = half if half <= 128 else half // 2
-            for d in range(0, half, step):
+        def weave(i, c, tag="wb", bufs=1):
+            half = WC // 2
+            wb[i, c] = psum.tile([P, 4 * half], BF16, name=f"wb{i}_{c}", tag=tag, bufs=bufs)
+            for d in range(0, half, half // 2):
                 col = half * c + d
                 nc.tensor.matmul(
-                    wb[i, c][:, 4 * d : 4 * (d + step)],
+                    wb[i, c][:, 4 * d : 4 * (d + half // 2)],
                     lhsT=ident_h[:],
-                    rhs=xw[i][:, :, col : col + step].rearrange("p t d -> p d t"),
+                    rhs=xw[i][:, :, col : col + half // 2].rearrange("p t d -> p d t"),
                     start=True,
                     stop=True,
                 )
 
-        def plane_up(i, c):
-            half = (D - VC) // 2
-            nc.scalar.copy(out=xi[i][:, 4 * (VC + half * c) : 4 * (VC + half * (c + 1))], in_=wb[i, c][:])
+        def unweave(i, c, on_vector=False):
+            half = WC // 2
+            move(on_vector, xi[i][:, 4 * (VC + half * c) : 4 * (VC + half * (c + 1))].bitcast(F32), wb[i, c][:].bitcast(F32))
 
-        def q_x(i, h):
-            s = slice(512 * h, 512 * (h + 1))
+        def q_x(i, u):
+            s = slice(512 * u, 512 * (u + 1))
             nc.vector.quantize_mx(
-                out=xq[:, i, s].bitcast(FP8X4), scales=xqs[:, i, s], in_=xi[i][:, 2048 * h : 2048 * (h + 1)]
+                out=xq[:, i, s].bitcast(FP8X4), scales=xqs[:, i, s], in_=xi[i][:, 2048 * u : 2048 * (u + 1)]
             )
 
-        def mm2(i, js):
-            for j in js:
+        def mm2(i, b):
+            for j in (2 * b, 2 * b + 1):
                 nc.tensor.matmul_mx(
-                    out=gbank[j][:, 0:F],
+                    out=gbank[b][:, F * (j % 2) : F * (j % 2 + 1)],
                     lhsT=xq[:, i, P * j : P * (j + 1)].bitcast(FP8X4),
                     lhsT_scale=xqs[:, i, P * j : P * (j + 1)],
                     rhs=daq[:, i, :].bitcast(FP8X4),
                     rhs_scale=daqs[:, i, :],
-                    start=(i == 0),
-                    stop=(i == NG - 1),
+                    start=(i == 0 and j % 2 == 0),
+                    stop=(i == NG - 1 and j % 2 == 1),
                 )
 
-        load_a(0)
-        nc.scalar.dma_start(out=xs[:], in_=x_scale.rearrange("(g p t) o -> p g (t o)", p=P, t=4))
-        load_x(0)
-        nc.sync.dma_start(out=w2r[:], in_=w2.rearrange("(h p) d -> p h d", p=P))
-        load_dy(0)
-        load_a(1)
-        load_x(1)
-        load_dy(1)
-        nc.vector.memset(warm[:], 1.0)
-        for k, n in enumerate((-2.0, 3.0, 6.0)):
-            nc.vector.memset(offs[:, k : k + 1], n * H)
-        nc.vector.memset(ones[:], 1.0)
-        nc.scalar.activation(out=warm[:, 0:1], in_=warm[:, 1:2], func=ACT.Gelu, bias=offs[:, 0:1])
-        make_identity(nc, ident[:])
-        nc.vector.tensor_copy(out=ident_h[:], in_=ident[:])
-        clamp(0)
-
-        def w2_transposes(h):
+        def turn_w2(h):
             bank = psum.tile([P, NC, 2, P], F32, name=f"w2_{h}", tag="dh", bufs=2)
             words = w2r[:, h, :].bitcast(F32)
             for c in range(NC):
@@ -239,182 +241,239 @@ def tile_lambmlpbackwardstep_t_kernel(tc, x_bytes, x_scale, a, dy, w2, w1, m, v,
                     nc.tensor.transpose(bank[:, c, u, :], words[:, 256 * c + u : 256 * (c + 1) : 2], ident[:])
             return bank
 
-        def prep_w2(banks):
+        def empty_w2(h, bank):
             dst = w2g[:].bitcast(F32).rearrange("q (c f u) -> q c f u", c=NC, u=2)
-            for h in range(2):
-                nc.vector.tensor_copy(out=dst[:, :, P * h : P * (h + 1), :], in_=banks[h][:].rearrange("q c u r -> q c r u"))
+            nc.scalar.copy(out=dst[:, :, P * h : P * (h + 1), :], in_=bank[:].rearrange("q c u r -> q c r u"))
+
+        def q_w2():
             nc.vector.quantize_mx(
                 out=w2q[:].rearrange("p c f -> p (c f)").bitcast(FP8X4), scales=w2qs[:].rearrange("p c f -> p (c f)"), in_=w2g[:]
             )
 
-        def w1_norm(b):
-            s = slice(2 * b, 2 * b + 2)
-            nc.scalar.activation(out=junk[:], in_=w1t[:, s, :], func=ACT.Square, scale=0.5, accum_out=stats[:, b : b + 1])
+        load_a(0)
+        nc.scalar.dma_start(out=xs[:], in_=x_scale.rearrange("(g p t) o -> p g (t o)", p=P, t=4))
+        load_x(0)
+        load_dy(0, 0)
+        load_dy(0, 1)
+        nc.sync.dma_start(out=w2r[:], in_=w2.rearrange("(h p) d -> p h d", p=P))
+        load_a(1)
+        load_x(1)
+        load_dy(1, 0)
+        load_dy(1, 1)
+        for k, n in enumerate((-2.0, 3.0, 6.0)):
+            nc.vector.memset(offs[:, k : k + 1], n * H)
+        nc.vector.memset(ones[:], 1.0)
+        make_identity(nc, ident[:])
+        nc.vector.tensor_copy(out=ident_h[:], in_=ident[:])
+        clamp(0)
+        load_a(2)
+        load_x(2)
+        load_dy(2, 0)
+        load_dy(2, 1)
+        gelu(0, 0)
+        for t in range(4):
+            widen_rows(0, t, True)
+        weave(0, 0)
+        weave(0, 1, "g2")
+        turn(0, 0)
+        turn(0, 1)
+        turn(0, 2, "g0", 1)
+        turn(0, 3, "g1", 1)
+        w2_banks = [turn_w2(h) for h in range(2)]
+        gelu(0, 1)
+        for t in range(4):
+            widen_pairs(0, t)
+        new_xi(0)
+        unweave(0, 0, True)
+        gelu(0, 2)
+        join_pairs(0, 0, VC, True)
+        unweave(0, 1, True)
+        empty(0, 0)
+        diff(0, 0)
+        empty(0, 1)
+        turn(1, 0)
+        turn(1, 1)
+        clamp(1)
+        empty(0, 2)
+        diff(0, 1)
+        empty(0, 3)
+        q_x(0, 0)
+        empty_w2(0, w2_banks[0])
+        q_dy(0, 0)
+        empty_w2(1, w2_banks[1])
+        q_dy(0, 1)
+        q_w2()
+        for t in range(4 - WS):
+            widen_rows(1, t, True)
+        for t in range(4):
+            widen_pairs(1, t)
+        for b in range(LIVE):
+            gbank.append(psum.tile([P, 2 * F], F32, name=f"g{b}", tag=f"g{b}", bufs=1))
 
-        for s in range(NG + 1):
+        last = NG - 1
+        for s in range(1, last):
             if s + 2 < NG:
                 load_a(s + 2)
                 load_x(s + 2)
-                load_dy(s + 2)
-            if s == 2:
-                nc.sync.dma_start(out=w1t[:], in_=w1.rearrange("(j p) f -> p j f", p=P))
-            if s == 4:
-                nc.sync.dma_start(out=mt[:], in_=m.rearrange("(j p) f -> p j f", p=P))
-                nc.sync.dma_start(out=vt[:], in_=v.rearrange("(j p) f -> p j f", p=P))
-            if s == 0:
-                w2_banks = [w2_transposes(h) for h in range(2)]
-            if s == 0:
-                gelu(0, range(3))
-            if s < NG:
-                widen(s, 0)
-            if s < NG:
-                widen(s, 3)
-            if 2 <= s and s - 2 < NG - 1:
-                q_da(s - 2)
-            if 1 <= s:
-                fd1(s - 1)
-            if s < NG:
-                widen(s, 2)
-            if s < NG:
-                widen_s(s, 0)
-            if s < NG:
-                widen_s(s, 3)
-            if 0 < s < NG:
-                gelu(s, [1])
-            if s < NG:
-                widen_s(s, 1)
-            if 2 <= s and s - 2 < NG - 1:
-                mm2(s - 2, range(LIVE))
-            if s < NG:
-                transposes_pe(s, 0)
-            if 1 <= s:
-                q_dy(s - 1)
-            if 1 <= s:
-                mm1(s - 1, 0)
-            if 1 <= s:
-                mm1(s - 1, 1)
-            if s < NG:
-                widen_s(s, 2)
-            if s < NG:
-                weave(s, 0)
-            if s < NG:
-                copy_t(s, 0)
-            if s < NG:
-                widen(s, 1)
-            if s == 0:
-                prep_w2(w2_banks)
-            if 0 < s < NG:
-                gelu(s, [0])
-            if s < NG:
-                transposes_pe(s, 2)
-            if s < NG:
-                pair_up(s, 0)
-            if s < NG:
-                copy_t(s, 2)
-            if 1 <= s:
-                fd2(s - 1)
-            if s < NG:
-                transposes_pe(s, 1)
-            if s + 1 < NG:
-                clamp(s + 1)
-            if 1 <= s:
-                q_x(s - 1, 1)
-            if s < NG:
-                plane_up(s, 0)
-            if s < NG:
-                pair_up(s, 1)
-            if 1 <= s:
-                make_da(s - 1, 0)
-            if 1 <= s:
-                make_da(s - 1, 1)
-            if s < NG:
-                copy_t(s, 1)
-            if s < NG:
-                transposes_pe(s, 3)
-            if s < NG:
-                copy_t(s, 3)
-            if s < NG:
-                weave(s, 1)
-            if 0 < s < NG:
-                gelu(s, [2])
-            if s < NG:
-                plane_up(s, 1)
-            if 1 <= s:
-                q_x(s - 1, 0)
-            if s == NG - 1:
-                for b in range(4):
-                    w1_norm(b)
-                nc.scalar.activation(out=warm[:, 0:1], in_=warm[:, 1:2], func=ACT.Abs_reciprocal_sqrt)
-            if s == NG:
-                for j, tag in ((3, "wb"), (4, "tp"), (5, "tp")):
-                    gbank.append(psum.tile([P, 512], F32, name=f"g{j}", tag=tag, bufs=1 if tag == "wb" else 2))
-                    for i in range(NG - 1):
-                        mm2(i, [j])
-        q_da(NG - 1)
-        mm2(NG - 1, range(6))
-        for j in (6, 7):
-            gbank.append(psum.tile([P, 512], F32, name=f"g{j}", tag="dh", bufs=2))
-            for i in range(NG):
-                mm2(i, [j])
-        def moments(b):
-            for js, jv in ((2 * b, 2 * b + 1), (2 * b + 1, 2 * b)):
-                nc.scalar.activation(
-                    out=sq[:, js, :], in_=gbank[js][:, 0:F], func=ACT.Square, scale=(2.0 / 3.0) ** 0.5 / 64.0
-                )
-                nc.vector.scalar_tensor_tensor(
-                    out=mn[:, jv, :], in0=gbank[jv][:, 0:F], scalar=-2.0 / 3.0 / 64.0, in1=mt[:, jv, :], op0=MULT, op1=SUB
-                )
-            s = slice(2 * b, 2 * b + 2)
-            nc.gpsimd.tensor_tensor(out=sq[:, s, :], in0=sq[:, s, :], in1=vt[:, s, :], op=ADD)
+                load_dy(s + 2, 0)
+                load_dy(s + 2, 1)
+            if s == 1:
+                load_rows(w1t, w1)
+            if s == 5:
+                load_rows(mt, m)
+                load_rows(vt, v)
+            rows_v = 4 if s + 1 == last else 4 - WS
+            empty(s, 0)
+            turn(s, 2)
+            empty(s, 1)
+            turn(s, 3)
+            if s == 1:
+                mm1(0, 0)
+                mm1(0, 1)
+                make_da(0, 0)
+                make_da(0, 1)
+                q_x(0, 1)
+                q_da(0)
+            for t in range(4 - WS, 4):
+                widen_rows(s, t)
+            weave(s, 0)
+            empty(s, 2)
+            turn(s + 1, 0)
+            q_dy(s, 0)
+            empty(s, 3)
+            turn(s + 1, 1)
+            q_dy(s, 1)
+            gelu(s, 0)
+            new_xi(s)
+            unweave(s, 0)
+            weave(s, 1)
+            mm1(s, 0)
+            mm1(s, 1)
+            for b in range(LIVE):
+                mm2(s - 1, b)
+            for t in range(rows_v):
+                widen_rows(s + 1, t, True)
+            for t in range(4):
+                widen_pairs(s + 1, t)
+            gelu(s, 1)
+            diff(s, 0)
+            clamp(s + 1)
+            gelu(s, 2)
+            diff(s, 1)
+            unweave(s, 1)
+            join_pairs(s, 0, VC)
+            if s == WN:
+                nc.scalar.activation(out=sq[:], in_=w1t[:], func=ACT.Square, scale=0.5, accum_out=wsum[:, 0:1])
+            q_x(s, 0)
+            make_da(s, 0)
+            make_da(s, 1)
+            q_x(s, 1)
+            q_da(s)
+
+        empty(last, 0)
+        turn(last, 2)
+        empty(last, 1)
+        turn(last, 3)
+        weave(last, 0)
+        gelu(last, 0)
+        empty(last, 2)
+        weave(last, 1, "tp", 2)
+        q_dy(last, 0)
+        empty(last, 3)
+        q_dy(last, 1)
+        tot = psum.tile([P, 8], F32, name="tot", tag="tp", bufs=2)
+        nc.tensor.matmul(tot[:, 0:1], lhsT=ones[:], rhs=wsum[:, 0:1], start=True, stop=True)
+        mm1(last, 0)
+        mm1(last, 1)
+        for b in range(LIVE):
+            mm2(last - 1, b)
+        gelu(last, 1)
+        diff(last, 0, 0, 2 * F)
+        diff(last, 0, 2 * F, 4 * F)
+        gelu(last, 2)
+        diff(last, 1, 0, 2 * F)
+        diff(last, 1, 2 * F, 4 * F)
+        new_xi(last)
+        unweave(last, 0)
+        gbank.append(psum.tile([P, 2 * F], F32, name="g3", tag="wb", bufs=1))
+        for i in range(last):
+            mm2(i, LIVE)
+        join_pairs(last, 0, VC)
+        unweave(last, 1)
+        nc.scalar.activation(out=winv[:, 0:1], in_=tot[:, 0:1], func=ACT.Abs_reciprocal_sqrt)
+        make_da(last, 0)
+        make_da(last, 1)
+        q_x(last, 0)
+        q_da(last)
+        q_x(last, 1)
+        nc.scalar.activation(out=winv2[:, 0:1], in_=winv[:, 0:1], func=ACT.Square)
+        for b in range(NB):
+            mm2(last, b)
+
+        def cols(b):
+            return slice(2 * F * b, 2 * F * (b + 1))
+
+        def square(b):
+            nc.scalar.activation(out=sq[:, cols(b)], in_=gbank[b][:], func=ACT.Square, scale=(2.0 / 3.0) ** 0.5 / 64.0)
+
+        def first_moment(b):
+            nc.vector.scalar_tensor_tensor(
+                out=mn[:, cols(b)], in0=gbank[b][:], scalar=-2.0 / 3.0 / 64.0, in1=mt[:, cols(b)], op0=MULT, op1=SUB
+            )
+
+        def second_moment(b):
+            nc.vector.tensor_tensor(out=sq[:, cols(b)], in0=sq[:, cols(b)], in1=vt[:, cols(b)], op=ADD)
 
         def inv_root(b):
-            s = slice(2 * b, 2 * b + 2)
-            nc.scalar.activation(out=sq[:, s, :], in_=sq[:, s, :], func=ACT.Abs_reciprocal_sqrt, scale=1.0 / 0.6)
+            nc.scalar.activation(out=sq[:, cols(b)], in_=sq[:, cols(b)], func=ACT.Abs_reciprocal_sqrt, scale=1.0 / 0.6)
 
         def ratio(b):
-            s = slice(2 * b, 2 * b + 2)
-            nc.vector.tensor_tensor(out=mn[:, s, :], in0=mn[:, s, :], in1=sq[:, s, :], op=MULT)
+            nc.vector.tensor_tensor(out=mn[:, cols(b)], in0=mn[:, cols(b)], in1=sq[:, cols(b)], op=MULT)
 
         def decay(b):
-            s = slice(2 * b, 2 * b + 2)
-            nc.vector.scalar_tensor_tensor(out=mn[:, s, :], in0=w1t[:, s, :], scalar=-0.1, in1=mn[:, s, :], op0=MULT, op1=ADD)
+            nc.vector.scalar_tensor_tensor(
+                out=mn[:, cols(b)], in0=w1t[:, cols(b)], scalar=-0.1, in1=mn[:, cols(b)], op0=MULT, op1=ADD
+            )
+
+        rtot = psum.tile([P, 8], F32, name="rtot", tag="dh", bufs=2)
 
         def r_norm(b):
-            s = slice(2 * b, 2 * b + 2)
-            nc.scalar.activation(out=sq[:, s, :], in_=mn[:, s, :], func=ACT.Square, accum_out=stats[:, 4 + b : 5 + b])
+            nc.scalar.activation(out=sq[:, cols(b)], in_=mn[:, cols(b)], func=ACT.Square, accum_out=rsum[:, b : b + 1])
+            nc.tensor.matmul(rtot[:, 0:1], lhsT=ones[:], rhs=rsum[:, b : b + 1], start=(b == 1), stop=(b == NB - 1))
 
-        moments(0)
-        moments(1)
-        tot = psum.tile([P, 8], F32, name="tot", tag="g0", bufs=1)
-        for b in range(4):
-            nc.tensor.matmul(tot[:, 1:2], lhsT=ones[:], rhs=stats[:, b : b + 1], start=(b == 0), stop=(b == 3))
-        moments(2)
-        inv_root(0)
-        moments(3)
+        first_moment(0)
+        square(1)
+        square(0)
+        first_moment(2)
+        first_moment(1)
+        square(2)
+        second_moment(1)
         inv_root(1)
-        ratio(0)
-        inv_root(2)
+        second_moment(0)
+        square(3)
+        inv_root(0)
+        second_moment(2)
         ratio(1)
+        first_moment(3)
+        inv_root(2)
+        second_moment(3)
+        ratio(0)
+        decay(1)
+        inv_root(3)
+        r_norm(1)
+        ratio(2)
         decay(0)
         r_norm(0)
-        inv_root(3)
-        ratio(2)
-        nc.vector.reciprocal(out=wsum[:, 0:1], in_=tot[:, 1:2])
-        decay(1)
-        r_norm(1)
         ratio(3)
         decay(2)
         r_norm(2)
         decay(3)
         r_norm(3)
-        for b in range(4):
-            nc.tensor.matmul(tot[:, 0:1], lhsT=ones[:], rhs=stats[:, 4 + b : 5 + b], start=(b == 0), stop=(b == 3))
-        nc.scalar.activation(out=small[:, 0:1], in_=tot[:, 0:1], func=ACT.Abs_reciprocal_sqrt, scale=wsum[:, 0:1])
+        nc.scalar.activation(out=step[:, 0:1], in_=rtot[:, 0:1], func=ACT.Abs_reciprocal_sqrt, scale=winv2[:, 0:1])
         out_v = out.rearrange("(j p) f -> p j f", p=P)
-        for b in range(4):
-            s = slice(2 * b, 2 * b + 2)
-            res = pool.tile([P, 2, F], F32, name=f"res{b}", tag="res", bufs=4)
+        for b in range(NB):
+            res = pool.tile([P, 2 * F], F32, name=f"res{b}", tag="res", bufs=4)
             nc.vector.scalar_tensor_tensor(
-                out=res[:], in0=mn[:, s, :], scalar=small[:, 0:1], in1=w1t[:, s, :], op0=MULT, op1=ADD
+                out=res[:], in0=mn[:, cols(b)], scalar=step[:, 0:1], in1=w1t[:, cols(b)], op0=MULT, op1=ADD
             )
-            nc.sync.dma_start(out=out_v[:, s, :], in_=res[:])
+            nc.sync.dma_start(out=out_v[:, 2 * b : 2 * b + 2, :], in_=res[:].rearrange("p (j f) -> p j f", f=F))

@@ -24,12 +24,12 @@ NG = T // 512
 NC = D // 512
 NJ = D // P
 NB = NJ // 2
-H = 1.5 * 2.0 ** -11
+H = 2.0 ** -21
+NODES = (-9184.0, 3999.0, -7083.0)
 LIVE = 3
-WC = 384
+WC = 128
 VC = D - WC
-WS = 3
-WN = 1
+TAIL = 0
 
 
 def tile_lambmlpbackwardstep_t_kernel(tc, x_bytes, x_scale, a, dy, w2, w1, m, v, out):
@@ -60,6 +60,7 @@ def tile_lambmlpbackwardstep_t_kernel(tc, x_bytes, x_scale, a, dy, w2, w1, m, v,
         mn = keep.tile([P, NJ * F], F32, name="mn")
         rsum = keep.tile([P, 8], F32, name="rsum")
         wsum = keep.tile([P, 8], F32, name="wsum")
+        wall = keep.tile([P, 8], F32, name="wall")
         winv = keep.tile([P, 8], F32, name="winv")
         winv2 = keep.tile([P, 8], F32, name="winv2")
         step = keep.tile([P, 8], F32, name="step")
@@ -70,7 +71,7 @@ def tile_lambmlpbackwardstep_t_kernel(tc, x_bytes, x_scale, a, dy, w2, w1, m, v,
         dy_v = dy.rearrange("(g p t) d -> g p t d", p=P, t=4)
         x_v = x_bytes.rearrange("(g p t) d -> g p t d", p=P, t=4)
 
-        at, dyt, x8, ac, ge, dyg, dyq, dyqs, dh, da, xp, xi, tp, xw, wb = ({} for k in range(15))
+        at, dyt, x8, ac, ge, dyg, dyq, dyqs, dh, da, xp, xi, tp, xw, wb, ta, sb = ({} for k in range(17))
 
         def load_a(i):
             at[i] = pool.tile([P, 4, F], BF16, name=f"a{i}", tag="a", bufs=3)
@@ -104,16 +105,45 @@ def tile_lambmlpbackwardstep_t_kernel(tc, x_bytes, x_scale, a, dy, w2, w1, m, v,
                 op1=MAX,
             )
 
-        def gelu(i, k):
-            ge[i, k] = pool.tile([P, 4 * F], F32, name=f"ge{i}_{k}", tag=f"ge{k}", bufs=2)
+        def turn_a(i, tag="aw"):
+            ta[i] = psum.tile([P, 4, P], F32, name=f"ta{i}", tag=tag, bufs=1)
+            words = ac[i][:].rearrange("p f t -> p (f t)").bitcast(F32)
+            for k in range(4):
+                nc.tensor.transpose(ta[i][:, k, :], words[:, P * k : P * (k + 1)], ident[:])
+
+        def gelu_turned(i, n):
+            ge[i, n] = pool.tile([P, 4, 2, P], F32, name=f"ge{i}_{n}", tag=f"ge{n}", bufs=2)
+            src = ta[i][:].rearrange("q k p -> q (k p)").bitcast(BF16).rearrange("q (k p e) -> q k e p", k=4, e=2)
+            nc.scalar.activation(out=ge[i, n][:], in_=src, func=ACT.Gelu, bias=offs[:, n : n + 1])
+
+        def gelu_plain(i, n=2):
+            ge[i, n] = pool.tile([P, 4 * F], F32, name=f"ge{i}_{n}", tag=f"ge{n}", bufs=2)
             nc.scalar.activation(
-                out=ge[i, k][:], in_=ac[i][:].rearrange("p f t -> p (f t)"), func=ACT.Gelu, bias=offs[:, k : k + 1]
+                out=ge[i, n][:], in_=ac[i][:].rearrange("p f t -> p (f t)"), func=ACT.Gelu, bias=offs[:, n : n + 1]
             )
 
-        def diff(i, k, lo=0, hi=4 * F):
-            src, weight = ((0, -27.0 / 32), (2, -5.0 / 32))[k]
+        def w_norm(j):
+            c = slice(F * j, F * (j + 1))
+            nc.scalar.activation(out=sq[:, c], in_=w1t[:, c], func=ACT.Square, scale=0.5, accum_out=wsum[:, j : j + 1])
+
+        def add_nodes(i, h, tag="dh", bufs=2):
+            sb[i, h] = psum.tile([P, 2, 2, P], F32, name=f"sb{i}_{h}", tag=tag, bufs=bufs)
+            for k in range(2):
+                for e in range(2):
+                    for n in range(2):
+                        nc.tensor.matmul(
+                            sb[i, h][:, e, k, :],
+                            lhsT=ge[i, n][:, 2 * h + k, e, :],
+                            rhs=ident[:],
+                            start=(n == 0),
+                            stop=(n == 1),
+                            is_transpose=True,
+                        )
+
+        def diff(i, h):
+            part = ge[i, 2][:, 512 * h : 512 * (h + 1)].rearrange("p (w e) -> p w e", e=2)
             nc.vector.scalar_tensor_tensor(
-                out=ge[i, 1][:, lo:hi], in0=ge[i, src][:, lo:hi], scalar=weight, in1=ge[i, 1][:, lo:hi], op0=MULT, op1=ADD
+                out=part, in0=part, scalar=-2.0, in1=sb[i, h][:].rearrange("p e k q -> p (k q) e"), op0=MULT, op1=ADD
             )
 
         def turn(i, t, tag="tp", bufs=2):
@@ -129,19 +159,19 @@ def tile_lambmlpbackwardstep_t_kernel(tc, x_bytes, x_scale, a, dy, w2, w1, m, v,
             dst = dyg[i][:, t, :].bitcast(F32).rearrange("q (c r u) -> q c r u", c=NC, u=2)
             move(on_vector, dst, tp[i, t][:].rearrange("q c u r -> q c r u"))
 
-        def q_dy(i, u):
-            if u == 0:
+        def q_dy(i, lo, hi):
+            if lo == 0:
                 dyq[i] = pool.tile([P, 4, NC, P], U32, name=f"dyq{i}", tag="dyq", bufs=2, align_bytes=64)
                 dyqs[i] = pool.tile([P, 4, NC, P], U8, name=f"dyqs{i}", tag="dyqs", bufs=2, align_bytes=64)
-            s = slice(2 * u, 2 * u + 2)
+            s = slice(lo, hi)
             nc.vector.quantize_mx(
                 out=dyq[i][:, s].rearrange("p t c r -> p (t c r)").bitcast(FP8X4),
                 scales=dyqs[i][:, s].rearrange("p t c r -> p (t c r)"),
                 in_=dyg[i][:, s].rearrange("p t k -> p (t k)"),
             )
 
-        def mm1(i, h):
-            dh[i, h] = psum.tile([P, 4, P], F32, name=f"dh{i}_{h}", tag="dh", bufs=2)
+        def mm1(i, h, tag="dh"):
+            dh[i, h] = psum.tile([P, 4, P], F32, name=f"dh{i}_{h}", tag=tag, bufs=2)
             for t in range(4):
                 for c in range(NC):
                     nc.tensor.matmul_mx(
@@ -160,8 +190,8 @@ def tile_lambmlpbackwardstep_t_kernel(tc, x_bytes, x_scale, a, dy, w2, w1, m, v,
             s = slice(512 * h, 512 * (h + 1))
             nc.vector.scalar_tensor_tensor(
                 out=da[i][:, s].rearrange("p (f t) -> p f t", t=4),
-                in0=ge[i, 1][:, s].rearrange("p (f t) -> p f t", t=4),
-                scalar=4.0 / (15.0 * H),
+                in0=ge[i, 2][:, s].rearrange("p (f t) -> p f t", t=4),
+                scalar=1.0 / ((NODES[0] + NODES[1] - 2 * NODES[2]) * H),
                 in1=dh[i, h][:].rearrange("p t f -> p f t"),
                 op0=MULT,
                 op1=MULT,
@@ -198,27 +228,24 @@ def tile_lambmlpbackwardstep_t_kernel(tc, x_bytes, x_scale, a, dy, w2, w1, m, v,
             dst = xi[i][:, 0 : 4 * VC].bitcast(F32).rearrange("p (d a) -> p d a", a=2)
             move(on_vector, dst[:, lo:hi, :], src[:, lo:hi, :])
 
-        def weave(i, c, tag="wb", bufs=1):
-            half = WC // 2
-            wb[i, c] = psum.tile([P, 4 * half], BF16, name=f"wb{i}_{c}", tag=tag, bufs=bufs)
-            for d in range(0, half, half // 2):
-                col = half * c + d
+        def weave(i, tag="aw", bufs=1):
+            wb[i] = psum.tile([P, 4 * WC], BF16, name=f"wb{i}", tag=tag, bufs=bufs)
+            for d in range(0, WC, WC // 2):
                 nc.tensor.matmul(
-                    wb[i, c][:, 4 * d : 4 * (d + half // 2)],
+                    wb[i][:, 4 * d : 4 * (d + WC // 2)],
                     lhsT=ident_h[:],
-                    rhs=xw[i][:, :, col : col + half // 2].rearrange("p t d -> p d t"),
+                    rhs=xw[i][:, :, d : d + WC // 2].rearrange("p t d -> p d t"),
                     start=True,
                     stop=True,
                 )
 
-        def unweave(i, c, on_vector=False):
-            half = WC // 2
-            move(on_vector, xi[i][:, 4 * (VC + half * c) : 4 * (VC + half * (c + 1))].bitcast(F32), wb[i, c][:].bitcast(F32))
+        def unweave(i, on_vector=False):
+            move(on_vector, xi[i][:, 4 * VC : 4 * D].bitcast(F32), wb[i][:].bitcast(F32))
 
-        def q_x(i, u):
-            s = slice(512 * u, 512 * (u + 1))
+        def q_x(i, lo, hi):
+            s = slice(lo, hi)
             nc.vector.quantize_mx(
-                out=xq[:, i, s].bitcast(FP8X4), scales=xqs[:, i, s], in_=xi[i][:, 2048 * u : 2048 * (u + 1)]
+                out=xq[:, i, s].bitcast(FP8X4), scales=xqs[:, i, s], in_=xi[i][:, 4 * lo : 4 * hi]
             )
 
         def mm2(i, b):
@@ -260,152 +287,120 @@ def tile_lambmlpbackwardstep_t_kernel(tc, x_bytes, x_scale, a, dy, w2, w1, m, v,
         load_x(1)
         load_dy(1, 0)
         load_dy(1, 1)
-        for k, n in enumerate((-2.0, 3.0, 6.0)):
+        for k, n in enumerate(NODES):
             nc.vector.memset(offs[:, k : k + 1], n * H)
         nc.vector.memset(ones[:], 1.0)
         make_identity(nc, ident[:])
         nc.vector.tensor_copy(out=ident_h[:], in_=ident[:])
         clamp(0)
         load_a(2)
+        load_rows(w1t, w1)
         load_x(2)
         load_dy(2, 0)
         load_dy(2, 1)
-        gelu(0, 0)
+        gelu_plain(0, 0)
+        gelu_plain(0, 1)
         for t in range(4):
             widen_rows(0, t, True)
-        weave(0, 0)
-        weave(0, 1, "g2")
+        weave(0, "g2")
         turn(0, 0)
         turn(0, 1)
         turn(0, 2, "g0", 1)
         turn(0, 3, "g1", 1)
         w2_banks = [turn_w2(h) for h in range(2)]
-        gelu(0, 1)
+        gelu_plain(0, 2)
         for t in range(4):
             widen_pairs(0, t)
         new_xi(0)
-        unweave(0, 0, True)
-        gelu(0, 2)
-        join_pairs(0, 0, VC, True)
-        unweave(0, 1, True)
+        unweave(0)
+        nc.vector.tensor_tensor(out=ge[0, 0][:], in0=ge[0, 0][:], in1=ge[0, 1][:], op=ADD)
         empty(0, 0)
-        diff(0, 0)
         empty(0, 1)
+        clamp(1)
+        turn_a(1)
         turn(1, 0)
         turn(1, 1)
-        clamp(1)
+        nc.vector.scalar_tensor_tensor(out=ge[0, 2][:], in0=ge[0, 2][:], scalar=-2.0, in1=ge[0, 0][:], op0=MULT, op1=ADD)
         empty(0, 2)
-        diff(0, 1)
         empty(0, 3)
-        q_x(0, 0)
         empty_w2(0, w2_banks[0])
-        q_dy(0, 0)
         empty_w2(1, w2_banks[1])
-        q_dy(0, 1)
-        q_w2()
-        for t in range(4 - WS):
-            widen_rows(1, t, True)
-        for t in range(4):
+        for t in range(2):
             widen_pairs(1, t)
+        q_dy(0, 0, 4)
+        q_w2()
+        join_pairs(0, 0, VC)
         for b in range(LIVE):
             gbank.append(psum.tile([P, 2 * F], F32, name=f"g{b}", tag=f"g{b}", bufs=1))
 
         last = NG - 1
-        for s in range(1, last):
+        for s in range(1, NG):
             if s + 2 < NG:
                 load_a(s + 2)
                 load_x(s + 2)
                 load_dy(s + 2, 0)
                 load_dy(s + 2, 1)
-            if s == 1:
-                load_rows(w1t, w1)
             if s == 5:
                 load_rows(mt, m)
                 load_rows(vt, v)
-            rows_v = 4 if s + 1 == last else 4 - WS
             empty(s, 0)
             turn(s, 2)
+            mm1(s - 1, 0)
             empty(s, 1)
             turn(s, 3)
-            if s == 1:
-                mm1(0, 0)
-                mm1(0, 1)
-                make_da(0, 0)
-                make_da(0, 1)
-                q_x(0, 1)
-                q_da(0)
-            for t in range(4 - WS, 4):
+            mm1(s - 1, 1)
+            gelu_turned(s, 0)
+            gelu_turned(s, 1)
+            for t in range(2, 4):
+                widen_pairs(s, t)
+            if s + 1 < NG:
+                clamp(s + 1)
+            q_x(s - 1, 0, 512)
+            make_da(s - 1, 0)
+            make_da(s - 1, 1)
+            q_x(s - 1, 512, D)
+            for t in range(4):
                 widen_rows(s, t)
-            weave(s, 0)
+            q_da(s - 1)
+            weave(s)
             empty(s, 2)
-            turn(s + 1, 0)
-            q_dy(s, 0)
+            if s < last:
+                turn(s + 1, 0)
+            add_nodes(s, 0)
             empty(s, 3)
-            turn(s + 1, 1)
-            q_dy(s, 1)
-            gelu(s, 0)
-            new_xi(s)
-            unweave(s, 0)
-            weave(s, 1)
-            mm1(s, 0)
-            mm1(s, 1)
+            if s < last:
+                turn(s + 1, 1)
+            add_nodes(s, 1)
             for b in range(LIVE):
                 mm2(s - 1, b)
-            for t in range(rows_v):
-                widen_rows(s + 1, t, True)
-            for t in range(4):
-                widen_pairs(s + 1, t)
-            gelu(s, 1)
-            diff(s, 0)
-            clamp(s + 1)
-            gelu(s, 2)
-            diff(s, 1)
-            unweave(s, 1)
+            q_dy(s, 0, 4)
+            gelu_plain(s)
+            w_norm(s - 1)
+            new_xi(s)
+            unweave(s)
+            if s < last:
+                turn_a(s + 1)
+                for t in range(2):
+                    widen_pairs(s + 1, t)
             join_pairs(s, 0, VC)
-            if s == WN:
-                nc.scalar.activation(out=sq[:], in_=w1t[:], func=ACT.Square, scale=0.5, accum_out=wsum[:, 0:1])
-            q_x(s, 0)
-            make_da(s, 0)
-            make_da(s, 1)
-            q_x(s, 1)
-            q_da(s)
+            diff(s, 0)
+            diff(s, 1)
 
-        empty(last, 0)
-        turn(last, 2)
-        empty(last, 1)
-        turn(last, 3)
-        weave(last, 0)
-        gelu(last, 0)
-        empty(last, 2)
-        weave(last, 1, "tp", 2)
-        q_dy(last, 0)
-        empty(last, 3)
-        q_dy(last, 1)
-        tot = psum.tile([P, 8], F32, name="tot", tag="tp", bufs=2)
-        nc.tensor.matmul(tot[:, 0:1], lhsT=ones[:], rhs=wsum[:, 0:1], start=True, stop=True)
-        mm1(last, 0)
-        mm1(last, 1)
-        for b in range(LIVE):
-            mm2(last - 1, b)
-        gelu(last, 1)
-        diff(last, 0, 0, 2 * F)
-        diff(last, 0, 2 * F, 4 * F)
-        gelu(last, 2)
-        diff(last, 1, 0, 2 * F)
-        diff(last, 1, 2 * F, 4 * F)
-        new_xi(last)
-        unweave(last, 0)
-        gbank.append(psum.tile([P, 2 * F], F32, name="g3", tag="wb", bufs=1))
+        mm1(last, 0, "tp")
+        mm1(last, 1, "tp")
+        gbank.append(psum.tile([P, 2 * F], F32, name="g3", tag="dh", bufs=2))
         for i in range(last):
             mm2(i, LIVE)
-        join_pairs(last, 0, VC)
-        unweave(last, 1)
+        w_norm(last)
+        nc.scalar.activation(out=winv2[:], in_=wsum[:], func=ACT.Copy, accum_out=wall[:, 0:1])
+        tot = psum.tile([P, 8], F32, name="tot", tag="aw", bufs=1)
+        nc.tensor.matmul(tot[:, 0:1], lhsT=ones[:], rhs=wall[:, 0:1], start=True, stop=True)
         nc.scalar.activation(out=winv[:, 0:1], in_=tot[:, 0:1], func=ACT.Abs_reciprocal_sqrt)
         make_da(last, 0)
         make_da(last, 1)
-        q_x(last, 0)
+        q_x(last, 0, 512)
         q_da(last)
-        q_x(last, 1)
+        q_x(last, 512, D)
         nc.scalar.activation(out=winv2[:, 0:1], in_=winv[:, 0:1], func=ACT.Square)
         for b in range(NB):
             mm2(last, b)
@@ -427,19 +422,17 @@ def tile_lambmlpbackwardstep_t_kernel(tc, x_bytes, x_scale, a, dy, w2, w1, m, v,
         def inv_root(b):
             nc.scalar.activation(out=sq[:, cols(b)], in_=sq[:, cols(b)], func=ACT.Abs_reciprocal_sqrt, scale=1.0 / 0.6)
 
-        def ratio(b):
-            nc.vector.tensor_tensor(out=mn[:, cols(b)], in0=mn[:, cols(b)], in1=sq[:, cols(b)], op=MULT)
+        def ratio(c):
+            nc.vector.tensor_tensor(out=mn[:, c], in0=mn[:, c], in1=sq[:, c], op=MULT)
 
-        def decay(b):
-            nc.vector.scalar_tensor_tensor(
-                out=mn[:, cols(b)], in0=w1t[:, cols(b)], scalar=-0.1, in1=mn[:, cols(b)], op0=MULT, op1=ADD
-            )
+        def decay(c):
+            nc.vector.scalar_tensor_tensor(out=mn[:, c], in0=w1t[:, c], scalar=-0.1, in1=mn[:, c], op0=MULT, op1=ADD)
 
         rtot = psum.tile([P, 8], F32, name="rtot", tag="dh", bufs=2)
 
-        def r_norm(b):
-            nc.scalar.activation(out=sq[:, cols(b)], in_=mn[:, cols(b)], func=ACT.Square, accum_out=rsum[:, b : b + 1])
-            nc.tensor.matmul(rtot[:, 0:1], lhsT=ones[:], rhs=rsum[:, b : b + 1], start=(b == 1), stop=(b == NB - 1))
+        def r_norm(c, k):
+            nc.scalar.activation(out=sq[:, c], in_=mn[:, c], func=ACT.Square, accum_out=rsum[:, k : k + 1])
+            nc.tensor.matmul(rtot[:, 0:1], lhsT=ones[:], rhs=rsum[:, k : k + 1], start=(k == 0), stop=(k == NB))
 
         first_moment(0)
         square(1)
@@ -453,22 +446,25 @@ def tile_lambmlpbackwardstep_t_kernel(tc, x_bytes, x_scale, a, dy, w2, w1, m, v,
         square(3)
         inv_root(0)
         second_moment(2)
-        ratio(1)
+        ratio(cols(1))
         first_moment(3)
         inv_root(2)
         second_moment(3)
-        ratio(0)
-        decay(1)
+        ratio(cols(0))
+        decay(cols(1))
         inv_root(3)
-        r_norm(1)
-        ratio(2)
-        decay(0)
-        r_norm(0)
-        ratio(3)
-        decay(2)
-        r_norm(2)
-        decay(3)
-        r_norm(3)
+        r_norm(cols(1), 0)
+        ratio(cols(2))
+        decay(cols(0))
+        r_norm(cols(0), 1)
+        decay(cols(2))
+        r_norm(cols(2), 2)
+        ends = (slice(6 * F, 7 * F + TAIL), slice(7 * F + TAIL, 8 * F))
+        for c in ends:
+            ratio(c)
+        for k, c in enumerate(ends):
+            decay(c)
+            r_norm(c, 3 + k)
         nc.scalar.activation(out=step[:, 0:1], in_=rtot[:, 0:1], func=ACT.Abs_reciprocal_sqrt, scale=winv2[:, 0:1])
         out_v = out.rearrange("(j p) f -> p j f", p=P)
         for b in range(NB):

@@ -27,9 +27,11 @@ NB = NJ // 2
 H = 2.0 ** -21
 NODES = (-9184.0, 3999.0, -7083.0)
 LIVE = 3
-WC = 128
+GS = 4
+GT = 12
+EARLY = 5
+WC = 144
 VC = D - WC
-TAIL = 0
 
 
 def tile_lambmlpbackwardstep_t_kernel(tc, x_bytes, x_scale, a, dy, w2, w1, m, v, out):
@@ -59,13 +61,12 @@ def tile_lambmlpbackwardstep_t_kernel(tc, x_bytes, x_scale, a, dy, w2, w1, m, v,
         sq = keep.tile([P, NJ * F], F32, name="sq")
         mn = keep.tile([P, NJ * F], F32, name="mn")
         rsum = keep.tile([P, 8], F32, name="rsum")
-        wsum = keep.tile([P, 8], F32, name="wsum")
         wall = keep.tile([P, 8], F32, name="wall")
         winv = keep.tile([P, 8], F32, name="winv")
         winv2 = keep.tile([P, 8], F32, name="winv2")
         step = keep.tile([P, 8], F32, name="step")
 
-        gbank = []
+        gbank = {}
 
         a_v = a.rearrange("(g p t) f -> g p t f", p=P, t=4)
         dy_v = dy.rearrange("(g p t) d -> g p t d", p=P, t=4)
@@ -81,9 +82,11 @@ def tile_lambmlpbackwardstep_t_kernel(tc, x_bytes, x_scale, a, dy, w2, w1, m, v,
             dyt[i, u] = pool.tile([P, 2, D], BF16, name=f"dy{i}_{u}", tag="dy", bufs=6)
             nc.sync.dma_start(out=dyt[i, u][:], in_=dy_v[i][:, 2 * u : 2 * u + 2, :])
 
-        def load_x(i):
+        def load_x(i, pieces=1):
             x8[i] = pool.tile([P, 4, D], U8, name=f"x8_{i}", tag="x8", bufs=3)
-            nc.sync.dma_start(out=x8[i][:], in_=x_v[i])
+            n = 4 // pieces
+            for t in range(0, 4, n):
+                nc.sync.dma_start(out=x8[i][:, t : t + n, :], in_=x_v[i][:, t : t + n, :])
 
         def load_rows(dst, src):
             nc.sync.dma_start(out=dst[:].rearrange("p (j f) -> p j f", f=F), in_=src.rearrange("(j p) f -> p j f", p=P))
@@ -122,9 +125,15 @@ def tile_lambmlpbackwardstep_t_kernel(tc, x_bytes, x_scale, a, dy, w2, w1, m, v,
                 out=ge[i, n][:], in_=ac[i][:].rearrange("p f t -> p (f t)"), func=ACT.Gelu, bias=offs[:, n : n + 1]
             )
 
-        def w_norm(j):
-            c = slice(F * j, F * (j + 1))
-            nc.scalar.activation(out=sq[:, c], in_=w1t[:, c], func=ACT.Square, scale=0.5, accum_out=wsum[:, j : j + 1])
+        def w_gram(lo, hi):
+            for k in range(lo, hi):
+                block = w1t[:, P * k : P * (k + 1)]
+                nc.tensor.matmul(gram[:], lhsT=block, rhs=block, start=(k == 0), stop=(k == 2 * NJ - 1))
+
+        def w_trace():
+            nc.vector.scalar_tensor_tensor(
+                out=sq[:, 0:P], in0=gram[:], scalar=0.25, in1=ident[:], op0=MULT, op1=MULT, accum_out=wall[:, 0:1]
+            )
 
         def add_nodes(i, h, tag="dh", bufs=2):
             sb[i, h] = psum.tile([P, 2, 2, P], F32, name=f"sb{i}_{h}", tag=tag, bufs=bufs)
@@ -137,7 +146,7 @@ def tile_lambmlpbackwardstep_t_kernel(tc, x_bytes, x_scale, a, dy, w2, w1, m, v,
                             rhs=ident[:],
                             start=(n == 0),
                             stop=(n == 1),
-                            is_transpose=True,
+                            is_transpose=None if (k, e, n) == (1, 1, 1) else True,
                         )
 
         def diff(i, h):
@@ -249,6 +258,8 @@ def tile_lambmlpbackwardstep_t_kernel(tc, x_bytes, x_scale, a, dy, w2, w1, m, v,
             )
 
         def mm2(i, b):
+            if i == 0 and b < LIVE:
+                gbank[b] = psum.tile([P, 2 * F], F32, name=f"g{b}", tag=f"g{b}", bufs=1)
             for j in (2 * b, 2 * b + 1):
                 nc.tensor.matmul_mx(
                     out=gbank[b][:, F * (j % 2) : F * (j % 2 + 1)],
@@ -279,13 +290,14 @@ def tile_lambmlpbackwardstep_t_kernel(tc, x_bytes, x_scale, a, dy, w2, w1, m, v,
 
         load_a(0)
         nc.scalar.dma_start(out=xs[:], in_=x_scale.rearrange("(g p t) o -> p g (t o)", p=P, t=4))
-        load_x(0)
+        load_x(0, 2)
         load_dy(0, 0)
         load_dy(0, 1)
         nc.sync.dma_start(out=w2r[:], in_=w2.rearrange("(h p) d -> p h d", p=P))
         load_a(1)
         load_x(1)
         load_dy(1, 0)
+        load_rows(w1t, w1)
         load_dy(1, 1)
         for k, n in enumerate(NODES):
             nc.vector.memset(offs[:, k : k + 1], n * H)
@@ -294,22 +306,23 @@ def tile_lambmlpbackwardstep_t_kernel(tc, x_bytes, x_scale, a, dy, w2, w1, m, v,
         nc.vector.tensor_copy(out=ident_h[:], in_=ident[:])
         clamp(0)
         load_a(2)
-        load_rows(w1t, w1)
         load_x(2)
         load_dy(2, 0)
         load_dy(2, 1)
         gelu_plain(0, 0)
         gelu_plain(0, 1)
+        for t in range(2):
+            widen_pairs(0, t)
         for t in range(4):
             widen_rows(0, t, True)
-        weave(0, "g2")
         turn(0, 0)
+        weave(0, "g2")
         turn(0, 1)
         turn(0, 2, "g0", 1)
         turn(0, 3, "g1", 1)
         w2_banks = [turn_w2(h) for h in range(2)]
         gelu_plain(0, 2)
-        for t in range(4):
+        for t in range(2, 4):
             widen_pairs(0, t)
         new_xi(0)
         unweave(0)
@@ -320,6 +333,8 @@ def tile_lambmlpbackwardstep_t_kernel(tc, x_bytes, x_scale, a, dy, w2, w1, m, v,
         turn_a(1)
         turn(1, 0)
         turn(1, 1)
+        gram = psum.tile([P, P], F32, name="gram", tag="g2", bufs=1)
+        w_gram(0, GS)
         nc.vector.scalar_tensor_tensor(out=ge[0, 2][:], in0=ge[0, 2][:], scalar=-2.0, in1=ge[0, 0][:], op0=MULT, op1=ADD)
         empty(0, 2)
         empty(0, 3)
@@ -330,8 +345,6 @@ def tile_lambmlpbackwardstep_t_kernel(tc, x_bytes, x_scale, a, dy, w2, w1, m, v,
         q_dy(0, 0, 4)
         q_w2()
         join_pairs(0, 0, VC)
-        for b in range(LIVE):
-            gbank.append(psum.tile([P, 2 * F], F32, name=f"g{b}", tag=f"g{b}", bufs=1))
 
         last = NG - 1
         for s in range(1, NG):
@@ -343,12 +356,19 @@ def tile_lambmlpbackwardstep_t_kernel(tc, x_bytes, x_scale, a, dy, w2, w1, m, v,
             if s == 5:
                 load_rows(mt, m)
                 load_rows(vt, v)
+            if s == 1:
+                mm1(0, 0)
             empty(s, 0)
             turn(s, 2)
-            mm1(s - 1, 0)
+            mm1(s - 1, 1 if s == 1 else 0)
             empty(s, 1)
             turn(s, 3)
-            mm1(s - 1, 1)
+            if s > 1:
+                mm1(s - 1, 1)
+            if s > 1:
+                mm2(s - 2, 1)
+            else:
+                w_gram(GS, GT)
             gelu_turned(s, 0)
             gelu_turned(s, 1)
             for t in range(2, 4):
@@ -356,6 +376,8 @@ def tile_lambmlpbackwardstep_t_kernel(tc, x_bytes, x_scale, a, dy, w2, w1, m, v,
             if s + 1 < NG:
                 clamp(s + 1)
             q_x(s - 1, 0, 512)
+            if s == 2:
+                w_trace()
             make_da(s - 1, 0)
             make_da(s - 1, 1)
             q_x(s - 1, 512, D)
@@ -367,15 +389,17 @@ def tile_lambmlpbackwardstep_t_kernel(tc, x_bytes, x_scale, a, dy, w2, w1, m, v,
             if s < last:
                 turn(s + 1, 0)
             add_nodes(s, 0)
+            if s > 1:
+                mm2(s - 2, 2)
+            else:
+                w_gram(GT, 2 * NJ)
             empty(s, 3)
             if s < last:
                 turn(s + 1, 1)
             add_nodes(s, 1)
-            for b in range(LIVE):
-                mm2(s - 1, b)
+            mm2(s - 1, 0)
             q_dy(s, 0, 4)
             gelu_plain(s)
-            w_norm(s - 1)
             new_xi(s)
             unweave(s)
             if s < last:
@@ -388,22 +412,23 @@ def tile_lambmlpbackwardstep_t_kernel(tc, x_bytes, x_scale, a, dy, w2, w1, m, v,
 
         mm1(last, 0, "tp")
         mm1(last, 1, "tp")
-        gbank.append(psum.tile([P, 2 * F], F32, name="g3", tag="dh", bufs=2))
-        for i in range(last):
-            mm2(i, LIVE)
-        w_norm(last)
-        nc.scalar.activation(out=winv2[:], in_=wsum[:], func=ACT.Copy, accum_out=wall[:, 0:1])
         tot = psum.tile([P, 8], F32, name="tot", tag="aw", bufs=1)
         nc.tensor.matmul(tot[:, 0:1], lhsT=ones[:], rhs=wall[:, 0:1], start=True, stop=True)
         nc.scalar.activation(out=winv[:, 0:1], in_=tot[:, 0:1], func=ACT.Abs_reciprocal_sqrt)
+        for b in (1, 2):
+            mm2(last - 1, b)
+        gbank[LIVE] = psum.tile([P, 2 * F], F32, name="g3", tag="dh", bufs=2)
+        for i in range(EARLY):
+            mm2(i, LIVE)
         make_da(last, 0)
         make_da(last, 1)
         q_x(last, 0, 512)
         q_da(last)
         q_x(last, 512, D)
-        nc.scalar.activation(out=winv2[:, 0:1], in_=winv[:, 0:1], func=ACT.Square)
-        for b in range(NB):
+        for b in range(LIVE):
             mm2(last, b)
+        for i in range(EARLY, NG):
+            mm2(i, LIVE)
 
         def cols(b):
             return slice(2 * F * b, 2 * F * (b + 1))
@@ -416,11 +441,17 @@ def tile_lambmlpbackwardstep_t_kernel(tc, x_bytes, x_scale, a, dy, w2, w1, m, v,
                 out=mn[:, cols(b)], in0=gbank[b][:], scalar=-2.0 / 3.0 / 64.0, in1=mt[:, cols(b)], op0=MULT, op1=SUB
             )
 
-        def second_moment(b):
-            nc.vector.tensor_tensor(out=sq[:, cols(b)], in0=sq[:, cols(b)], in1=vt[:, cols(b)], op=ADD)
+        vn = {}
 
-        def inv_root(b):
-            nc.scalar.activation(out=sq[:, cols(b)], in_=sq[:, cols(b)], func=ACT.Abs_reciprocal_sqrt, scale=1.0 / 0.6)
+        def open_v(b, tag, bufs):
+            vn[b] = psum.tile([P, 2 * F], F32, name=f"vn{b}", tag=tag, bufs=bufs)
+            nc.tensor.matmul(vn[b][:], lhsT=ident_h[:], rhs=vt[:, cols(b)], start=True, stop=False)
+
+        def second_moment(b):
+            nc.tensor.matmul(vn[b][:], lhsT=ident[:], rhs=sq[:, cols(b)], start=False, stop=True)
+
+        def inv_root(b, src):
+            nc.scalar.activation(out=sq[:, cols(b)], in_=src, func=ACT.Abs_reciprocal_sqrt, scale=1.0 / 0.6)
 
         def ratio(c):
             nc.vector.tensor_tensor(out=mn[:, c], in0=mn[:, c], in1=sq[:, c], op=MULT)
@@ -428,38 +459,41 @@ def tile_lambmlpbackwardstep_t_kernel(tc, x_bytes, x_scale, a, dy, w2, w1, m, v,
         def decay(c):
             nc.vector.scalar_tensor_tensor(out=mn[:, c], in0=w1t[:, c], scalar=-0.1, in1=mn[:, c], op0=MULT, op1=ADD)
 
-        rtot = psum.tile([P, 8], F32, name="rtot", tag="dh", bufs=2)
-
         def r_norm(c, k):
             nc.scalar.activation(out=sq[:, c], in_=mn[:, c], func=ACT.Square, accum_out=rsum[:, k : k + 1])
             nc.tensor.matmul(rtot[:, 0:1], lhsT=ones[:], rhs=rsum[:, k : k + 1], start=(k == 0), stop=(k == NB))
 
         first_moment(0)
         square(1)
-        square(0)
+        open_v(0, "dh", 2)
+        open_v(3, "tp", 2)
         first_moment(2)
+        square(0)
+        second_moment(0)
+        nc.vector.tensor_tensor(out=sq[:, cols(1)], in0=sq[:, cols(1)], in1=vt[:, cols(1)], op=ADD)
+        square(3)
+        second_moment(3)
         first_moment(1)
         square(2)
-        second_moment(1)
-        inv_root(1)
-        second_moment(0)
-        square(3)
-        inv_root(0)
+        open_v(2, "tp", 2)
         second_moment(2)
-        ratio(cols(1))
         first_moment(3)
-        inv_root(2)
-        second_moment(3)
+        inv_root(1, sq[:, cols(1)])
+        rtot = psum.tile([P, 8], F32, name="rtot", tag="g0", bufs=1)
+        ratio(cols(1))
+        inv_root(0, vn[0][:])
         ratio(cols(0))
+        nc.scalar.activation(out=winv2[:, 0:1], in_=winv[:, 0:1], func=ACT.Square)
+        inv_root(3, vn[3][:])
         decay(cols(1))
-        inv_root(3)
+        ratio(cols(3))
+        inv_root(2, vn[2][:])
         r_norm(cols(1), 0)
-        ratio(cols(2))
         decay(cols(0))
         r_norm(cols(0), 1)
-        decay(cols(2))
-        r_norm(cols(2), 2)
-        ends = (slice(6 * F, 7 * F + TAIL), slice(7 * F + TAIL, 8 * F))
+        ends = (slice(4 * F, 5 * F), slice(5 * F, 6 * F))
+        decay(cols(3))
+        r_norm(cols(3), 2)
         for c in ends:
             ratio(c)
         for k, c in enumerate(ends):
@@ -467,9 +501,8 @@ def tile_lambmlpbackwardstep_t_kernel(tc, x_bytes, x_scale, a, dy, w2, w1, m, v,
             r_norm(c, 3 + k)
         nc.scalar.activation(out=step[:, 0:1], in_=rtot[:, 0:1], func=ACT.Abs_reciprocal_sqrt, scale=winv2[:, 0:1])
         out_v = out.rearrange("(j p) f -> p j f", p=P)
-        for b in range(NB):
-            res = pool.tile([P, 2 * F], F32, name=f"res{b}", tag="res", bufs=4)
-            nc.vector.scalar_tensor_tensor(
-                out=res[:], in0=mn[:, cols(b)], scalar=step[:, 0:1], in1=w1t[:, cols(b)], op0=MULT, op1=ADD
-            )
-            nc.sync.dma_start(out=out_v[:, 2 * b : 2 * b + 2, :], in_=res[:].rearrange("p (j f) -> p j f", f=F))
+        for lo, hi in ((0, 2), (2, 4), (4, 6), (6, 7), (7, 8)):
+            c = slice(F * lo, F * hi)
+            res = pool.tile([P, (hi - lo) * F], F32, name=f"res{lo}", tag="res", bufs=5)
+            nc.vector.scalar_tensor_tensor(out=res[:], in0=mn[:, c], scalar=step[:, 0:1], in1=w1t[:, c], op0=MULT, op1=ADD)
+            nc.sync.dma_start(out=out_v[:, lo:hi, :], in_=res[:].rearrange("p (j f) -> p j f", f=F))

@@ -27,11 +27,9 @@ NB = NJ // 2
 H = 2.0 ** -21
 NODES = (-9184.0, 3999.0, -7083.0)
 LIVE = 3
-GS = 4
-GT = 12
+GS = 10
+GT = 14
 EARLY = 5
-WC = 144
-VC = D - WC
 
 
 def tile_lambmlpbackwardstep_t_kernel(tc, x_bytes, x_scale, a, dy, w2, w1, m, v, out):
@@ -43,6 +41,7 @@ def tile_lambmlpbackwardstep_t_kernel(tc, x_bytes, x_scale, a, dy, w2, w1, m, v,
         ctx.enter_context(tc.manual_schedule())
 
         ident = keep.tile([P, P], F32, name="ident")
+        minus2 = keep.tile([P, P], F32, name="minus2")
         ones = keep.tile([P, P], F32, name="ones")
         ident_h = keep.tile([P, P], BF16, name="ident_h")
         offs = keep.tile([P, 4], F32, name="offs")
@@ -135,8 +134,8 @@ def tile_lambmlpbackwardstep_t_kernel(tc, x_bytes, x_scale, a, dy, w2, w1, m, v,
                 out=sq[:, 0:P], in0=gram[:], scalar=0.25, in1=ident[:], op0=MULT, op1=MULT, accum_out=wall[:, 0:1]
             )
 
-        def add_nodes(i, h, tag="dh", bufs=2):
-            sb[i, h] = psum.tile([P, 2, 2, P], F32, name=f"sb{i}_{h}", tag=tag, bufs=bufs)
+        def add_nodes(i, h, closed=True):
+            sb[i, h] = psum.tile([P, 2, 2, P], F32, name=f"sb{i}_{h}", tag="dh", bufs=2)
             for k in range(2):
                 for e in range(2):
                     for n in range(2):
@@ -144,10 +143,24 @@ def tile_lambmlpbackwardstep_t_kernel(tc, x_bytes, x_scale, a, dy, w2, w1, m, v,
                             sb[i, h][:, e, k, :],
                             lhsT=ge[i, n][:, 2 * h + k, e, :],
                             rhs=ident[:],
-                            start=(n == 0),
-                            stop=(n == 1),
-                            is_transpose=None if (k, e, n) == (1, 1, 1) else True,
+                            start=(n == 0 if closed else (k, e, n) == (0, 0, 0)),
+                            stop=(n == 1 and closed),
+                            is_transpose=None if (h, k, e, n) == (0, 1, 1, 1) else True,
                         )
+
+        def third_node(i):
+            nc.tensor.matmul(
+                sb[i, 1][:].rearrange("p e k q -> p (e k q)"),
+                lhsT=minus2[:],
+                rhs=ge[i, 2][:, 512:1024].rearrange("p (w e) -> p e w", e=2),
+                start=False,
+                stop=True,
+            )
+
+        def empty_sum(i):
+            nc.scalar.copy(
+                out=ge[i, 2][:, 512:1024].rearrange("p (w e) -> p w e", e=2), in_=sb[i, 1][:].rearrange("p e k q -> p (k q) e")
+            )
 
         def diff(i, h):
             part = ge[i, 2][:, 512 * h : 512 * (h + 1)].rearrange("p (w e) -> p w e", e=2)
@@ -211,45 +224,22 @@ def tile_lambmlpbackwardstep_t_kernel(tc, x_bytes, x_scale, a, dy, w2, w1, m, v,
 
         def widen_pairs(i, t):
             if t == 0:
-                xp[i] = pool.tile([P, 2, VC, 2], BF16, name=f"xp{i}", tag="xp", bufs=2)
+                xp[i] = pool.tile([P, 2, D, 2], BF16, name=f"xp{i}", tag="xp", bufs=2)
             nc.vector.tensor_scalar(
                 out=xp[i][:, t // 2, :, t % 2],
-                in0=x8[i][:, t, 0:VC].bitcast(FP8),
+                in0=x8[i][:, t, 0:D].bitcast(FP8),
                 scalar1=xs[:, i, t : t + 1],
                 scalar2=None,
                 op0=MULT,
             )
-
-        def widen_rows(i, t, on_vector=False):
-            if t == 0:
-                xw[i] = pool.tile([P, 4, WC], BF16, name=f"xw{i}", tag="xw", bufs=2)
-            src = x8[i][:, t, VC:D].bitcast(FP8)
-            if on_vector:
-                nc.vector.tensor_scalar(out=xw[i][:, t, :], in0=src, scalar1=xs[:, i, t : t + 1], scalar2=None, op0=MULT)
-            else:
-                nc.scalar.activation(out=xw[i][:, t, :], in_=src, func=ACT.Copy, scale=xs[:, i, t : t + 1])
 
         def new_xi(i):
             xi[i] = pool.tile([P, D * 4], BF16, name=f"xi{i}", tag="xi", bufs=2, align_bytes=64)
 
         def join_pairs(i, lo, hi, on_vector=False):
             src = xp[i][:].rearrange("p a d e -> p (a d e)").bitcast(F32).rearrange("p (a d) -> p d a", a=2)
-            dst = xi[i][:, 0 : 4 * VC].bitcast(F32).rearrange("p (d a) -> p d a", a=2)
+            dst = xi[i][:, 0 : 4 * D].bitcast(F32).rearrange("p (d a) -> p d a", a=2)
             move(on_vector, dst[:, lo:hi, :], src[:, lo:hi, :])
-
-        def weave(i, tag="aw", bufs=1):
-            wb[i] = psum.tile([P, 4 * WC], BF16, name=f"wb{i}", tag=tag, bufs=bufs)
-            for d in range(0, WC, WC // 2):
-                nc.tensor.matmul(
-                    wb[i][:, 4 * d : 4 * (d + WC // 2)],
-                    lhsT=ident_h[:],
-                    rhs=xw[i][:, :, d : d + WC // 2].rearrange("p t d -> p d t"),
-                    start=True,
-                    stop=True,
-                )
-
-        def unweave(i, on_vector=False):
-            move(on_vector, xi[i][:, 4 * VC : 4 * D].bitcast(F32), wb[i][:].bitcast(F32))
 
         def q_x(i, lo, hi):
             s = slice(lo, hi)
@@ -304,6 +294,7 @@ def tile_lambmlpbackwardstep_t_kernel(tc, x_bytes, x_scale, a, dy, w2, w1, m, v,
         nc.vector.memset(ones[:], 1.0)
         make_identity(nc, ident[:])
         nc.vector.tensor_copy(out=ident_h[:], in_=ident[:])
+        nc.vector.tensor_scalar(out=minus2[:], in0=ident[:], scalar1=-2.0, scalar2=None, op0=MULT)
         clamp(0)
         load_a(2)
         load_x(2)
@@ -313,10 +304,7 @@ def tile_lambmlpbackwardstep_t_kernel(tc, x_bytes, x_scale, a, dy, w2, w1, m, v,
         gelu_plain(0, 1)
         for t in range(2):
             widen_pairs(0, t)
-        for t in range(4):
-            widen_rows(0, t, True)
         turn(0, 0)
-        weave(0, "g2")
         turn(0, 1)
         turn(0, 2, "g0", 1)
         turn(0, 3, "g1", 1)
@@ -325,7 +313,6 @@ def tile_lambmlpbackwardstep_t_kernel(tc, x_bytes, x_scale, a, dy, w2, w1, m, v,
         for t in range(2, 4):
             widen_pairs(0, t)
         new_xi(0)
-        unweave(0)
         nc.vector.tensor_tensor(out=ge[0, 0][:], in0=ge[0, 0][:], in1=ge[0, 1][:], op=ADD)
         empty(0, 0)
         empty(0, 1)
@@ -344,7 +331,7 @@ def tile_lambmlpbackwardstep_t_kernel(tc, x_bytes, x_scale, a, dy, w2, w1, m, v,
             widen_pairs(1, t)
         q_dy(0, 0, 4)
         q_w2()
-        join_pairs(0, 0, VC)
+        join_pairs(0, 0, D)
 
         last = NG - 1
         for s in range(1, NG):
@@ -360,31 +347,30 @@ def tile_lambmlpbackwardstep_t_kernel(tc, x_bytes, x_scale, a, dy, w2, w1, m, v,
                 mm1(0, 0)
             empty(s, 0)
             turn(s, 2)
-            mm1(s - 1, 1 if s == 1 else 0)
             empty(s, 1)
             turn(s, 3)
             if s > 1:
-                mm1(s - 1, 1)
-            if s > 1:
+                mm1(s - 1, 0)
                 mm2(s - 2, 1)
             else:
+                mm1(0, 1)
                 w_gram(GS, GT)
             gelu_turned(s, 0)
             gelu_turned(s, 1)
             for t in range(2, 4):
                 widen_pairs(s, t)
-            if s + 1 < NG:
+            if s < last:
                 clamp(s + 1)
+                turn_a(s + 1)
+            if s > 1:
+                empty_sum(s - 1)
+                mm1(s - 1, 1)
             q_x(s - 1, 0, 512)
             if s == 2:
                 w_trace()
             make_da(s - 1, 0)
-            make_da(s - 1, 1)
             q_x(s - 1, 512, D)
-            for t in range(4):
-                widen_rows(s, t)
-            q_da(s - 1)
-            weave(s)
+            make_da(s - 1, 1)
             empty(s, 2)
             if s < last:
                 turn(s + 1, 0)
@@ -396,30 +382,32 @@ def tile_lambmlpbackwardstep_t_kernel(tc, x_bytes, x_scale, a, dy, w2, w1, m, v,
             empty(s, 3)
             if s < last:
                 turn(s + 1, 1)
-            add_nodes(s, 1)
-            mm2(s - 1, 0)
+            add_nodes(s, 1, s == last)
             q_dy(s, 0, 4)
+            q_da(s - 1)
             gelu_plain(s)
-            new_xi(s)
-            unweave(s)
             if s < last:
-                turn_a(s + 1)
+                third_node(s)
+                mm2(s - 1, 0)
+            new_xi(s)
+            if s < last:
                 for t in range(2):
                     widen_pairs(s + 1, t)
-            join_pairs(s, 0, VC)
+            join_pairs(s, 0, D)
             diff(s, 0)
-            diff(s, 1)
+        diff(last, 1)
 
         mm1(last, 0, "tp")
         mm1(last, 1, "tp")
         tot = psum.tile([P, 8], F32, name="tot", tag="aw", bufs=1)
         nc.tensor.matmul(tot[:, 0:1], lhsT=ones[:], rhs=wall[:, 0:1], start=True, stop=True)
         nc.scalar.activation(out=winv[:, 0:1], in_=tot[:, 0:1], func=ACT.Abs_reciprocal_sqrt)
-        for b in (1, 2):
+        for b in range(LIVE):
             mm2(last - 1, b)
         gbank[LIVE] = psum.tile([P, 2 * F], F32, name="g3", tag="dh", bufs=2)
         for i in range(EARLY):
             mm2(i, LIVE)
+        nc.scalar.activation(out=winv2[:, 0:1], in_=winv[:, 0:1], func=ACT.Square)
         make_da(last, 0)
         make_da(last, 1)
         q_x(last, 0, 512)
@@ -430,6 +418,8 @@ def tile_lambmlpbackwardstep_t_kernel(tc, x_bytes, x_scale, a, dy, w2, w1, m, v,
         for i in range(EARLY, NG):
             mm2(i, LIVE)
 
+        vn, rt = {}, {}
+
         def cols(b):
             return slice(2 * F * b, 2 * F * (b + 1))
 
@@ -438,70 +428,84 @@ def tile_lambmlpbackwardstep_t_kernel(tc, x_bytes, x_scale, a, dy, w2, w1, m, v,
 
         def first_moment(b):
             nc.vector.scalar_tensor_tensor(
-                out=mn[:, cols(b)], in0=gbank[b][:], scalar=-2.0 / 3.0 / 64.0, in1=mt[:, cols(b)], op0=MULT, op1=SUB
+                out=mn[:, cols(b)], in0=gbank[b][:], scalar=2.0 / 3.0 / 64.0, in1=mt[:, cols(b)], op0=MULT, op1=ADD
             )
-
-        vn = {}
 
         def open_v(b, tag, bufs):
             vn[b] = psum.tile([P, 2 * F], F32, name=f"vn{b}", tag=tag, bufs=bufs)
             nc.tensor.matmul(vn[b][:], lhsT=ident_h[:], rhs=vt[:, cols(b)], start=True, stop=False)
 
-        def second_moment(b):
+        def second_moment_tensor(b):
             nc.tensor.matmul(vn[b][:], lhsT=ident[:], rhs=sq[:, cols(b)], start=False, stop=True)
 
+        def second_moment_vector(b):
+            nc.vector.tensor_tensor(out=sq[:, cols(b)], in0=sq[:, cols(b)], in1=vt[:, cols(b)], op=ADD)
+
         def inv_root(b, src):
-            nc.scalar.activation(out=sq[:, cols(b)], in_=src, func=ACT.Abs_reciprocal_sqrt, scale=1.0 / 0.6)
+            nc.scalar.activation(out=sq[:, cols(b)], in_=src, func=ACT.Abs_reciprocal_sqrt, scale=1.0 / 60.0)
 
         def ratio(c):
             nc.vector.tensor_tensor(out=mn[:, c], in0=mn[:, c], in1=sq[:, c], op=MULT)
 
-        def decay(c):
-            nc.vector.scalar_tensor_tensor(out=mn[:, c], in0=w1t[:, c], scalar=-0.1, in1=mn[:, c], op0=MULT, op1=ADD)
+        def open_r(b):
+            rt[b] = psum.tile([P, 4, P], F32, name=f"rt{b}", tag=f"g{b}" if b < LIVE else "tp", bufs=1 if b < LIVE else 2)
+            for k in range(4):
+                col = 2 * F * b + P * k
+                nc.tensor.matmul(rt[b][:, k, :], lhsT=w1t[:, col : col + P], rhs=ident_h[:], start=(k == 0), stop=False)
 
-        def r_norm(c, k):
-            nc.scalar.activation(out=sq[:, c], in_=mn[:, c], func=ACT.Square, accum_out=rsum[:, k : k + 1])
-            nc.tensor.matmul(rtot[:, 0:1], lhsT=ones[:], rhs=rsum[:, k : k + 1], start=(k == 0), stop=(k == NB))
+        def add_r(b):
+            for k in range(4):
+                col = 2 * F * b + P * k
+                nc.tensor.matmul(
+                    rt[b][:, k, :], lhsT=mn[:, col : col + P], rhs=ident[:], start=False, stop=(k == 3), is_transpose=True
+                )
+
+        def r_norm(b, k):
+            nc.scalar.activation(
+                out=sq[:, cols(b)], in_=rt[b][:].rearrange("p k q -> p (k q)"), func=ACT.Square, accum_out=rsum[:, k : k + 1]
+            )
+
+        def decay(b):
+            nc.vector.scalar_tensor_tensor(
+                out=mn[:, cols(b)], in0=mn[:, cols(b)], scalar=-1.0, in1=w1t[:, cols(b)], op0=MULT, op1=SUB
+            )
 
         first_moment(0)
         square(1)
-        open_v(0, "dh", 2)
-        open_v(3, "tp", 2)
+        open_v(1, "dh", 2)
+        open_v(0, "tp", 2)
+        second_moment_tensor(1)
         first_moment(2)
         square(0)
-        second_moment(0)
-        nc.vector.tensor_tensor(out=sq[:, cols(1)], in0=sq[:, cols(1)], in1=vt[:, cols(1)], op=ADD)
-        square(3)
-        second_moment(3)
-        first_moment(1)
+        second_moment_tensor(0)
         square(2)
-        open_v(2, "tp", 2)
-        second_moment(2)
         first_moment(3)
-        inv_root(1, sq[:, cols(1)])
-        rtot = psum.tile([P, 8], F32, name="rtot", tag="g0", bufs=1)
+        square(3)
+        first_moment(1)
+        second_moment_vector(2)
+        inv_root(1, vn[1][:])
+        second_moment_vector(3)
+        order = (1, 2, 0, 3)
+        for b in order:
+            open_r(b)
+        rtot = psum.tile([P, 8], F32, name="rtot", tag="aw", bufs=1)
+        inv_root(2, sq[:, cols(2)])
         ratio(cols(1))
+        add_r(1)
         inv_root(0, vn[0][:])
-        ratio(cols(0))
-        nc.scalar.activation(out=winv2[:, 0:1], in_=winv[:, 0:1], func=ACT.Square)
-        inv_root(3, vn[3][:])
-        decay(cols(1))
-        ratio(cols(3))
-        inv_root(2, vn[2][:])
-        r_norm(cols(1), 0)
-        decay(cols(0))
-        r_norm(cols(0), 1)
-        ends = (slice(4 * F, 5 * F), slice(5 * F, 6 * F))
-        decay(cols(3))
-        r_norm(cols(3), 2)
-        for c in ends:
-            ratio(c)
-        for k, c in enumerate(ends):
-            decay(c)
-            r_norm(c, 3 + k)
+        ratio(cols(2))
+        add_r(2)
+        inv_root(3, sq[:, cols(3)])
+        for b in (0, 3):
+            ratio(cols(b))
+            add_r(b)
+        for k, b in enumerate(order):
+            r_norm(b, k)
+            nc.tensor.matmul(rtot[:, 0:1], lhsT=ones[:], rhs=rsum[:, k : k + 1], start=(k == 0), stop=(k == NB - 1))
+            decay(b)
         nc.scalar.activation(out=step[:, 0:1], in_=rtot[:, 0:1], func=ACT.Abs_reciprocal_sqrt, scale=winv2[:, 0:1])
         out_v = out.rearrange("(j p) f -> p j f", p=P)
-        for lo, hi in ((0, 2), (2, 4), (4, 6), (6, 7), (7, 8)):
+        for lo, hi in ((2, 4), (4, 6), (0, 2), (6, 7), (7, 8)):
             c = slice(F * lo, F * hi)
             res = pool.tile([P, (hi - lo) * F], F32, name=f"res{lo}", tag="res", bufs=5)
             nc.vector.scalar_tensor_tensor(out=res[:], in0=mn[:, c], scalar=step[:, 0:1], in1=w1t[:, c], op0=MULT, op1=ADD)

@@ -97,19 +97,14 @@ def tile_lambmlpbackwardstep_t_kernel(tc, x_bytes, x_scale, a, dy, w2, w1, m, v,
                 nc.scalar.copy(out=dst, in_=src)
 
         def clamp(i):
-            ac[i] = pool.tile([P, F, 4], BF16, name=f"ac{i}", tag="ac", bufs=2)
+            ac[i] = pool.tile([P, 4 * F], BF16, name=f"ac{i}", tag="ac", bufs=2)
             nc.vector.tensor_scalar(
-                out=ac[i][:].rearrange("p (c e) t -> p c t e", e=4),
-                in0=at[i][:].rearrange("p t (c e) -> p c t e", e=4),
-                scalar1=7.0,
-                scalar2=-7.0,
-                op0=MIN,
-                op1=MAX,
+                out=ac[i][:], in0=at[i][:].rearrange("p t f -> p (t f)"), scalar1=7.0, scalar2=-7.0, op0=MIN, op1=MAX
             )
 
         def turn_a(i, tag="aw"):
             ta[i] = psum.tile([P, 4, P], F32, name=f"ta{i}", tag=tag, bufs=1)
-            words = ac[i][:].rearrange("p f t -> p (f t)").bitcast(F32)
+            words = ac[i][:].bitcast(F32)
             for k in range(4):
                 nc.tensor.transpose(ta[i][:, k, :], words[:, P * k : P * (k + 1)], ident[:])
 
@@ -121,7 +116,7 @@ def tile_lambmlpbackwardstep_t_kernel(tc, x_bytes, x_scale, a, dy, w2, w1, m, v,
         def gelu_plain(i, n=2):
             ge[i, n] = pool.tile([P, 4 * F], F32, name=f"ge{i}_{n}", tag=f"ge{n}", bufs=2)
             nc.scalar.activation(
-                out=ge[i, n][:], in_=ac[i][:].rearrange("p f t -> p (f t)"), func=ACT.Gelu, bias=offs[:, n : n + 1]
+                out=ge[i, n][:], in_=ac[i][:], func=ACT.Gelu, bias=offs[:, n : n + 1]
             )
 
         def w_gram(lo, hi):
@@ -212,7 +207,7 @@ def tile_lambmlpbackwardstep_t_kernel(tc, x_bytes, x_scale, a, dy, w2, w1, m, v,
             s = slice(512 * h, 512 * (h + 1))
             nc.vector.scalar_tensor_tensor(
                 out=da[i][:, s].rearrange("p (f t) -> p f t", t=4),
-                in0=ge[i, 2][:, s].rearrange("p (f t) -> p f t", t=4),
+                in0=ge[i, 2][:].rearrange("p (t f) -> p f t", t=4)[:, P * h : P * (h + 1), :],
                 scalar=1.0 / ((NODES[0] + NODES[1] - 2 * NODES[2]) * H),
                 in1=dh[i, h][:].rearrange("p t f -> p f t"),
                 op0=MULT,

@@ -27,6 +27,7 @@ NB = NJ // 2
 H = 2.0 ** -21
 NODES = (-9184.0, 3999.0, -7083.0)
 LIVE = 3
+JV = 64
 GS = 10
 GT = 14
 EARLY = 5
@@ -71,7 +72,7 @@ def tile_lambmlpbackwardstep_t_kernel(tc, x_bytes, x_scale, a, dy, w2, w1, m, v,
         dy_v = dy.rearrange("(g p t) d -> g p t d", p=P, t=4)
         x_v = x_bytes.rearrange("(g p t) d -> g p t d", p=P, t=4)
 
-        at, dyt, x8, ac, ge, dyg, dyq, dyqs, dh, da, xp, xi, tp, xw, wb, ta, sb = ({} for k in range(17))
+        at, dyt, x8, ac, ge, dyg, dyq, dyqs, dh, da, xp, xi, tp, xw, wb, ta, sb, odd = ({} for k in range(18))
 
         def load_a(i):
             at[i] = pool.tile([P, 4, F], BF16, name=f"a{i}", tag="a", bufs=3)
@@ -113,11 +114,29 @@ def tile_lambmlpbackwardstep_t_kernel(tc, x_bytes, x_scale, a, dy, w2, w1, m, v,
             src = ta[i][:].rearrange("q k p -> q (k p)").bitcast(BF16).rearrange("q (k p e) -> q k e p", k=4, e=2)
             nc.scalar.activation(out=ge[i, n][:], in_=src, func=ACT.Gelu, bias=offs[:, n : n + 1])
 
-        def gelu_plain(i, n=2):
+        def gelu_plain(i, n):
             ge[i, n] = pool.tile([P, 4 * F], F32, name=f"ge{i}_{n}", tag=f"ge{n}", bufs=2)
-            nc.scalar.activation(
-                out=ge[i, n][:], in_=ac[i][:], func=ACT.Gelu, bias=offs[:, n : n + 1]
-            )
+            nc.scalar.activation(out=ge[i, n][:], in_=ac[i][:], func=ACT.Gelu, bias=offs[:, n : n + 1])
+
+        def slots(i, e):
+            return ge[i, 2][:].rearrange("p (q e t) -> p q e t", e=2, t=4)[:, :, e, :]
+
+        def gelu_third(i, whole):
+            ge[i, 2] = pool.tile([P, 4 * F], F32, name=f"ge{i}_2", tag="ge2", bufs=2)
+            src = ac[i][:].rearrange("p (t q e) -> p t q e", t=4, e=2)
+            if whole:
+                nc.scalar.activation(
+                    out=ge[i, 2][:].rearrange("p (f t) -> p f t", t=4),
+                    in_=ac[i][:].rearrange("p (t f) -> p f t", t=4),
+                    func=ACT.Gelu,
+                    bias=offs[:, 2:3],
+                )
+            else:
+                odd[i] = pool.tile([P, 4, P], F32, name=f"odd{i}", tag="odd", bufs=1)
+                nc.scalar.activation(out=odd[i][:], in_=src[:, :, :, 1], func=ACT.Gelu, bias=offs[:, 2:3])
+                nc.scalar.activation(
+                    out=slots(i, 0), in_=src[:, :, :, 0].rearrange("p t q -> p q t"), func=ACT.Gelu, bias=offs[:, 2:3]
+                )
 
         def w_gram(lo, hi):
             for k in range(lo, hi):
@@ -129,38 +148,39 @@ def tile_lambmlpbackwardstep_t_kernel(tc, x_bytes, x_scale, a, dy, w2, w1, m, v,
                 out=sq[:, 0:P], in0=gram[:], scalar=0.25, in1=ident[:], op0=MULT, op1=MULT, accum_out=wall[:, 0:1]
             )
 
-        def add_nodes(i, h, closed=True):
-            sb[i, h] = psum.tile([P, 2, 2, P], F32, name=f"sb{i}_{h}", tag="dh", bufs=2)
-            for k in range(2):
-                for e in range(2):
-                    for n in range(2):
-                        nc.tensor.matmul(
-                            sb[i, h][:, e, k, :],
-                            lhsT=ge[i, n][:, 2 * h + k, e, :],
-                            rhs=ident[:],
-                            start=(n == 0 if closed else (k, e, n) == (0, 0, 0)),
-                            stop=(n == 1 and closed),
-                            is_transpose=None if (h, k, e, n) == (0, 1, 1, 1) else True,
-                        )
+        def add_nodes(i, e, closed=True):
+            sb[i, e] = psum.tile([P, 4, P], F32, name=f"sb{i}_{e}", tag="dh", bufs=2)
+            for t in range(4):
+                for n in range(2):
+                    nc.tensor.matmul(
+                        sb[i, e][:, t, :],
+                        lhsT=ge[i, n][:, t, e, :],
+                        rhs=ident[:],
+                        start=(n == 0 if closed else (t, n) == (0, 0)),
+                        stop=(n == 1 and closed),
+                        is_transpose=None if (e, t, n) == (0, 3, 1) else True,
+                    )
 
         def third_node(i):
             nc.tensor.matmul(
-                sb[i, 1][:].rearrange("p e k q -> p (e k q)"),
+                sb[i, 1][:].rearrange("p t q -> p (t q)"),
                 lhsT=minus2[:],
-                rhs=ge[i, 2][:, 512:1024].rearrange("p (w e) -> p e w", e=2),
+                rhs=odd[i][:].rearrange("p t q -> p (t q)"),
                 start=False,
                 stop=True,
             )
 
         def empty_sum(i):
-            nc.scalar.copy(
-                out=ge[i, 2][:, 512:1024].rearrange("p (w e) -> p w e", e=2), in_=sb[i, 1][:].rearrange("p e k q -> p (k q) e")
-            )
+            nc.scalar.copy(out=slots(i, 1), in_=sb[i, 1][:].rearrange("p t q -> p q t"))
 
-        def diff(i, h):
-            part = ge[i, 2][:, 512 * h : 512 * (h + 1)].rearrange("p (w e) -> p w e", e=2)
+        def diff(i, e):
             nc.vector.scalar_tensor_tensor(
-                out=part, in0=part, scalar=-2.0, in1=sb[i, h][:].rearrange("p e k q -> p (k q) e"), op0=MULT, op1=ADD
+                out=slots(i, e),
+                in0=slots(i, e),
+                scalar=-2.0,
+                in1=sb[i, e][:].rearrange("p t q -> p q t"),
+                op0=MULT,
+                op1=ADD,
             )
 
         def turn(i, t, tag="tp", bufs=2):
@@ -205,9 +225,13 @@ def tile_lambmlpbackwardstep_t_kernel(tc, x_bytes, x_scale, a, dy, w2, w1, m, v,
             if h == 0:
                 da[i] = pool.tile([P, 4 * F], BF16, name=f"da{i}", tag="da", bufs=2, align_bytes=64)
             s = slice(512 * h, 512 * (h + 1))
+            if i == 0:
+                slope = ge[i, 2][:].rearrange("p (t f) -> p f t", t=4)[:, P * h : P * (h + 1), :]
+            else:
+                slope = ge[i, 2][:, s].rearrange("p (f t) -> p f t", t=4)
             nc.vector.scalar_tensor_tensor(
                 out=da[i][:, s].rearrange("p (f t) -> p f t", t=4),
-                in0=ge[i, 2][:].rearrange("p (t f) -> p f t", t=4)[:, P * h : P * (h + 1), :],
+                in0=slope,
                 scalar=1.0 / ((NODES[0] + NODES[1] - 2 * NODES[2]) * H),
                 in1=dh[i, h][:].rearrange("p t f -> p f t"),
                 op0=MULT,
@@ -357,6 +381,8 @@ def tile_lambmlpbackwardstep_t_kernel(tc, x_bytes, x_scale, a, dy, w2, w1, m, v,
             if s < last:
                 clamp(s + 1)
                 turn_a(s + 1)
+            new_xi(s)
+            join_pairs(s, 0, JV, True)
             if s > 1:
                 empty_sum(s - 1)
                 mm1(s - 1, 1)
@@ -380,15 +406,14 @@ def tile_lambmlpbackwardstep_t_kernel(tc, x_bytes, x_scale, a, dy, w2, w1, m, v,
             add_nodes(s, 1, s == last)
             q_dy(s, 0, 4)
             q_da(s - 1)
-            gelu_plain(s)
+            gelu_third(s, s == last)
             if s < last:
                 third_node(s)
                 mm2(s - 1, 0)
-            new_xi(s)
             if s < last:
                 for t in range(2):
                     widen_pairs(s + 1, t)
-            join_pairs(s, 0, D)
+            join_pairs(s, JV, D)
             diff(s, 0)
         diff(last, 1)
 

@@ -370,6 +370,7 @@ def tile_lambmlpbackwardstep_t_kernel(tc, x_bytes, x_scale, a, dy, w2, w1, m, v,
             turn(s, 3)
             if s > 1:
                 mm1(s - 1, 0)
+                mm2(s - 2, 0)
                 mm2(s - 2, 1)
             else:
                 mm1(0, 1)
@@ -380,7 +381,6 @@ def tile_lambmlpbackwardstep_t_kernel(tc, x_bytes, x_scale, a, dy, w2, w1, m, v,
                 widen_pairs(s, t)
             if s < last:
                 clamp(s + 1)
-                turn_a(s + 1)
             new_xi(s)
             join_pairs(s, 0, JV, True)
             if s > 1:
@@ -392,6 +392,8 @@ def tile_lambmlpbackwardstep_t_kernel(tc, x_bytes, x_scale, a, dy, w2, w1, m, v,
             make_da(s - 1, 0)
             q_x(s - 1, 512, D)
             make_da(s - 1, 1)
+            if s < last:
+                turn_a(s + 1)
             empty(s, 2)
             if s < last:
                 turn(s + 1, 0)
@@ -409,7 +411,6 @@ def tile_lambmlpbackwardstep_t_kernel(tc, x_bytes, x_scale, a, dy, w2, w1, m, v,
             gelu_third(s, s == last)
             if s < last:
                 third_node(s)
-                mm2(s - 1, 0)
             if s < last:
                 for t in range(2):
                     widen_pairs(s + 1, t)

@@ -28,6 +28,7 @@ H = 2.0 ** -21
 NODES = (-9184.0, 3999.0, -7083.0)
 LIVE = 3
 JV = 64
+DL = 192
 GS = 10
 GT = 14
 EARLY = 5
@@ -46,7 +47,6 @@ def tile_lambmlpbackwardstep_t_kernel(tc, x_bytes, x_scale, a, dy, w2, w1, m, v,
         ones = keep.tile([P, P], F32, name="ones")
         ident_h = keep.tile([P, P], BF16, name="ident_h")
         offs = keep.tile([P, 4], F32, name="offs")
-        xs = keep.tile([P, NG, 4], F32, name="xs")
         xq = keep.tile([P, NG, D], U32, name="xq", align_bytes=64)
         xqs = keep.tile([P, NG, D], U8, name="xqs", align_bytes=64)
         daq = keep.tile([P, NG, F], U32, name="daq", align_bytes=64)
@@ -70,9 +70,10 @@ def tile_lambmlpbackwardstep_t_kernel(tc, x_bytes, x_scale, a, dy, w2, w1, m, v,
 
         a_v = a.rearrange("(g p t) f -> g p t f", p=P, t=4)
         dy_v = dy.rearrange("(g p t) d -> g p t d", p=P, t=4)
+        s_v = x_scale.rearrange("(g p t) o -> g p (t o)", p=P, t=4)
         x_v = x_bytes.rearrange("(g p t) d -> g p t d", p=P, t=4)
 
-        at, dyt, x8, ac, ge, dyg, dyq, dyqs, dh, da, xp, xi, tp, xw, wb, ta, sb, odd = ({} for k in range(18))
+        at, dyt, x8, ac, ge, dyg, dyq, dyqs, dh, da, xp, xi, tp, xw, wb, ta, sb, odd, xs = ({} for k in range(19))
 
         def load_a(i):
             at[i] = pool.tile([P, 4, F], BF16, name=f"a{i}", tag="a", bufs=3)
@@ -82,7 +83,13 @@ def tile_lambmlpbackwardstep_t_kernel(tc, x_bytes, x_scale, a, dy, w2, w1, m, v,
             dyt[i, u] = pool.tile([P, 2, D], BF16, name=f"dy{i}_{u}", tag="dy", bufs=6)
             nc.sync.dma_start(out=dyt[i, u][:], in_=dy_v[i][:, 2 * u : 2 * u + 2, :])
 
+        def load_scale(i, queue):
+            xs[i] = keep.tile([P, 4], F32, name=f"xs{i}")
+            queue.dma_start(out=xs[i][:], in_=s_v[i])
+
         def load_x(i, pieces=1):
+            if i > 0:
+                load_scale(i, nc.sync)
             x8[i] = pool.tile([P, 4, D], U8, name=f"x8_{i}", tag="x8", bufs=3)
             n = 4 // pieces
             for t in range(0, 4, n):
@@ -244,12 +251,23 @@ def tile_lambmlpbackwardstep_t_kernel(tc, x_bytes, x_scale, a, dy, w2, w1, m, v,
         def widen_pairs(i, t):
             if t == 0:
                 xp[i] = pool.tile([P, 2, D, 2], BF16, name=f"xp{i}", tag="xp", bufs=2)
+            width = D - DL if i == NG - 1 else D
             nc.vector.tensor_scalar(
-                out=xp[i][:, t // 2, :, t % 2],
-                in0=x8[i][:, t, 0:D].bitcast(FP8),
-                scalar1=xs[:, i, t : t + 1],
+                out=xp[i][:, t // 2, 0:width, t % 2],
+                in0=x8[i][:, t, 0:width].bitcast(FP8),
+                scalar1=xs[i][:, t : t + 1],
                 scalar2=None,
                 op0=MULT,
+            )
+
+        def widen_rest(i):
+            rows = pool.tile([P, 4, DL], BF16, name="rows", tag="rows", bufs=1)
+            for t in range(4):
+                nc.scalar.activation(
+                    out=rows[:, t, :], in_=x8[i][:, t, D - DL : D].bitcast(FP8), func=ACT.Copy, scale=xs[i][:, t : t + 1]
+                )
+            nc.scalar.copy(
+                out=xi[i][:, 4 * (D - DL) : 4 * D].rearrange("p (d t) -> p d t", t=4), in_=rows[:].rearrange("p t d -> p d t")
             )
 
         def new_xi(i):
@@ -298,7 +316,7 @@ def tile_lambmlpbackwardstep_t_kernel(tc, x_bytes, x_scale, a, dy, w2, w1, m, v,
             )
 
         load_a(0)
-        nc.scalar.dma_start(out=xs[:], in_=x_scale.rearrange("(g p t) o -> p g (t o)", p=P, t=4))
+        load_scale(0, nc.scalar)
         load_x(0, 2)
         load_dy(0, 0)
         load_dy(0, 1)
@@ -381,12 +399,12 @@ def tile_lambmlpbackwardstep_t_kernel(tc, x_bytes, x_scale, a, dy, w2, w1, m, v,
                 widen_pairs(s, t)
             if s < last:
                 clamp(s + 1)
-            new_xi(s)
-            join_pairs(s, 0, JV, True)
             if s > 1:
                 empty_sum(s - 1)
                 mm1(s - 1, 1)
             q_x(s - 1, 0, 512)
+            new_xi(s)
+            join_pairs(s, 0, JV, True)
             if s == 2:
                 w_trace()
             make_da(s - 1, 0)
@@ -414,9 +432,10 @@ def tile_lambmlpbackwardstep_t_kernel(tc, x_bytes, x_scale, a, dy, w2, w1, m, v,
             if s < last:
                 for t in range(2):
                     widen_pairs(s + 1, t)
-            join_pairs(s, JV, D)
+            join_pairs(s, JV, D if s < last else D - DL)
             diff(s, 0)
         diff(last, 1)
+        widen_rest(last)
 
         mm1(last, 0, "tp")
         mm1(last, 1, "tp")

@@ -20,17 +20,21 @@ T, D, F = 4096, 1024, 256
 FLOPS = 4 * T * D * F
 
 P = 128
-NG = T // 512
-NC = D // 512
+GROUP = 4 * P
+NG = T // GROUP
+NC = D // GROUP
 NJ = D // P
 NB = NJ // 2
-H = 2.0 ** -21
-NODES = (-9184.0, 3999.0, -7083.0)
+BANK = 2 * F
 LIVE = 3
-JV = 64
-DL = 192
-GS = 10
-GT = 14
+
+GRID = 2.0**-21
+NODES = (-9184.0, 3999.0, -7083.0)
+CLAMP = 7.0
+
+JOIN_VECTOR = 64
+REST_SCALAR = 256
+GRAM_HEAD, GRAM_STEP = 8, 12
 EARLY = 5
 
 
@@ -66,14 +70,12 @@ def tile_lambmlpbackwardstep_t_kernel(tc, x_bytes, x_scale, a, dy, w2, w1, m, v,
         winv2 = keep.tile([P, 8], F32, name="winv2")
         step = keep.tile([P, 8], F32, name="step")
 
-        gbank = {}
-
         a_v = a.rearrange("(g p t) f -> g p t f", p=P, t=4)
         dy_v = dy.rearrange("(g p t) d -> g p t d", p=P, t=4)
         s_v = x_scale.rearrange("(g p t) o -> g p (t o)", p=P, t=4)
         x_v = x_bytes.rearrange("(g p t) d -> g p t d", p=P, t=4)
 
-        at, dyt, x8, ac, ge, dyg, dyq, dyqs, dh, da, xp, xi, tp, xw, wb, ta, sb, odd, xs = ({} for k in range(19))
+        at, ac, ta, ge, odd, sb, dyt, tp, dyg, dyq, dyqs, dh, da, xs, x8, xp, xi, gbank = ({} for k in range(18))
 
         def load_a(i):
             at[i] = pool.tile([P, 4, F], BF16, name=f"a{i}", tag="a", bufs=3)
@@ -98,20 +100,14 @@ def tile_lambmlpbackwardstep_t_kernel(tc, x_bytes, x_scale, a, dy, w2, w1, m, v,
         def load_rows(dst, src):
             nc.sync.dma_start(out=dst[:].rearrange("p (j f) -> p j f", f=F), in_=src.rearrange("(j p) f -> p j f", p=P))
 
-        def move(on_vector, dst, src):
-            if on_vector:
-                nc.vector.tensor_copy(out=dst, in_=src)
-            else:
-                nc.scalar.copy(out=dst, in_=src)
-
         def clamp(i):
             ac[i] = pool.tile([P, 4 * F], BF16, name=f"ac{i}", tag="ac", bufs=2)
             nc.vector.tensor_scalar(
-                out=ac[i][:], in0=at[i][:].rearrange("p t f -> p (t f)"), scalar1=7.0, scalar2=-7.0, op0=MIN, op1=MAX
+                out=ac[i][:], in0=at[i][:].rearrange("p t f -> p (t f)"), scalar1=CLAMP, scalar2=-CLAMP, op0=MIN, op1=MAX
             )
 
-        def turn_a(i, tag="aw"):
-            ta[i] = psum.tile([P, 4, P], F32, name=f"ta{i}", tag=tag, bufs=1)
+        def turn_a(i):
+            ta[i] = psum.tile([P, 4, P], F32, name=f"ta{i}", tag="aw", bufs=1)
             words = ac[i][:].bitcast(F32)
             for k in range(4):
                 nc.tensor.transpose(ta[i][:, k, :], words[:, P * k : P * (k + 1)], ident[:])
@@ -197,21 +193,19 @@ def tile_lambmlpbackwardstep_t_kernel(tc, x_bytes, x_scale, a, dy, w2, w1, m, v,
                 for u in range(2):
                     nc.tensor.transpose(tp[i, t][:, c, u, :], words[:, 256 * c + u : 256 * (c + 1) : 2], ident[:])
 
-        def empty(i, t, on_vector=False):
+        def empty(i, t):
             if t == 0:
                 dyg[i] = pool.tile([P, 4, D], BF16, name=f"dyg{i}", tag="dyg", bufs=2, align_bytes=64)
             dst = dyg[i][:, t, :].bitcast(F32).rearrange("q (c r u) -> q c r u", c=NC, u=2)
-            move(on_vector, dst, tp[i, t][:].rearrange("q c u r -> q c r u"))
+            nc.scalar.copy(out=dst, in_=tp[i, t][:].rearrange("q c u r -> q c r u"))
 
-        def q_dy(i, lo, hi):
-            if lo == 0:
-                dyq[i] = pool.tile([P, 4, NC, P], U32, name=f"dyq{i}", tag="dyq", bufs=2, align_bytes=64)
-                dyqs[i] = pool.tile([P, 4, NC, P], U8, name=f"dyqs{i}", tag="dyqs", bufs=2, align_bytes=64)
-            s = slice(lo, hi)
+        def q_dy(i):
+            dyq[i] = pool.tile([P, 4, NC, P], U32, name=f"dyq{i}", tag="dyq", bufs=2, align_bytes=64)
+            dyqs[i] = pool.tile([P, 4, NC, P], U8, name=f"dyqs{i}", tag="dyqs", bufs=2, align_bytes=64)
             nc.vector.quantize_mx(
-                out=dyq[i][:, s].rearrange("p t c r -> p (t c r)").bitcast(FP8X4),
-                scales=dyqs[i][:, s].rearrange("p t c r -> p (t c r)"),
-                in_=dyg[i][:, s].rearrange("p t k -> p (t k)"),
+                out=dyq[i][:].rearrange("p t c r -> p (t c r)").bitcast(FP8X4),
+                scales=dyqs[i][:].rearrange("p t c r -> p (t c r)"),
+                in_=dyg[i][:].rearrange("p t k -> p (t k)"),
             )
 
         def mm1(i, h, tag="dh"):
@@ -231,7 +225,7 @@ def tile_lambmlpbackwardstep_t_kernel(tc, x_bytes, x_scale, a, dy, w2, w1, m, v,
         def make_da(i, h):
             if h == 0:
                 da[i] = pool.tile([P, 4 * F], BF16, name=f"da{i}", tag="da", bufs=2, align_bytes=64)
-            s = slice(512 * h, 512 * (h + 1))
+            s = slice(BANK * h, BANK * (h + 1))
             if i == 0:
                 slope = ge[i, 2][:].rearrange("p (t f) -> p f t", t=4)[:, P * h : P * (h + 1), :]
             else:
@@ -239,7 +233,7 @@ def tile_lambmlpbackwardstep_t_kernel(tc, x_bytes, x_scale, a, dy, w2, w1, m, v,
             nc.vector.scalar_tensor_tensor(
                 out=da[i][:, s].rearrange("p (f t) -> p f t", t=4),
                 in0=slope,
-                scalar=1.0 / ((NODES[0] + NODES[1] - 2 * NODES[2]) * H),
+                scalar=1.0 / ((NODES[0] + NODES[1] - 2 * NODES[2]) * GRID),
                 in1=dh[i, h][:].rearrange("p t f -> p f t"),
                 op0=MULT,
                 op1=MULT,
@@ -251,7 +245,7 @@ def tile_lambmlpbackwardstep_t_kernel(tc, x_bytes, x_scale, a, dy, w2, w1, m, v,
         def widen_pairs(i, t):
             if t == 0:
                 xp[i] = pool.tile([P, 2, D, 2], BF16, name=f"xp{i}", tag="xp", bufs=2)
-            width = D - DL if i == NG - 1 else D
+            width = D - REST_SCALAR if i == NG - 1 else D
             nc.vector.tensor_scalar(
                 out=xp[i][:, t // 2, 0:width, t % 2],
                 in0=x8[i][:, t, 0:width].bitcast(FP8),
@@ -260,23 +254,26 @@ def tile_lambmlpbackwardstep_t_kernel(tc, x_bytes, x_scale, a, dy, w2, w1, m, v,
                 op0=MULT,
             )
 
-        def widen_rest(i):
-            rows = pool.tile([P, 4, DL], BF16, name="rows", tag="rows", bufs=1)
+        def widen_rows(i):
+            rows = pool.tile([P, 4, REST_SCALAR], BF16, name="rows", tag="rows", bufs=1)
             for t in range(4):
                 nc.scalar.activation(
-                    out=rows[:, t, :], in_=x8[i][:, t, D - DL : D].bitcast(FP8), func=ACT.Copy, scale=xs[i][:, t : t + 1]
+                    out=rows[:, t, :], in_=x8[i][:, t, D - REST_SCALAR : D].bitcast(FP8), func=ACT.Copy, scale=xs[i][:, t : t + 1]
                 )
+            return rows
+
+        def join_rows(i, rows):
             nc.scalar.copy(
-                out=xi[i][:, 4 * (D - DL) : 4 * D].rearrange("p (d t) -> p d t", t=4), in_=rows[:].rearrange("p t d -> p d t")
+                out=xi[i][:, 4 * (D - REST_SCALAR) : 4 * D].rearrange("p (d t) -> p d t", t=4), in_=rows[:].rearrange("p t d -> p d t")
             )
 
         def new_xi(i):
             xi[i] = pool.tile([P, D * 4], BF16, name=f"xi{i}", tag="xi", bufs=2, align_bytes=64)
 
-        def join_pairs(i, lo, hi, on_vector=False):
+        def join_pairs(i, lo, hi, copy):
             src = xp[i][:].rearrange("p a d e -> p (a d e)").bitcast(F32).rearrange("p (a d) -> p d a", a=2)
-            dst = xi[i][:, 0 : 4 * D].bitcast(F32).rearrange("p (d a) -> p d a", a=2)
-            move(on_vector, dst[:, lo:hi, :], src[:, lo:hi, :])
+            dst = xi[i][:].bitcast(F32).rearrange("p (d a) -> p d a", a=2)
+            copy(out=dst[:, lo:hi, :], in_=src[:, lo:hi, :])
 
         def q_x(i, lo, hi):
             s = slice(lo, hi)
@@ -286,7 +283,7 @@ def tile_lambmlpbackwardstep_t_kernel(tc, x_bytes, x_scale, a, dy, w2, w1, m, v,
 
         def mm2(i, b):
             if i == 0 and b < LIVE:
-                gbank[b] = psum.tile([P, 2 * F], F32, name=f"g{b}", tag=f"g{b}", bufs=1)
+                gbank[b] = psum.tile([P, BANK], F32, name=f"g{b}", tag=f"g{b}", bufs=1)
             for j in (2 * b, 2 * b + 1):
                 nc.tensor.matmul_mx(
                     out=gbank[b][:, F * (j % 2) : F * (j % 2 + 1)],
@@ -327,7 +324,7 @@ def tile_lambmlpbackwardstep_t_kernel(tc, x_bytes, x_scale, a, dy, w2, w1, m, v,
         load_rows(w1t, w1)
         load_dy(1, 1)
         for k, n in enumerate(NODES):
-            nc.vector.memset(offs[:, k : k + 1], n * H)
+            nc.vector.memset(offs[:, k : k + 1], n * GRID)
         nc.vector.memset(ones[:], 1.0)
         make_identity(nc, ident[:])
         nc.vector.tensor_copy(out=ident_h[:], in_=ident[:])
@@ -358,7 +355,7 @@ def tile_lambmlpbackwardstep_t_kernel(tc, x_bytes, x_scale, a, dy, w2, w1, m, v,
         turn(1, 0)
         turn(1, 1)
         gram = psum.tile([P, P], F32, name="gram", tag="g2", bufs=1)
-        w_gram(0, GS)
+        w_gram(0, GRAM_HEAD)
         nc.vector.scalar_tensor_tensor(out=ge[0, 2][:], in0=ge[0, 2][:], scalar=-2.0, in1=ge[0, 0][:], op0=MULT, op1=ADD)
         empty(0, 2)
         empty(0, 3)
@@ -366,9 +363,9 @@ def tile_lambmlpbackwardstep_t_kernel(tc, x_bytes, x_scale, a, dy, w2, w1, m, v,
         empty_w2(1, w2_banks[1])
         for t in range(2):
             widen_pairs(1, t)
-        q_dy(0, 0, 4)
+        q_dy(0)
         q_w2()
-        join_pairs(0, 0, D)
+        join_pairs(0, 0, D, nc.scalar.copy)
 
         last = NG - 1
         for s in range(1, NG):
@@ -392,7 +389,7 @@ def tile_lambmlpbackwardstep_t_kernel(tc, x_bytes, x_scale, a, dy, w2, w1, m, v,
                 mm2(s - 2, 1)
             else:
                 mm1(0, 1)
-                w_gram(GS, GT)
+                w_gram(GRAM_HEAD, GRAM_STEP)
             gelu_turned(s, 0)
             gelu_turned(s, 1)
             for t in range(2, 4):
@@ -402,13 +399,13 @@ def tile_lambmlpbackwardstep_t_kernel(tc, x_bytes, x_scale, a, dy, w2, w1, m, v,
             if s > 1:
                 empty_sum(s - 1)
                 mm1(s - 1, 1)
-            q_x(s - 1, 0, 512)
+            q_x(s - 1, 0, D // 2)
             new_xi(s)
-            join_pairs(s, 0, JV, True)
+            join_pairs(s, 0, JOIN_VECTOR, nc.vector.tensor_copy)
             if s == 2:
                 w_trace()
             make_da(s - 1, 0)
-            q_x(s - 1, 512, D)
+            q_x(s - 1, D // 2, D)
             make_da(s - 1, 1)
             if s < last:
                 turn_a(s + 1)
@@ -419,23 +416,24 @@ def tile_lambmlpbackwardstep_t_kernel(tc, x_bytes, x_scale, a, dy, w2, w1, m, v,
             if s > 1:
                 mm2(s - 2, 2)
             else:
-                w_gram(GT, 2 * NJ)
+                w_gram(GRAM_STEP, 2 * NJ)
             empty(s, 3)
             if s < last:
                 turn(s + 1, 1)
             add_nodes(s, 1, s == last)
-            q_dy(s, 0, 4)
+            q_dy(s)
             q_da(s - 1)
             gelu_third(s, s == last)
             if s < last:
                 third_node(s)
-            if s < last:
                 for t in range(2):
                     widen_pairs(s + 1, t)
-            join_pairs(s, JV, D if s < last else D - DL)
+            else:
+                rows = widen_rows(s)
+            join_pairs(s, JOIN_VECTOR, D if s < last else D - REST_SCALAR, nc.scalar.copy)
             diff(s, 0)
         diff(last, 1)
-        widen_rest(last)
+        join_rows(last, rows)
 
         mm1(last, 0, "tp")
         mm1(last, 1, "tp")
@@ -444,15 +442,14 @@ def tile_lambmlpbackwardstep_t_kernel(tc, x_bytes, x_scale, a, dy, w2, w1, m, v,
         nc.scalar.activation(out=winv[:, 0:1], in_=tot[:, 0:1], func=ACT.Abs_reciprocal_sqrt)
         for b in range(LIVE):
             mm2(last - 1, b)
-        gbank[LIVE] = psum.tile([P, 2 * F], F32, name="g3", tag="dh", bufs=2)
+        gbank[LIVE] = psum.tile([P, BANK], F32, name="g3", tag="dh", bufs=2)
         for i in range(EARLY):
             mm2(i, LIVE)
-        nc.scalar.activation(out=winv2[:, 0:1], in_=winv[:, 0:1], func=ACT.Square)
         make_da(last, 0)
         make_da(last, 1)
-        q_x(last, 0, 512)
+        q_x(last, 0, D // 2)
         q_da(last)
-        q_x(last, 512, D)
+        q_x(last, D // 2, D)
         for b in range(LIVE):
             mm2(last, b)
         for i in range(EARLY, NG):
@@ -461,7 +458,7 @@ def tile_lambmlpbackwardstep_t_kernel(tc, x_bytes, x_scale, a, dy, w2, w1, m, v,
         vn, rt = {}, {}
 
         def cols(b):
-            return slice(2 * F * b, 2 * F * (b + 1))
+            return slice(BANK * b, BANK * (b + 1))
 
         def square(b):
             nc.scalar.activation(out=sq[:, cols(b)], in_=gbank[b][:], func=ACT.Square, scale=(2.0 / 3.0) ** 0.5 / 64.0)
@@ -472,7 +469,7 @@ def tile_lambmlpbackwardstep_t_kernel(tc, x_bytes, x_scale, a, dy, w2, w1, m, v,
             )
 
         def open_v(b, tag, bufs):
-            vn[b] = psum.tile([P, 2 * F], F32, name=f"vn{b}", tag=tag, bufs=bufs)
+            vn[b] = psum.tile([P, BANK], F32, name=f"vn{b}", tag=tag, bufs=bufs)
             nc.tensor.matmul(vn[b][:], lhsT=ident_h[:], rhs=vt[:, cols(b)], start=True, stop=False)
 
         def second_moment_tensor(b):
@@ -484,18 +481,18 @@ def tile_lambmlpbackwardstep_t_kernel(tc, x_bytes, x_scale, a, dy, w2, w1, m, v,
         def inv_root(b, src):
             nc.scalar.activation(out=sq[:, cols(b)], in_=src, func=ACT.Abs_reciprocal_sqrt, scale=1.0 / 60.0)
 
-        def ratio(c):
-            nc.vector.tensor_tensor(out=mn[:, c], in0=mn[:, c], in1=sq[:, c], op=MULT)
+        def ratio(b):
+            nc.vector.tensor_tensor(out=mn[:, cols(b)], in0=mn[:, cols(b)], in1=sq[:, cols(b)], op=MULT)
 
         def open_r(b):
             rt[b] = psum.tile([P, 4, P], F32, name=f"rt{b}", tag=f"g{b}" if b < LIVE else "tp", bufs=1 if b < LIVE else 2)
             for k in range(4):
-                col = 2 * F * b + P * k
+                col = BANK * b + P * k
                 nc.tensor.matmul(rt[b][:, k, :], lhsT=w1t[:, col : col + P], rhs=ident_h[:], start=(k == 0), stop=False)
 
         def add_r(b):
             for k in range(4):
-                col = 2 * F * b + P * k
+                col = BANK * b + P * k
                 nc.tensor.matmul(
                     rt[b][:, k, :], lhsT=mn[:, col : col + P], rhs=ident[:], start=False, stop=(k == 3), is_transpose=True
                 )
@@ -530,14 +527,15 @@ def tile_lambmlpbackwardstep_t_kernel(tc, x_bytes, x_scale, a, dy, w2, w1, m, v,
             open_r(b)
         rtot = psum.tile([P, 8], F32, name="rtot", tag="aw", bufs=1)
         inv_root(2, sq[:, cols(2)])
-        ratio(cols(1))
+        ratio(1)
         add_r(1)
         inv_root(0, vn[0][:])
-        ratio(cols(2))
+        ratio(2)
         add_r(2)
         inv_root(3, sq[:, cols(3)])
+        nc.scalar.activation(out=winv2[:, 0:1], in_=winv[:, 0:1], func=ACT.Square)
         for b in (0, 3):
-            ratio(cols(b))
+            ratio(b)
             add_r(b)
         for k, b in enumerate(order):
             r_norm(b, k)

@@ -26,11 +26,15 @@ NC = D // GROUP
 NJ = D // P
 NB = NJ // 2
 BANK = 2 * F
+WORDS = GROUP // 2
+AHEAD = 2
 LIVE = 3
 
 GRID = 2.0**-21
 NODES = (-9184.0, 3999.0, -7083.0)
 CLAMP = 7.0
+G_SCALE = 1.0 / 64.0
+NEW_SHARE = 0.4 / 0.6
 
 JOIN_VECTOR = 64
 REST_SCALAR = 256
@@ -78,11 +82,11 @@ def tile_lambmlpbackwardstep_t_kernel(tc, x_bytes, x_scale, a, dy, w2, w1, m, v,
         at, ac, ta, ge, odd, sb, dyt, tp, dyg, dyq, dyqs, dh, da, xs, x8, xp, xi, gbank = ({} for k in range(18))
 
         def load_a(i):
-            at[i] = pool.tile([P, 4, F], BF16, name=f"a{i}", tag="a", bufs=3)
+            at[i] = pool.tile([P, 4, F], BF16, name=f"a{i}", tag="a", bufs=AHEAD + 1)
             nc.sync.dma_start(out=at[i][:], in_=a_v[i])
 
         def load_dy(i, u):
-            dyt[i, u] = pool.tile([P, 2, D], BF16, name=f"dy{i}_{u}", tag="dy", bufs=6)
+            dyt[i, u] = pool.tile([P, 2, D], BF16, name=f"dy{i}_{u}", tag="dy", bufs=2 * (AHEAD + 1))
             nc.sync.dma_start(out=dyt[i, u][:], in_=dy_v[i][:, 2 * u : 2 * u + 2, :])
 
         def load_scale(i, queue):
@@ -92,7 +96,7 @@ def tile_lambmlpbackwardstep_t_kernel(tc, x_bytes, x_scale, a, dy, w2, w1, m, v,
         def load_x(i, pieces=1):
             if i > 0:
                 load_scale(i, nc.sync)
-            x8[i] = pool.tile([P, 4, D], U8, name=f"x8_{i}", tag="x8", bufs=3)
+            x8[i] = pool.tile([P, 4, D], U8, name=f"x8_{i}", tag="x8", bufs=AHEAD + 1)
             n = 4 // pieces
             for t in range(0, 4, n):
                 nc.sync.dma_start(out=x8[i][:, t : t + n, :], in_=x_v[i][:, t : t + n, :])
@@ -191,7 +195,7 @@ def tile_lambmlpbackwardstep_t_kernel(tc, x_bytes, x_scale, a, dy, w2, w1, m, v,
             words = dyt[i, t // 2][:, t % 2, :].bitcast(F32)
             for c in range(NC):
                 for u in range(2):
-                    nc.tensor.transpose(tp[i, t][:, c, u, :], words[:, 256 * c + u : 256 * (c + 1) : 2], ident[:])
+                    nc.tensor.transpose(tp[i, t][:, c, u, :], words[:, WORDS * c + u : WORDS * (c + 1) : 2], ident[:])
 
         def empty(i, t):
             if t == 0:
@@ -258,13 +262,17 @@ def tile_lambmlpbackwardstep_t_kernel(tc, x_bytes, x_scale, a, dy, w2, w1, m, v,
             rows = pool.tile([P, 4, REST_SCALAR], BF16, name="rows", tag="rows", bufs=1)
             for t in range(4):
                 nc.scalar.activation(
-                    out=rows[:, t, :], in_=x8[i][:, t, D - REST_SCALAR : D].bitcast(FP8), func=ACT.Copy, scale=xs[i][:, t : t + 1]
+                    out=rows[:, t, :],
+                    in_=x8[i][:, t, D - REST_SCALAR : D].bitcast(FP8),
+                    func=ACT.Copy,
+                    scale=xs[i][:, t : t + 1],
                 )
             return rows
 
         def join_rows(i, rows):
             nc.scalar.copy(
-                out=xi[i][:, 4 * (D - REST_SCALAR) : 4 * D].rearrange("p (d t) -> p d t", t=4), in_=rows[:].rearrange("p t d -> p d t")
+                out=xi[i][:, 4 * (D - REST_SCALAR) : 4 * D].rearrange("p (d t) -> p d t", t=4),
+                in_=rows[:].rearrange("p t d -> p d t"),
             )
 
         def new_xi(i):
@@ -300,7 +308,7 @@ def tile_lambmlpbackwardstep_t_kernel(tc, x_bytes, x_scale, a, dy, w2, w1, m, v,
             words = w2r[:, h, :].bitcast(F32)
             for c in range(NC):
                 for u in range(2):
-                    nc.tensor.transpose(bank[:, c, u, :], words[:, 256 * c + u : 256 * (c + 1) : 2], ident[:])
+                    nc.tensor.transpose(bank[:, c, u, :], words[:, WORDS * c + u : WORDS * (c + 1) : 2], ident[:])
             return bank
 
         def empty_w2(h, bank):
@@ -309,7 +317,9 @@ def tile_lambmlpbackwardstep_t_kernel(tc, x_bytes, x_scale, a, dy, w2, w1, m, v,
 
         def q_w2():
             nc.vector.quantize_mx(
-                out=w2q[:].rearrange("p c f -> p (c f)").bitcast(FP8X4), scales=w2qs[:].rearrange("p c f -> p (c f)"), in_=w2g[:]
+                out=w2q[:].rearrange("p c f -> p (c f)").bitcast(FP8X4),
+                scales=w2qs[:].rearrange("p c f -> p (c f)"),
+                in_=w2g[:],
             )
 
         load_a(0)
@@ -327,8 +337,8 @@ def tile_lambmlpbackwardstep_t_kernel(tc, x_bytes, x_scale, a, dy, w2, w1, m, v,
             nc.vector.memset(offs[:, k : k + 1], n * GRID)
         nc.vector.memset(ones[:], 1.0)
         make_identity(nc, ident[:])
-        nc.vector.tensor_copy(out=ident_h[:], in_=ident[:])
-        nc.vector.tensor_scalar(out=minus2[:], in0=ident[:], scalar1=-2.0, scalar2=None, op0=MULT)
+        make_identity(nc, ident_h[:])
+        nc.gpsimd.tensor_scalar(out=minus2[:], in0=ident[:], scalar1=-2.0, scalar2=0.0, op0=MULT, op1=ADD)
         clamp(0)
         load_a(2)
         load_x(2)
@@ -369,12 +379,12 @@ def tile_lambmlpbackwardstep_t_kernel(tc, x_bytes, x_scale, a, dy, w2, w1, m, v,
 
         last = NG - 1
         for s in range(1, NG):
-            if s + 2 < NG:
-                load_a(s + 2)
-                load_x(s + 2)
-                load_dy(s + 2, 0)
-                load_dy(s + 2, 1)
-            if s == 5:
+            if s + AHEAD < NG:
+                load_a(s + AHEAD)
+                load_x(s + AHEAD)
+                load_dy(s + AHEAD, 0)
+                load_dy(s + AHEAD, 1)
+            if s + AHEAD == last:
                 load_rows(mt, m)
                 load_rows(vt, v)
             if s == 1:
@@ -461,11 +471,11 @@ def tile_lambmlpbackwardstep_t_kernel(tc, x_bytes, x_scale, a, dy, w2, w1, m, v,
             return slice(BANK * b, BANK * (b + 1))
 
         def square(b):
-            nc.scalar.activation(out=sq[:, cols(b)], in_=gbank[b][:], func=ACT.Square, scale=(2.0 / 3.0) ** 0.5 / 64.0)
+            nc.scalar.activation(out=sq[:, cols(b)], in_=gbank[b][:], func=ACT.Square, scale=NEW_SHARE**0.5 * G_SCALE)
 
         def first_moment(b):
             nc.vector.scalar_tensor_tensor(
-                out=mn[:, cols(b)], in0=gbank[b][:], scalar=2.0 / 3.0 / 64.0, in1=mt[:, cols(b)], op0=MULT, op1=ADD
+                out=mn[:, cols(b)], in0=gbank[b][:], scalar=NEW_SHARE * G_SCALE, in1=mt[:, cols(b)], op0=MULT, op1=ADD
             )
 
         def open_v(b, tag, bufs):
@@ -499,7 +509,10 @@ def tile_lambmlpbackwardstep_t_kernel(tc, x_bytes, x_scale, a, dy, w2, w1, m, v,
 
         def r_norm(b, k):
             nc.scalar.activation(
-                out=sq[:, cols(b)], in_=rt[b][:].rearrange("p k q -> p (k q)"), func=ACT.Square, accum_out=rsum[:, k : k + 1]
+                out=sq[:, cols(b)],
+                in_=rt[b][:].rearrange("p k q -> p (k q)"),
+                func=ACT.Square,
+                accum_out=rsum[:, k : k + 1],
             )
 
         def decay(b):
@@ -534,7 +547,7 @@ def tile_lambmlpbackwardstep_t_kernel(tc, x_bytes, x_scale, a, dy, w2, w1, m, v,
         add_r(2)
         inv_root(3, sq[:, cols(3)])
         nc.scalar.activation(out=winv2[:, 0:1], in_=winv[:, 0:1], func=ACT.Square)
-        for b in (0, 3):
+        for b in order[2:]:
             ratio(b)
             add_r(b)
         for k, b in enumerate(order):
@@ -543,8 +556,9 @@ def tile_lambmlpbackwardstep_t_kernel(tc, x_bytes, x_scale, a, dy, w2, w1, m, v,
             decay(b)
         nc.scalar.activation(out=step[:, 0:1], in_=rtot[:, 0:1], func=ACT.Abs_reciprocal_sqrt, scale=winv2[:, 0:1])
         out_v = out.rearrange("(j p) f -> p j f", p=P)
-        for lo, hi in ((2, 4), (4, 6), (0, 2), (6, 7), (7, 8)):
+        pieces = [(2 * b, 2 * b + 2) for b in order[:-1]] + [(NJ - 2, NJ - 1), (NJ - 1, NJ)]
+        for lo, hi in pieces:
             c = slice(F * lo, F * hi)
-            res = pool.tile([P, (hi - lo) * F], F32, name=f"res{lo}", tag="res", bufs=5)
+            res = pool.tile([P, (hi - lo) * F], F32, name=f"res{lo}", tag="res", bufs=len(pieces))
             nc.vector.scalar_tensor_tensor(out=res[:], in0=mn[:, c], scalar=step[:, 0:1], in1=w1t[:, c], op0=MULT, op1=ADD)
             nc.sync.dma_start(out=out_v[:, lo:hi, :], in_=res[:].rearrange("p (j f) -> p j f", f=F))

@@ -36,10 +36,13 @@ CLAMP = 7.0
 G_SCALE = 1.0 / 64.0
 NEW_SHARE = 0.4 / 0.6
 
-JOIN_VECTOR = 64
-REST_SCALAR = 256
-GRAM_HEAD, GRAM_STEP = 8, 12
+WOVEN = 320
+LACED = 192
+ROWS = WOVEN + LACED
+REST = 256
+JOIN_HEAD = 896
 EARLY = 5
+GRAM_HEAD, GRAM_STEP = 8, 12
 
 
 def tile_lambmlpbackwardstep_t_kernel(tc, x_bytes, x_scale, a, dy, w2, w1, m, v, out):
@@ -51,9 +54,9 @@ def tile_lambmlpbackwardstep_t_kernel(tc, x_bytes, x_scale, a, dy, w2, w1, m, v,
         ctx.enter_context(tc.manual_schedule())
 
         ident = keep.tile([P, P], F32, name="ident")
-        minus2 = keep.tile([P, P], F32, name="minus2")
         ones = keep.tile([P, P], F32, name="ones")
         ident_h = keep.tile([P, P], BF16, name="ident_h")
+        minus_h = keep.tile([P, P], BF16, name="minus_h")
         offs = keep.tile([P, 4], F32, name="offs")
         xq = keep.tile([P, NG, D], U32, name="xq", align_bytes=64)
         xqs = keep.tile([P, NG, D], U8, name="xqs", align_bytes=64)
@@ -66,10 +69,10 @@ def tile_lambmlpbackwardstep_t_kernel(tc, x_bytes, x_scale, a, dy, w2, w1, m, v,
         w1t = keep.tile([P, NJ * F], BF16, name="w1t")
         mt = keep.tile([P, NJ * F], BF16, name="mt")
         vt = keep.tile([P, NJ * F], BF16, name="vt")
-        sq = keep.tile([P, NJ * F], F32, name="sq")
-        mn = keep.tile([P, NJ * F], F32, name="mn")
+        diag = keep.tile([P, P], F32, name="diag")
         rsum = keep.tile([P, 8], F32, name="rsum")
         wall = keep.tile([P, 8], F32, name="wall")
+        wsum = keep.tile([P, 8], F32, name="wsum")
         winv = keep.tile([P, 8], F32, name="winv")
         winv2 = keep.tile([P, 8], F32, name="winv2")
         step = keep.tile([P, 8], F32, name="step")
@@ -79,7 +82,7 @@ def tile_lambmlpbackwardstep_t_kernel(tc, x_bytes, x_scale, a, dy, w2, w1, m, v,
         s_v = x_scale.rearrange("(g p t) o -> g p (t o)", p=P, t=4)
         x_v = x_bytes.rearrange("(g p t) d -> g p t d", p=P, t=4)
 
-        at, ac, ta, ge, odd, sb, dyt, tp, dyg, dyq, dyqs, dh, da, xs, x8, xp, xi, gbank = ({} for k in range(18))
+        at, ac, ta, ge, odd, sb, dyt, tp, dyg, dyq, dyqs, dh, da, xs, x8, xp, xr, xw, xi, gbank = ({} for k in range(20))
 
         def load_a(i):
             at[i] = pool.tile([P, 4, F], BF16, name=f"a{i}", tag="a", bufs=AHEAD + 1)
@@ -105,13 +108,13 @@ def tile_lambmlpbackwardstep_t_kernel(tc, x_bytes, x_scale, a, dy, w2, w1, m, v,
             nc.sync.dma_start(out=dst[:].rearrange("p (j f) -> p j f", f=F), in_=src.rearrange("(j p) f -> p j f", p=P))
 
         def clamp(i):
-            ac[i] = pool.tile([P, 4 * F], BF16, name=f"ac{i}", tag="ac", bufs=2)
+            ac[i] = pool.tile([P, 4 * F], BF16, name=f"ac{i}", tag="ac", bufs=3)
             nc.vector.tensor_scalar(
                 out=ac[i][:], in0=at[i][:].rearrange("p t f -> p (t f)"), scalar1=CLAMP, scalar2=-CLAMP, op0=MIN, op1=MAX
             )
 
-        def turn_a(i):
-            ta[i] = psum.tile([P, 4, P], F32, name=f"ta{i}", tag="aw", bufs=1)
+        def turn_a(i, tag):
+            ta[i] = psum.tile([P, 4, P], F32, name=f"ta{i}", tag=tag, bufs=1)
             words = ac[i][:].bitcast(F32)
             for k in range(4):
                 nc.tensor.transpose(ta[i][:, k, :], words[:, P * k : P * (k + 1)], ident[:])
@@ -152,11 +155,16 @@ def tile_lambmlpbackwardstep_t_kernel(tc, x_bytes, x_scale, a, dy, w2, w1, m, v,
 
         def w_trace():
             nc.vector.scalar_tensor_tensor(
-                out=sq[:, 0:P], in0=gram[:], scalar=0.25, in1=ident[:], op0=MULT, op1=MULT, accum_out=wall[:, 0:1]
+                out=diag[:], in0=gram[:], scalar=0.25, in1=ident[:], op0=MULT, op1=MULT, accum_out=wall[:, 0:1]
             )
 
-        def add_nodes(i, e, closed=True):
-            sb[i, e] = psum.tile([P, 4, P], F32, name=f"sb{i}_{e}", tag="dh", bufs=2)
+        def w_total():
+            tot = psum.tile([P, 8], F32, name="tot", tag="g2", bufs=1)
+            nc.tensor.matmul(tot[:, 0:1], lhsT=ones[:], rhs=wall[:, 0:1], start=True, stop=True)
+            return tot
+
+        def add_nodes(i, e, tag, closed=True):
+            sb[i, e] = psum.tile([P, 4, P], F32, name=f"sb{i}_{e}", tag=tag, bufs=1)
             for t in range(4):
                 for n in range(2):
                     nc.tensor.matmul(
@@ -165,20 +173,8 @@ def tile_lambmlpbackwardstep_t_kernel(tc, x_bytes, x_scale, a, dy, w2, w1, m, v,
                         rhs=ident[:],
                         start=(n == 0 if closed else (t, n) == (0, 0)),
                         stop=(n == 1 and closed),
-                        is_transpose=None if (e, t, n) == (0, 3, 1) else True,
+                        is_transpose=True,
                     )
-
-        def third_node(i):
-            nc.tensor.matmul(
-                sb[i, 1][:].rearrange("p t q -> p (t q)"),
-                lhsT=minus2[:],
-                rhs=odd[i][:].rearrange("p t q -> p (t q)"),
-                start=False,
-                stop=True,
-            )
-
-        def empty_sum(i):
-            nc.scalar.copy(out=slots(i, 1), in_=sb[i, 1][:].rearrange("p t q -> p q t"))
 
         def diff(i, e):
             nc.vector.scalar_tensor_tensor(
@@ -190,8 +186,8 @@ def tile_lambmlpbackwardstep_t_kernel(tc, x_bytes, x_scale, a, dy, w2, w1, m, v,
                 op1=ADD,
             )
 
-        def turn(i, t, tag="tp", bufs=2):
-            tp[i, t] = psum.tile([P, NC, 2, P], F32, name=f"tp{i}_{t}", tag=tag, bufs=bufs)
+        def turn(i, t, tag):
+            tp[i, t] = psum.tile([P, NC, 2, P], F32, name=f"tp{i}_{t}", tag=tag, bufs=1)
             words = dyt[i, t // 2][:, t % 2, :].bitcast(F32)
             for c in range(NC):
                 for u in range(2):
@@ -212,8 +208,8 @@ def tile_lambmlpbackwardstep_t_kernel(tc, x_bytes, x_scale, a, dy, w2, w1, m, v,
                 in_=dyg[i][:].rearrange("p t k -> p (t k)"),
             )
 
-        def mm1(i, h, tag="dh"):
-            dh[i, h] = psum.tile([P, 4, P], F32, name=f"dh{i}_{h}", tag=tag, bufs=2)
+        def mm1(i, h, tag):
+            dh[i, h] = psum.tile([P, 4, P], F32, name=f"dh{i}_{h}", tag=tag, bufs=1)
             for t in range(4):
                 for c in range(NC):
                     nc.tensor.matmul_mx(
@@ -246,33 +242,65 @@ def tile_lambmlpbackwardstep_t_kernel(tc, x_bytes, x_scale, a, dy, w2, w1, m, v,
         def q_da(i):
             nc.vector.quantize_mx(out=daq[:, i, :].bitcast(FP8X4), scales=daqs[:, i, :], in_=da[i][:])
 
-        def widen_pairs(i, t):
-            if t == 0:
-                xp[i] = pool.tile([P, 2, D, 2], BF16, name=f"xp{i}", tag="xp", bufs=2)
-            width = D - REST_SCALAR if i == NG - 1 else D
+        def widen_pairs(i, t, lo, hi):
+            if (i, t) not in xp:
+                if t == 0:
+                    xp[i] = pool.tile([P, 2, D, 2], BF16, name=f"xp{i}", tag="xp", bufs=2)
+                xp[i, t] = True
             nc.vector.tensor_scalar(
-                out=xp[i][:, t // 2, 0:width, t % 2],
-                in0=x8[i][:, t, 0:width].bitcast(FP8),
+                out=xp[i][:, t // 2, lo:hi, t % 2],
+                in0=x8[i][:, t, lo:hi].bitcast(FP8),
                 scalar1=xs[i][:, t : t + 1],
                 scalar2=None,
                 op0=MULT,
             )
 
-        def widen_rows(i):
-            rows = pool.tile([P, 4, REST_SCALAR], BF16, name="rows", tag="rows", bufs=1)
-            for t in range(4):
-                nc.scalar.activation(
-                    out=rows[:, t, :],
-                    in_=x8[i][:, t, D - REST_SCALAR : D].bitcast(FP8),
-                    func=ACT.Copy,
-                    scale=xs[i][:, t : t + 1],
-                )
-            return rows
+        def new_rows(i, lo, hi):
+            xr[i, lo] = pool.tile([P, 4, hi - lo], BF16, name=f"xr{i}_{lo}", tag="xr", bufs=3)
 
-        def join_rows(i, rows):
+        def row_vector(i, t, lo, hi):
+            nc.vector.tensor_scalar(
+                out=xr[i, lo][:, t, :],
+                in0=x8[i][:, t, lo:hi].bitcast(FP8),
+                scalar1=xs[i][:, t : t + 1],
+                scalar2=None,
+                op0=MULT,
+            )
+
+        def row_scalar(i, t, lo, hi):
+            nc.scalar.activation(
+                out=xr[i, lo][:, t, :], in_=x8[i][:, t, lo:hi].bitcast(FP8), func=ACT.Copy, scale=xs[i][:, t : t + 1]
+            )
+
+        def weave(i, base, lo, hi):
+            nc.gpsimd.tensor_scalar(
+                out=xi[i][:, 4 * lo : 4 * hi].rearrange("p (d t) -> p d t", t=4),
+                in0=xr[i, base][:, :, lo - base : hi - base].rearrange("p t d -> p d t"),
+                scalar1=1.0,
+                scalar2=0.0,
+                op0=MULT,
+                op1=ADD,
+            )
+
+        def lace(i, base, lo, hi, tag):
+            xw[i] = psum.tile([P, 4 * (hi - lo)], BF16, name=f"xw{i}", tag=tag, bufs=1)
+            for c in range(lo, hi, P):
+                e = min(c + P, hi)
+                nc.tensor.matmul(
+                    xw[i][:, 4 * (c - lo) : 4 * (e - lo)],
+                    lhsT=ident_h[:],
+                    rhs=xr[i, base][:, :, c - base : e - base].rearrange("p t d -> p d t"),
+                    start=True,
+                    stop=True,
+                )
+
+        def empty_lace(i, lo, hi):
+            nc.scalar.copy(out=xi[i][:, 4 * lo : 4 * hi], in_=xw[i][:])
+
+        def join_rows(i, lo, hi):
             nc.scalar.copy(
-                out=xi[i][:, 4 * (D - REST_SCALAR) : 4 * D].rearrange("p (d t) -> p d t", t=4),
-                in_=rows[:].rearrange("p t d -> p d t"),
+                out=xi[i][:, 4 * lo : 4 * hi].rearrange("p (d t) -> p d t", t=4),
+                in_=xr[i, lo][:].rearrange("p t d -> p d t"),
             )
 
         def new_xi(i):
@@ -303,8 +331,8 @@ def tile_lambmlpbackwardstep_t_kernel(tc, x_bytes, x_scale, a, dy, w2, w1, m, v,
                     stop=(i == NG - 1 and j % 2 == 1),
                 )
 
-        def turn_w2(h):
-            bank = psum.tile([P, NC, 2, P], F32, name=f"w2_{h}", tag="dh", bufs=2)
+        def turn_w2(h, tag):
+            bank = psum.tile([P, NC, 2, P], F32, name=f"w2_{h}", tag=tag, bufs=1)
             words = w2r[:, h, :].bitcast(F32)
             for c in range(NC):
                 for u in range(2):
@@ -331,234 +359,289 @@ def tile_lambmlpbackwardstep_t_kernel(tc, x_bytes, x_scale, a, dy, w2, w1, m, v,
         load_a(1)
         load_x(1)
         load_dy(1, 0)
-        load_rows(w1t, w1)
         load_dy(1, 1)
+        load_rows(w1t, w1)
         for k, n in enumerate(NODES):
             nc.vector.memset(offs[:, k : k + 1], n * GRID)
         nc.vector.memset(ones[:], 1.0)
         make_identity(nc, ident[:])
         make_identity(nc, ident_h[:])
-        nc.gpsimd.tensor_scalar(out=minus2[:], in0=ident[:], scalar1=-2.0, scalar2=0.0, op0=MULT, op1=ADD)
+        nc.gpsimd.tensor_scalar(out=minus_h[:], in0=ident[:], scalar1=-1.0, scalar2=0.0, op0=MULT, op1=ADD)
         clamp(0)
         load_a(2)
-        load_x(2)
         load_dy(2, 0)
+        load_x(2)
         load_dy(2, 1)
         gelu_plain(0, 0)
         gelu_plain(0, 1)
         for t in range(2):
-            widen_pairs(0, t)
-        turn(0, 0)
-        turn(0, 1)
-        turn(0, 2, "g0", 1)
-        turn(0, 3, "g1", 1)
-        w2_banks = [turn_w2(h) for h in range(2)]
+            widen_pairs(0, t, 0, D)
+        turn(0, 0, "g0")
+        turn(0, 1, "g1")
+        turn(0, 2, "a")
+        turn(0, 3, "b")
+        w2_banks = [turn_w2(h, "cx"[h]) for h in range(2)]
         gelu_plain(0, 2)
         for t in range(2, 4):
-            widen_pairs(0, t)
+            widen_pairs(0, t, 0, D)
         new_xi(0)
         nc.vector.tensor_tensor(out=ge[0, 0][:], in0=ge[0, 0][:], in1=ge[0, 1][:], op=ADD)
         empty(0, 0)
         empty(0, 1)
         clamp(1)
-        turn_a(1)
-        turn(1, 0)
-        turn(1, 1)
-        gram = psum.tile([P, P], F32, name="gram", tag="g2", bufs=1)
-        w_gram(0, GRAM_HEAD)
+        turn_a(1, "d")
         nc.vector.scalar_tensor_tensor(out=ge[0, 2][:], in0=ge[0, 2][:], scalar=-2.0, in1=ge[0, 0][:], op0=MULT, op1=ADD)
         empty(0, 2)
         empty(0, 3)
         empty_w2(0, w2_banks[0])
         empty_w2(1, w2_banks[1])
+        turn(1, 0, "g0")
+        turn(1, 1, "g1")
+        turn(1, 2, "b")
+        turn(1, 3, "c")
+        gram = psum.tile([P, P], F32, name="gram", tag="g2", bufs=1)
+        w_gram(0, GRAM_HEAD)
+        join_pairs(0, 0, JOIN_HEAD, nc.vector.tensor_copy)
         for t in range(2):
-            widen_pairs(1, t)
+            widen_pairs(1, t, ROWS, D)
         q_dy(0)
         q_w2()
-        join_pairs(0, 0, D, nc.scalar.copy)
+        join_pairs(0, JOIN_HEAD, D, nc.scalar.copy)
+        gelu_turned(1, 0)
+        gelu_turned(1, 1)
+        for t in range(4):
+            empty(1, t)
+        mm1(0, 0, "a")
+        w_gram(GRAM_HEAD, GRAM_STEP)
+        mm1(0, 1, "d")
+        for t in range(2, 4):
+            widen_pairs(1, t, ROWS, D)
+        q_x(0, 0, D)
+        clamp(2)
+        new_rows(1, 0, ROWS)
+        for t in range(2):
+            row_vector(1, t, 0, ROWS)
+        q_dy(1)
+        gelu_third(1, True)
+        for t in range(2, 4):
+            row_vector(1, t, 0, ROWS)
+        turn(2, 0, "x")
+        w_gram(GRAM_STEP, 2 * NJ)
+        add_nodes(1, 0, "b")
+        add_nodes(1, 1, "c")
 
         last = NG - 1
-        for s in range(1, NG):
+        for s in range(1, last):
+            late, held = ("d", "x") if s % 2 else ("x", "d")
+            end = D if s + 1 < last else D - REST
             if s + AHEAD < NG:
-                load_a(s + AHEAD)
-                load_x(s + AHEAD)
                 load_dy(s + AHEAD, 0)
                 load_dy(s + AHEAD, 1)
+                load_a(s + AHEAD)
+                load_x(s + AHEAD)
             if s + AHEAD == last:
                 load_rows(mt, m)
                 load_rows(vt, v)
-            if s == 1:
-                mm1(0, 0)
-            empty(s, 0)
-            turn(s, 2)
-            empty(s, 1)
-            turn(s, 3)
-            if s > 1:
-                mm1(s - 1, 0)
-                mm2(s - 2, 0)
-                mm2(s - 2, 1)
-            else:
-                mm1(0, 1)
-                w_gram(GRAM_HEAD, GRAM_STEP)
-            gelu_turned(s, 0)
-            gelu_turned(s, 1)
-            for t in range(2, 4):
-                widen_pairs(s, t)
-            if s < last:
-                clamp(s + 1)
-            if s > 1:
-                empty_sum(s - 1)
-                mm1(s - 1, 1)
-            q_x(s - 1, 0, D // 2)
             new_xi(s)
-            join_pairs(s, 0, JOIN_VECTOR, nc.vector.tensor_copy)
-            if s == 2:
-                w_trace()
+            weave(s, 0, LACED, ROWS)
             make_da(s - 1, 0)
-            q_x(s - 1, D // 2, D)
             make_da(s - 1, 1)
-            if s < last:
-                turn_a(s + 1)
-            empty(s, 2)
-            if s < last:
-                turn(s + 1, 0)
-            add_nodes(s, 0)
+            diff(s, 0)
+            diff(s, 1)
+            if s == 1:
+                w_trace()
+            empty(s + 1, 0)
+            turn_a(s + 1, held)
+            join_pairs(s, ROWS, D, nc.scalar.copy)
+            lace(s, 0, 0, LACED, "a")
+            if s == 1:
+                tot = w_total()
+            turn(s + 1, 1, late)
+            turn(s + 1, 2, "b")
             if s > 1:
                 mm2(s - 2, 2)
-            else:
-                w_gram(GRAM_STEP, 2 * NJ)
-            empty(s, 3)
-            if s < last:
-                turn(s + 1, 1)
-            add_nodes(s, 1, s == last)
-            q_dy(s)
+            turn(s + 1, 3, "c")
+            gelu_turned(s + 1, 0)
+            gelu_turned(s + 1, 1)
+            empty_lace(s, 0, LACED)
+            for t in range(1, 4):
+                empty(s + 1, t)
+            mm1(s, 1, held)
+            mm1(s, 0, "a")
+            if s + 2 < NG:
+                turn(s + 2, 0, late)
             q_da(s - 1)
-            gelu_third(s, s == last)
-            if s < last:
-                third_node(s)
-                for t in range(2):
-                    widen_pairs(s + 1, t)
-            else:
-                rows = widen_rows(s)
-            join_pairs(s, JOIN_VECTOR, D if s < last else D - REST_SCALAR, nc.scalar.copy)
-            diff(s, 0)
-        diff(last, 1)
-        join_rows(last, rows)
+            if s == 1:
+                nc.vector.tensor_copy(out=wsum[:, 0:1], in_=tot[:, 0:1])
+            if s + 2 < NG:
+                clamp(s + 2)
+            for t in range(4):
+                widen_pairs(s + 1, t, ROWS, end)
+            new_rows(s + 1, 0, ROWS)
+            if s + 1 == last:
+                row_vector(s + 1, 0, 0, ROWS)
+                row_vector(s + 1, 1, 0, ROWS)
+            q_x(s, 0, D)
+            if s + 1 < last:
+                row_vector(s + 1, 1, 0, ROWS)
+            q_dy(s + 1)
+            if s + 1 < last:
+                row_scalar(s + 1, 0, 0, ROWS)
+            gelu_third(s + 1, True)
+            for t in range(2, 4):
+                row_vector(s + 1, t, 0, ROWS)
+            add_nodes(s + 1, 0, "b")
+            add_nodes(s + 1, 1, "c")
+            mm2(s - 1, 0)
+            mm2(s - 1, 1)
 
-        mm1(last, 0, "tp")
-        mm1(last, 1, "tp")
-        tot = psum.tile([P, 8], F32, name="tot", tag="aw", bufs=1)
-        nc.tensor.matmul(tot[:, 0:1], lhsT=ones[:], rhs=wall[:, 0:1], start=True, stop=True)
-        nc.scalar.activation(out=winv[:, 0:1], in_=tot[:, 0:1], func=ACT.Abs_reciprocal_sqrt)
-        for b in range(LIVE):
-            mm2(last - 1, b)
-        gbank[LIVE] = psum.tile([P, BANK], F32, name="g3", tag="dh", bufs=2)
+        G3, SPARE = "x", ("c", "d", "a", "b")
+        gbank[LIVE] = psum.tile([P, BANK], F32, name="g3", tag=G3, bufs=1)
+        new_xi(last)
+        weave(last, 0, LACED, ROWS)
+        make_da(last - 1, 0)
+        make_da(last - 1, 1)
+        diff(last, 0)
+        diff(last, 1)
+        join_pairs(last, ROWS, D - REST, nc.scalar.copy)
+        new_rows(last, D - REST, D)
+        for t in range(4):
+            row_scalar(last, t, D - REST, D)
         for i in range(EARLY):
             mm2(i, LIVE)
+        lace(last, 0, 0, LACED, "a")
+        mm1(last, 0, "d")
+        mm1(last, 1, "b")
+        join_rows(last, D - REST, D)
+        empty_lace(last, 0, LACED)
+        nc.scalar.activation(out=winv[:, 0:1], in_=wsum[:, 0:1], func=ACT.Abs_reciprocal_sqrt)
+        nc.scalar.activation(out=winv2[:, 0:1], in_=winv[:, 0:1], func=ACT.Square)
+        q_da(last - 1)
+        mm2(last - 2, 2)
+        for i in range(EARLY, last - 1):
+            mm2(i, LIVE)
+        for b in range(NB):
+            mm2(last - 1, b)
         make_da(last, 0)
         make_da(last, 1)
         q_x(last, 0, D // 2)
         q_da(last)
-        q_x(last, D // 2, D)
-        for b in range(LIVE):
-            mm2(last, b)
-        for i in range(EARLY, NG):
-            mm2(i, LIVE)
+        q_x(last, D // 2, D - REST)
+        sq = pool.tile([P, NJ * F], F32, name="sq", tag="dyg", bufs=2, align_bytes=64)
+        mn = pool.tile([P, NJ * F], F32, name="mn", tag="dyg", bufs=2, align_bytes=64)
 
-        vn, rt = {}, {}
+        vn, mb, rb = {}, {}, {}
+        spare = SPARE
 
         def cols(b):
             return slice(BANK * b, BANK * (b + 1))
+
+        def block(b, k):
+            return slice(BANK * b + P * k, BANK * b + P * (k + 1))
 
         def square(b):
             nc.scalar.activation(out=sq[:, cols(b)], in_=gbank[b][:], func=ACT.Square, scale=NEW_SHARE**0.5 * G_SCALE)
 
         def first_moment(b):
             nc.vector.scalar_tensor_tensor(
-                out=mn[:, cols(b)], in0=gbank[b][:], scalar=NEW_SHARE * G_SCALE, in1=mt[:, cols(b)], op0=MULT, op1=ADD
+                out=mn[:, cols(b)], in0=gbank[b][:], scalar=-NEW_SHARE * G_SCALE, in1=mt[:, cols(b)], op0=MULT, op1=SUB
             )
 
-        def open_v(b, tag, bufs):
-            vn[b] = psum.tile([P, BANK], F32, name=f"vn{b}", tag=tag, bufs=bufs)
-            nc.tensor.matmul(vn[b][:], lhsT=ident_h[:], rhs=vt[:, cols(b)], start=True, stop=False)
-
-        def second_moment_tensor(b):
-            nc.tensor.matmul(vn[b][:], lhsT=ident[:], rhs=sq[:, cols(b)], start=False, stop=True)
-
-        def second_moment_vector(b):
-            nc.vector.tensor_tensor(out=sq[:, cols(b)], in0=sq[:, cols(b)], in1=vt[:, cols(b)], op=ADD)
-
-        def inv_root(b, src):
-            nc.scalar.activation(out=sq[:, cols(b)], in_=src, func=ACT.Abs_reciprocal_sqrt, scale=1.0 / 60.0)
-
-        def ratio(b):
-            nc.vector.tensor_tensor(out=mn[:, cols(b)], in0=mn[:, cols(b)], in1=sq[:, cols(b)], op=MULT)
-
-        def open_r(b):
-            rt[b] = psum.tile([P, 4, P], F32, name=f"rt{b}", tag=f"g{b}" if b < LIVE else "tp", bufs=1 if b < LIVE else 2)
+        def open_v(b):
+            vn[b] = psum.tile([P, 4, P], F32, name=f"vn{b}", tag=spare[b], bufs=1)
             for k in range(4):
-                col = BANK * b + P * k
-                nc.tensor.matmul(rt[b][:, k, :], lhsT=w1t[:, col : col + P], rhs=ident_h[:], start=(k == 0), stop=False)
+                nc.tensor.matmul(vn[b][:, k, :], lhsT=vt[:, block(b, k)], rhs=ident_h[:], start=(k == 0), stop=False)
 
-        def add_r(b):
+        def add_turned(bank, src, b):
             for k in range(4):
-                col = BANK * b + P * k
                 nc.tensor.matmul(
-                    rt[b][:, k, :], lhsT=mn[:, col : col + P], rhs=ident[:], start=False, stop=(k == 3), is_transpose=True
+                    bank[:, k, :], lhsT=src[:, block(b, k)], rhs=ident[:], start=False, stop=(k == 3), is_transpose=True
                 )
 
-        def r_norm(b, k):
+        def inv_root(b):
             nc.scalar.activation(
                 out=sq[:, cols(b)],
-                in_=rt[b][:].rearrange("p k q -> p (k q)"),
+                in_=vn[b][:].rearrange("p k q -> p (k q)"),
+                func=ACT.Abs_reciprocal_sqrt,
+                scale=1.0 / 60.0,
+            )
+
+        def turn_m(b):
+            mb[b] = psum.tile([P, 4, P], F32, name=f"mb{b}", tag=f"g{b}" if b < LIVE else G3, bufs=1)
+            for k in range(4):
+                nc.tensor.transpose(mb[b][:, k, :], mn[:, block(b, k)], ident[:])
+
+        def ratio(b):
+            nc.vector.tensor_tensor(
+                out=mn[:, cols(b)], in0=mb[b][:].rearrange("p k q -> p (k q)"), in1=sq[:, cols(b)], op=MULT
+            )
+
+        def open_r(b):
+            rb[b] = psum.tile([P, 4, P], F32, name=f"rb{b}", tag=spare[b], bufs=1)
+            nc.tensor.matmul(
+                rb[b][:].rearrange("p k q -> p (k q)"), lhsT=minus_h[:], rhs=w1t[:, cols(b)], start=True, stop=False
+            )
+
+        def r_norm(b):
+            nc.scalar.activation(
+                out=sq[:, cols(b)],
+                in_=rb[b][:].rearrange("p k q -> p (k q)"),
                 func=ACT.Square,
-                accum_out=rsum[:, k : k + 1],
+                accum_out=rsum[:, b : b + 1],
             )
 
-        def decay(b):
-            nc.vector.scalar_tensor_tensor(
-                out=mn[:, cols(b)], in0=mn[:, cols(b)], scalar=-1.0, in1=w1t[:, cols(b)], op0=MULT, op1=SUB
-            )
-
-        first_moment(0)
-        square(1)
-        open_v(1, "dh", 2)
-        open_v(0, "tp", 2)
-        second_moment_tensor(1)
-        first_moment(2)
+        open_v(0)
+        open_v(2)
+        for b in range(LIVE):
+            mm2(last, b)
+        q_x(last, D - REST, D)
         square(0)
-        second_moment_tensor(0)
-        square(2)
-        first_moment(3)
-        square(3)
         first_moment(1)
-        second_moment_vector(2)
-        inv_root(1, vn[1][:])
-        second_moment_vector(3)
-        order = (1, 2, 0, 3)
-        for b in order:
-            open_r(b)
-        rtot = psum.tile([P, 8], F32, name="rtot", tag="aw", bufs=1)
-        inv_root(2, sq[:, cols(2)])
-        ratio(1)
-        add_r(1)
-        inv_root(0, vn[0][:])
+        open_v(1)
+        mm2(last, LIVE)
+        add_turned(vn[0], sq, 0)
+        square(2)
+        first_moment(0)
+        open_v(3)
+        add_turned(vn[2], sq, 2)
+        square(1)
+        first_moment(3)
+        turn_m(0)
+        add_turned(vn[1], sq, 1)
+        inv_root(0)
+        first_moment(2)
+        square(3)
+        open_r(0)
+        turn_m(2)
+        add_turned(vn[3], sq, 3)
+        ratio(0)
+        inv_root(2)
+        turn_m(1)
+        turn_m(3)
+        add_turned(rb[0], mn, 0)
+        inv_root(1)
         ratio(2)
-        add_r(2)
-        inv_root(3, sq[:, cols(3)])
-        nc.scalar.activation(out=winv2[:, 0:1], in_=winv[:, 0:1], func=ACT.Square)
-        for b in order[2:]:
-            ratio(b)
-            add_r(b)
+        inv_root(3)
+        ratio(1)
+        ratio(3)
+        open_r(2)
+        open_r(1)
+        add_turned(rb[2], mn, 2)
+        add_turned(rb[1], mn, 1)
+        open_r(3)
+        add_turned(rb[3], mn, 3)
+        rtot = psum.tile([P, 8], F32, name="rtot", tag="g0", bufs=1)
+        order = (0, 2, 1, 3)
         for k, b in enumerate(order):
-            r_norm(b, k)
-            nc.tensor.matmul(rtot[:, 0:1], lhsT=ones[:], rhs=rsum[:, k : k + 1], start=(k == 0), stop=(k == NB - 1))
-            decay(b)
+            r_norm(b)
+        for k, b in enumerate(order):
+            nc.tensor.matmul(rtot[:, 0:1], lhsT=ones[:], rhs=rsum[:, b : b + 1], start=(k == 0), stop=(k == NB - 1))
         nc.scalar.activation(out=step[:, 0:1], in_=rtot[:, 0:1], func=ACT.Abs_reciprocal_sqrt, scale=winv2[:, 0:1])
         out_v = out.rearrange("(j p) f -> p j f", p=P)
         pieces = [(2 * b, 2 * b + 2) for b in order[:-1]] + [(NJ - 2, NJ - 1), (NJ - 1, NJ)]
         for lo, hi in pieces:
             c = slice(F * lo, F * hi)
-            res = pool.tile([P, (hi - lo) * F], F32, name=f"res{lo}", tag="res", bufs=len(pieces))
-            nc.vector.scalar_tensor_tensor(out=res[:], in0=mn[:, c], scalar=step[:, 0:1], in1=w1t[:, c], op0=MULT, op1=ADD)
+            src = rb[lo // 2][:].rearrange("p k q -> p (k q)")[:, F * (lo % 2) : F * (lo % 2 + hi - lo)]
+            res = pool.tile([P, (hi - lo) * F], F32, name=f"res{lo}", tag="dy", bufs=2 * (AHEAD + 1))
+            nc.vector.scalar_tensor_tensor(out=res[:], in0=src, scalar=step[:, 0:1], in1=w1t[:, c], op0=MULT, op1=ADD)
             nc.sync.dma_start(out=out_v[:, lo:hi, :], in_=res[:].rearrange("p (j f) -> p j f", f=F))

@@ -41,6 +41,7 @@ LACED = 192
 ROWS = WOVEN + LACED
 REST = 256
 JOIN_HEAD = 896
+HEAD_LACED = 384
 EARLY = 5
 GRAM_HEAD, GRAM_STEP = 8, 12
 
@@ -223,7 +224,7 @@ def tile_lambmlpbackwardstep_t_kernel(tc, x_bytes, x_scale, a, dy, w2, w1, m, v,
                     )
 
         def make_da(i, h):
-            if h == 0:
+            if i not in da:
                 da[i] = pool.tile([P, 4 * F], BF16, name=f"da{i}", tag="da", bufs=2, align_bytes=64)
             s = slice(BANK * h, BANK * (h + 1))
             if i == 0:
@@ -258,9 +259,10 @@ def tile_lambmlpbackwardstep_t_kernel(tc, x_bytes, x_scale, a, dy, w2, w1, m, v,
         def new_rows(i, lo, hi):
             xr[i, lo] = pool.tile([P, 4, hi - lo], BF16, name=f"xr{i}_{lo}", tag="xr", bufs=3)
 
-        def row_vector(i, t, lo, hi):
+        def row_vector(i, t, lo, hi, base=None):
+            base = lo if base is None else base
             nc.vector.tensor_scalar(
-                out=xr[i, lo][:, t, :],
+                out=xr[i, base][:, t, lo - base : hi - base],
                 in0=x8[i][:, t, lo:hi].bitcast(FP8),
                 scalar1=xs[i][:, t : t + 1],
                 scalar2=None,
@@ -283,19 +285,25 @@ def tile_lambmlpbackwardstep_t_kernel(tc, x_bytes, x_scale, a, dy, w2, w1, m, v,
             )
 
         def lace(i, base, lo, hi, tag):
-            xw[i] = psum.tile([P, 4 * (hi - lo)], BF16, name=f"xw{i}", tag=tag, bufs=1)
+            xw[i, lo] = psum.tile([P, 4 * (hi - lo)], BF16, name=f"xw{i}_{lo}", tag=tag, bufs=1)
             for c in range(lo, hi, P):
                 e = min(c + P, hi)
                 nc.tensor.matmul(
-                    xw[i][:, 4 * (c - lo) : 4 * (e - lo)],
+                    xw[i, lo][:, 4 * (c - lo) : 4 * (e - lo)],
                     lhsT=ident_h[:],
                     rhs=xr[i, base][:, :, c - base : e - base].rearrange("p t d -> p d t"),
                     start=True,
                     stop=True,
                 )
 
-        def empty_lace(i, lo, hi):
-            nc.scalar.copy(out=xi[i][:, 4 * lo : 4 * hi], in_=xw[i][:])
+        def empty_lace(i, lo, hi, copy=nc.scalar.copy):
+            copy(out=xi[i][:, 4 * lo : 4 * hi], in_=xw[i, lo][:])
+
+        def join_part(i, base, lo, hi):
+            nc.scalar.copy(
+                out=xi[i][:, 4 * lo : 4 * hi].rearrange("p (d t) -> p d t", t=4),
+                in_=xr[i, base][:, :, lo - base : hi - base].rearrange("p t d -> p d t"),
+            )
 
         def join_rows(i, lo, hi):
             nc.scalar.copy(
@@ -365,8 +373,8 @@ def tile_lambmlpbackwardstep_t_kernel(tc, x_bytes, x_scale, a, dy, w2, w1, m, v,
             nc.vector.memset(offs[:, k : k + 1], n * GRID)
         nc.vector.memset(ones[:], 1.0)
         make_identity(nc, ident[:])
-        make_identity(nc, ident_h[:])
-        nc.gpsimd.tensor_scalar(out=minus_h[:], in0=ident[:], scalar1=-1.0, scalar2=0.0, op0=MULT, op1=ADD)
+        nc.vector.tensor_copy(out=ident_h[:], in_=ident[:])
+        nc.vector.tensor_scalar(out=minus_h[:], in0=ident[:], scalar1=-1.0, scalar2=None, op0=MULT)
         clamp(0)
         load_a(2)
         load_dy(2, 0)
@@ -411,8 +419,8 @@ def tile_lambmlpbackwardstep_t_kernel(tc, x_bytes, x_scale, a, dy, w2, w1, m, v,
         gelu_turned(1, 1)
         for t in range(4):
             empty(1, t)
+        turn(2, 0, "x")
         mm1(0, 0, "a")
-        w_gram(GRAM_HEAD, GRAM_STEP)
         mm1(0, 1, "d")
         for t in range(2, 4):
             widen_pairs(1, t, ROWS, D)
@@ -425,10 +433,11 @@ def tile_lambmlpbackwardstep_t_kernel(tc, x_bytes, x_scale, a, dy, w2, w1, m, v,
         gelu_third(1, True)
         for t in range(2, 4):
             row_vector(1, t, 0, ROWS)
-        turn(2, 0, "x")
-        w_gram(GRAM_STEP, 2 * NJ)
+        empty(2, 0)
+        turn_a(2, "x")
         add_nodes(1, 0, "b")
         add_nodes(1, 1, "c")
+        w_gram(GRAM_HEAD, 2 * NJ)
 
         last = NG - 1
         for s in range(1, last):
@@ -450,12 +459,13 @@ def tile_lambmlpbackwardstep_t_kernel(tc, x_bytes, x_scale, a, dy, w2, w1, m, v,
             diff(s, 1)
             if s == 1:
                 w_trace()
-            empty(s + 1, 0)
-            turn_a(s + 1, held)
+            if s == 2:
+                nc.scalar.copy(out=wsum[:, 0:1], in_=tot[:, 0:1])
+            if s > 1:
+                empty(s + 1, 0)
+                turn_a(s + 1, held)
             join_pairs(s, ROWS, D, nc.scalar.copy)
             lace(s, 0, 0, LACED, "a")
-            if s == 1:
-                tot = w_total()
             turn(s + 1, 1, late)
             turn(s + 1, 2, "b")
             if s > 1:
@@ -468,11 +478,11 @@ def tile_lambmlpbackwardstep_t_kernel(tc, x_bytes, x_scale, a, dy, w2, w1, m, v,
                 empty(s + 1, t)
             mm1(s, 1, held)
             mm1(s, 0, "a")
+            if s == 1:
+                tot = w_total()
             if s + 2 < NG:
                 turn(s + 2, 0, late)
             q_da(s - 1)
-            if s == 1:
-                nc.vector.tensor_copy(out=wsum[:, 0:1], in_=tot[:, 0:1])
             if s + 2 < NG:
                 clamp(s + 2)
             for t in range(4):
@@ -495,7 +505,7 @@ def tile_lambmlpbackwardstep_t_kernel(tc, x_bytes, x_scale, a, dy, w2, w1, m, v,
             mm2(s - 1, 0)
             mm2(s - 1, 1)
 
-        G3, SPARE = "x", ("c", "d", "a", "b")
+        G3, SPARE = "x", ("b", "a", "c", "d")
         gbank[LIVE] = psum.tile([P, BANK], F32, name="g3", tag=G3, bufs=1)
         new_xi(last)
         weave(last, 0, LACED, ROWS)
@@ -509,13 +519,11 @@ def tile_lambmlpbackwardstep_t_kernel(tc, x_bytes, x_scale, a, dy, w2, w1, m, v,
             row_scalar(last, t, D - REST, D)
         for i in range(EARLY):
             mm2(i, LIVE)
-        lace(last, 0, 0, LACED, "a")
-        mm1(last, 0, "d")
-        mm1(last, 1, "b")
+        mm1(last, 0, "a")
+        mm1(last, 1, "d")
+        join_part(last, 0, 0, LACED)
         join_rows(last, D - REST, D)
-        empty_lace(last, 0, LACED)
         nc.scalar.activation(out=winv[:, 0:1], in_=wsum[:, 0:1], func=ACT.Abs_reciprocal_sqrt)
-        nc.scalar.activation(out=winv2[:, 0:1], in_=winv[:, 0:1], func=ACT.Square)
         q_da(last - 1)
         mm2(last - 2, 2)
         for i in range(EARLY, last - 1):
@@ -526,7 +534,7 @@ def tile_lambmlpbackwardstep_t_kernel(tc, x_bytes, x_scale, a, dy, w2, w1, m, v,
         make_da(last, 1)
         q_x(last, 0, D // 2)
         q_da(last)
-        q_x(last, D // 2, D - REST)
+        q_x(last, D // 2, D)
         sq = pool.tile([P, NJ * F], F32, name="sq", tag="dyg", bufs=2, align_bytes=64)
         mn = pool.tile([P, NJ * F], F32, name="mn", tag="dyg", bufs=2, align_bytes=64)
 
@@ -590,24 +598,41 @@ def tile_lambmlpbackwardstep_t_kernel(tc, x_bytes, x_scale, a, dy, w2, w1, m, v,
                 accum_out=rsum[:, b : b + 1],
             )
 
+        def add_v(b):
+            nc.vector.tensor_tensor(out=sq[:, cols(b)], in0=sq[:, cols(b)], in1=vt[:, cols(b)], op=ADD)
+
+        def inv_root_plain(b):
+            nc.scalar.activation(out=sq[:, cols(b)], in_=sq[:, cols(b)], func=ACT.Abs_reciprocal_sqrt, scale=1.0 / 60.0)
+
+        def ratio_plain(b):
+            nc.vector.tensor_tensor(out=mn[:, cols(b)], in0=mn[:, cols(b)], in1=sq[:, cols(b)], op=MULT)
+
+        def decay(b):
+            nc.vector.tensor_tensor(out=mn[:, cols(b)], in0=mn[:, cols(b)], in1=w1t[:, cols(b)], op=SUB)
+
+        def r_norm_plain(b):
+            nc.scalar.activation(out=sq[:, cols(b)], in_=mn[:, cols(b)], func=ACT.Square, accum_out=rsum[:, b : b + 1])
+
+        order = (0, 2, 1, 3)
         open_v(0)
         open_v(2)
-        for b in range(LIVE):
-            mm2(last, b)
-        q_x(last, D - REST, D)
+        mm2(last, 0)
+        mm2(last, 1)
+        mm2(last, 2)
+        mm2(last, 3)
+        open_v(1)
+        open_v(3)
         square(0)
         first_moment(1)
-        open_v(1)
-        mm2(last, LIVE)
         add_turned(vn[0], sq, 0)
         square(2)
-        first_moment(0)
-        open_v(3)
+        first_moment(3)
         add_turned(vn[2], sq, 2)
         square(1)
-        first_moment(3)
-        turn_m(0)
+        first_moment(0)
         add_turned(vn[1], sq, 1)
+        turn_m(0)
+        turn_m(1)
         inv_root(0)
         first_moment(2)
         square(3)
@@ -616,32 +641,38 @@ def tile_lambmlpbackwardstep_t_kernel(tc, x_bytes, x_scale, a, dy, w2, w1, m, v,
         add_turned(vn[3], sq, 3)
         ratio(0)
         inv_root(2)
-        turn_m(1)
         turn_m(3)
         add_turned(rb[0], mn, 0)
         inv_root(1)
+        open_r(2)
         ratio(2)
         inv_root(3)
-        ratio(1)
-        ratio(3)
-        open_r(2)
         open_r(1)
         add_turned(rb[2], mn, 2)
-        add_turned(rb[1], mn, 1)
+        nc.vector.tensor_tensor(out=winv2[:, 0:1], in0=winv[:, 0:1], in1=winv[:, 0:1], op=MULT)
+        ratio(1)
         open_r(3)
+        add_turned(rb[1], mn, 1)
+        ratio(3)
         add_turned(rb[3], mn, 3)
         rtot = psum.tile([P, 8], F32, name="rtot", tag="g0", bufs=1)
-        order = (0, 2, 1, 3)
-        for k, b in enumerate(order):
-            r_norm(b)
-        for k, b in enumerate(order):
-            nc.tensor.matmul(rtot[:, 0:1], lhsT=ones[:], rhs=rsum[:, b : b + 1], start=(k == 0), stop=(k == NB - 1))
+        r_norm(0)
+        r_norm(2)
+        r_norm(1)
+        r_norm(3)
+        nc.tensor.matmul(rtot[:, 0:1], lhsT=ones[:], rhs=rsum[:, order[0] : order[0] + 1], start=True, stop=False)
+        nc.tensor.matmul(rtot[:, 0:1], lhsT=ones[:], rhs=rsum[:, order[1] : order[1] + 1], start=False, stop=False)
+        nc.tensor.matmul(rtot[:, 0:1], lhsT=ones[:], rhs=rsum[:, order[2] : order[2] + 1], start=False, stop=False)
+        nc.tensor.matmul(rtot[:, 0:1], lhsT=ones[:], rhs=rsum[:, order[3] : order[3] + 1], start=False, stop=True)
         nc.scalar.activation(out=step[:, 0:1], in_=rtot[:, 0:1], func=ACT.Abs_reciprocal_sqrt, scale=winv2[:, 0:1])
         out_v = out.rearrange("(j p) f -> p j f", p=P)
-        pieces = [(2 * b, 2 * b + 2) for b in order[:-1]] + [(NJ - 2, NJ - 1), (NJ - 1, NJ)]
+        pieces = [(0, 1), (1, 2), (4, 6), (2, 4), (6, 7), (7, 8)]
         for lo, hi in pieces:
             c = slice(F * lo, F * hi)
-            src = rb[lo // 2][:].rearrange("p k q -> p (k q)")[:, F * (lo % 2) : F * (lo % 2 + hi - lo)]
+            if lo // 2 in rb:
+                src = rb[lo // 2][:].rearrange("p k q -> p (k q)")[:, F * (lo % 2) : F * (lo % 2 + hi - lo)]
+            else:
+                src = mn[:, c]
             res = pool.tile([P, (hi - lo) * F], F32, name=f"res{lo}", tag="dy", bufs=2 * (AHEAD + 1))
             nc.vector.scalar_tensor_tensor(out=res[:], in0=src, scalar=step[:, 0:1], in1=w1t[:, c], op0=MULT, op1=ADD)
             nc.sync.dma_start(out=out_v[:, lo:hi, :], in_=res[:].rearrange("p (j f) -> p j f", f=F))

@@ -36,13 +36,14 @@ CLAMP = 7.0
 G_SCALE = 1.0 / 64.0
 NEW_SHARE = 0.4 / 0.6
 
-WOVEN = 320
-LACED = 192
+WOVEN = 288
+LACED = 256
 ROWS = WOVEN + LACED
 REST = 256
 JOIN_HEAD = 896
 HEAD_LACED = 384
-EARLY = 5
+SPLIT = 128
+EARLY = 2
 GRAM_HEAD, GRAM_STEP = 8, 12
 
 
@@ -271,7 +272,7 @@ def tile_lambmlpbackwardstep_t_kernel(tc, x_bytes, x_scale, a, dy, w2, w1, m, v,
 
         def row_scalar(i, t, lo, hi):
             nc.scalar.activation(
-                out=xr[i, lo][:, t, :], in_=x8[i][:, t, lo:hi].bitcast(FP8), func=ACT.Copy, scale=xs[i][:, t : t + 1]
+                out=xr[i, lo][:, t, 0 : hi - lo], in_=x8[i][:, t, lo:hi].bitcast(FP8), func=ACT.Copy, scale=xs[i][:, t : t + 1]
             )
 
         def weave(i, base, lo, hi):
@@ -363,12 +364,14 @@ def tile_lambmlpbackwardstep_t_kernel(tc, x_bytes, x_scale, a, dy, w2, w1, m, v,
         load_x(0, 2)
         load_dy(0, 0)
         load_dy(0, 1)
-        nc.sync.dma_start(out=w2r[:], in_=w2.rearrange("(h p) d -> p h d", p=P))
         load_a(1)
+        nc.sync.dma_start(out=w2r[:], in_=w2.rearrange("(h p) d -> p h d", p=P))
         load_x(1)
         load_dy(1, 0)
         load_dy(1, 1)
+        load_a(2)
         load_rows(w1t, w1)
+        load_dy(2, 0)
         for k, n in enumerate(NODES):
             nc.vector.memset(offs[:, k : k + 1], n * GRID)
         nc.vector.memset(ones[:], 1.0)
@@ -376,8 +379,7 @@ def tile_lambmlpbackwardstep_t_kernel(tc, x_bytes, x_scale, a, dy, w2, w1, m, v,
         nc.vector.tensor_copy(out=ident_h[:], in_=ident[:])
         nc.vector.tensor_scalar(out=minus_h[:], in0=ident[:], scalar1=-1.0, scalar2=None, op0=MULT)
         clamp(0)
-        load_a(2)
-        load_dy(2, 0)
+        load_a(3)
         load_x(2)
         load_dy(2, 1)
         gelu_plain(0, 0)
@@ -388,66 +390,58 @@ def tile_lambmlpbackwardstep_t_kernel(tc, x_bytes, x_scale, a, dy, w2, w1, m, v,
         turn(0, 1, "g1")
         turn(0, 2, "a")
         turn(0, 3, "b")
-        w2_banks = [turn_w2(h, "cx"[h]) for h in range(2)]
         gelu_plain(0, 2)
         for t in range(2, 4):
             widen_pairs(0, t, 0, D)
         new_xi(0)
         nc.vector.tensor_tensor(out=ge[0, 0][:], in0=ge[0, 0][:], in1=ge[0, 1][:], op=ADD)
-        empty(0, 0)
-        empty(0, 1)
         clamp(1)
         turn_a(1, "d")
+        w2_banks = [turn_w2(h, "cx"[h]) for h in range(2)]
         nc.vector.scalar_tensor_tensor(out=ge[0, 2][:], in0=ge[0, 2][:], scalar=-2.0, in1=ge[0, 0][:], op0=MULT, op1=ADD)
-        empty(0, 2)
-        empty(0, 3)
+        for t in range(4):
+            empty(0, t)
+        gelu_turned(1, 0)
+        gelu_turned(1, 1)
         empty_w2(0, w2_banks[0])
         empty_w2(1, w2_banks[1])
         turn(1, 0, "g0")
         turn(1, 1, "g1")
         turn(1, 2, "b")
-        turn(1, 3, "c")
-        gram = psum.tile([P, P], F32, name="gram", tag="g2", bufs=1)
-        w_gram(0, GRAM_HEAD)
-        join_pairs(0, 0, JOIN_HEAD, nc.vector.tensor_copy)
-        for t in range(2):
-            widen_pairs(1, t, ROWS, D)
+        turn(1, 3, "g2")
+        join_pairs(0, 0, D, nc.vector.tensor_copy)
         q_dy(0)
+        for t in range(4):
+            widen_pairs(1, t, ROWS, D)
+        clamp(2)
         q_w2()
-        join_pairs(0, JOIN_HEAD, D, nc.scalar.copy)
-        gelu_turned(1, 0)
-        gelu_turned(1, 1)
         for t in range(4):
             empty(1, t)
-        turn(2, 0, "x")
+        turn_a(2, "x")
         mm1(0, 0, "a")
         mm1(0, 1, "d")
-        for t in range(2, 4):
-            widen_pairs(1, t, ROWS, D)
         q_x(0, 0, D)
-        clamp(2)
         new_rows(1, 0, ROWS)
-        for t in range(2):
-            row_vector(1, t, 0, ROWS)
+        row_vector(1, 1, 0, ROWS)
         q_dy(1)
+        row_scalar(1, 0, 0, ROWS)
         gelu_third(1, True)
         for t in range(2, 4):
             row_vector(1, t, 0, ROWS)
-        empty(2, 0)
-        turn_a(2, "x")
         add_nodes(1, 0, "b")
         add_nodes(1, 1, "c")
-        w_gram(GRAM_HEAD, 2 * NJ)
+        gram = psum.tile([P, P], F32, name="gram", tag="g2", bufs=1)
+        w_gram(0, GRAM_HEAD)
 
         last = NG - 1
         for s in range(1, last):
-            late, held = ("d", "x") if s % 2 else ("x", "d")
             end = D if s + 1 < last else D - REST
+            if s + AHEAD + 1 < NG:
+                load_a(s + AHEAD + 1)
             if s + AHEAD < NG:
                 load_dy(s + AHEAD, 0)
-                load_dy(s + AHEAD, 1)
-                load_a(s + AHEAD)
                 load_x(s + AHEAD)
+                load_dy(s + AHEAD, 1)
             if s + AHEAD == last:
                 load_rows(mt, m)
                 load_rows(vt, v)
@@ -457,43 +451,39 @@ def tile_lambmlpbackwardstep_t_kernel(tc, x_bytes, x_scale, a, dy, w2, w1, m, v,
             make_da(s - 1, 1)
             diff(s, 0)
             diff(s, 1)
-            if s == 1:
-                w_trace()
-            if s == 2:
-                nc.scalar.copy(out=wsum[:, 0:1], in_=tot[:, 0:1])
-            if s > 1:
-                empty(s + 1, 0)
-                turn_a(s + 1, held)
-            join_pairs(s, ROWS, D, nc.scalar.copy)
-            lace(s, 0, 0, LACED, "a")
-            turn(s + 1, 1, late)
-            turn(s + 1, 2, "b")
-            if s > 1:
-                mm2(s - 2, 2)
-            turn(s + 1, 3, "c")
             gelu_turned(s + 1, 0)
             gelu_turned(s + 1, 1)
-            empty_lace(s, 0, LACED)
-            for t in range(1, 4):
-                empty(s + 1, t)
-            mm1(s, 1, held)
-            mm1(s, 0, "a")
+            join_pairs(s, ROWS, D if s + 1 < last else D - 256, nc.scalar.copy)
+            if s == 2:
+                nc.scalar.copy(out=wsum[:, 0:1], in_=tot[:, 0:1])
+            lace(s, 0, 0, LACED, "a")
+            turn(s + 1, 0, "d")
+            turn(s + 1, 1, "b")
             if s == 1:
-                tot = w_total()
-            if s + 2 < NG:
-                turn(s + 2, 0, late)
+                w_gram(GRAM_HEAD, 2 * NJ)
+            turn(s + 1, 2, "c")
+            turn(s + 1, 3, "x")
+            empty_lace(s, 0, LACED)
+            for t in range(4):
+                empty(s + 1, t)
+            if s > 1:
+                mm2(s - 2, 2)
+            mm1(s, 0, "a")
+            mm1(s, 1, "d")
             q_da(s - 1)
+            if s + 1 == last:
+                join_pairs(s, D - 256, D, nc.vector.tensor_copy)
             if s + 2 < NG:
                 clamp(s + 2)
             for t in range(4):
                 widen_pairs(s + 1, t, ROWS, end)
+            if s == 1:
+                w_trace()
             new_rows(s + 1, 0, ROWS)
             if s + 1 == last:
                 row_vector(s + 1, 0, 0, ROWS)
-                row_vector(s + 1, 1, 0, ROWS)
             q_x(s, 0, D)
-            if s + 1 < last:
-                row_vector(s + 1, 1, 0, ROWS)
+            row_vector(s + 1, 1, 0, ROWS)
             q_dy(s + 1)
             if s + 1 < last:
                 row_scalar(s + 1, 0, 0, ROWS)
@@ -501,7 +491,11 @@ def tile_lambmlpbackwardstep_t_kernel(tc, x_bytes, x_scale, a, dy, w2, w1, m, v,
             for t in range(2, 4):
                 row_vector(s + 1, t, 0, ROWS)
             add_nodes(s + 1, 0, "b")
+            if s + 2 < NG:
+                turn_a(s + 2, "x")
             add_nodes(s + 1, 1, "c")
+            if s == 1:
+                tot = w_total()
             mm2(s - 1, 0)
             mm2(s - 1, 1)
 
@@ -614,52 +608,49 @@ def tile_lambmlpbackwardstep_t_kernel(tc, x_bytes, x_scale, a, dy, w2, w1, m, v,
             nc.scalar.activation(out=sq[:, cols(b)], in_=mn[:, cols(b)], func=ACT.Square, accum_out=rsum[:, b : b + 1])
 
         order = (0, 2, 1, 3)
-        open_v(0)
-        open_v(2)
         mm2(last, 0)
         mm2(last, 1)
         mm2(last, 2)
         mm2(last, 3)
-        open_v(1)
-        open_v(3)
+        open_v(0)
+        open_v(2)
         square(0)
         first_moment(1)
         add_turned(vn[0], sq, 0)
         square(2)
         first_moment(3)
         add_turned(vn[2], sq, 2)
+        open_v(1)
         square(1)
         first_moment(0)
-        add_turned(vn[1], sq, 1)
         turn_m(0)
-        turn_m(1)
+        add_turned(vn[1], sq, 1)
+        square(3)
         inv_root(0)
         first_moment(2)
-        square(3)
-        open_r(0)
         turn_m(2)
-        add_turned(vn[3], sq, 3)
-        ratio(0)
+        turn_m(1)
+        add_v(3)
+        open_r(0)
         inv_root(2)
-        turn_m(3)
-        add_turned(rb[0], mn, 0)
+        ratio(0)
         inv_root(1)
+        add_turned(rb[0], mn, 0)
         open_r(2)
+        inv_root_plain(3)
         ratio(2)
-        inv_root(3)
-        open_r(1)
-        add_turned(rb[2], mn, 2)
         nc.vector.tensor_tensor(out=winv2[:, 0:1], in0=winv[:, 0:1], in1=winv[:, 0:1], op=MULT)
         ratio(1)
-        open_r(3)
+        open_r(1)
+        add_turned(rb[2], mn, 2)
         add_turned(rb[1], mn, 1)
-        ratio(3)
-        add_turned(rb[3], mn, 3)
+        ratio_plain(3)
+        decay(3)
         rtot = psum.tile([P, 8], F32, name="rtot", tag="g0", bufs=1)
         r_norm(0)
         r_norm(2)
         r_norm(1)
-        r_norm(3)
+        r_norm_plain(3)
         nc.tensor.matmul(rtot[:, 0:1], lhsT=ones[:], rhs=rsum[:, order[0] : order[0] + 1], start=True, stop=False)
         nc.tensor.matmul(rtot[:, 0:1], lhsT=ones[:], rhs=rsum[:, order[1] : order[1] + 1], start=False, stop=False)
         nc.tensor.matmul(rtot[:, 0:1], lhsT=ones[:], rhs=rsum[:, order[2] : order[2] + 1], start=False, stop=False)

@@ -36,15 +36,11 @@ CLAMP = 7.0
 G_SCALE = 1.0 / 64.0
 NEW_SHARE = 0.4 / 0.6
 
-WOVEN = 288
+WOVEN = 352
 LACED = 256
 ROWS = WOVEN + LACED
-REST = 256
-JOIN_HEAD = 896
-HEAD_LACED = 384
-SPLIT = 128
-EARLY = 2
-GRAM_HEAD, GRAM_STEP = 8, 12
+REST = 384
+GRAM_HEAD = 8
 
 
 def tile_lambmlpbackwardstep_t_kernel(tc, x_bytes, x_scale, a, dy, w2, w1, m, v, out):
@@ -84,7 +80,7 @@ def tile_lambmlpbackwardstep_t_kernel(tc, x_bytes, x_scale, a, dy, w2, w1, m, v,
         s_v = x_scale.rearrange("(g p t) o -> g p (t o)", p=P, t=4)
         x_v = x_bytes.rearrange("(g p t) d -> g p t d", p=P, t=4)
 
-        at, ac, ta, ge, odd, sb, dyt, tp, dyg, dyq, dyqs, dh, da, xs, x8, xp, xr, xw, xi, gbank = ({} for k in range(20))
+        at, ac, ta, ge, sb, dyt, tp, dyg, dyq, dyqs, dh, da, xs, x8, xp, xr, xw, xi, gbank = ({} for k in range(19))
 
         def load_a(i):
             at[i] = pool.tile([P, 4, F], BF16, name=f"a{i}", tag="a", bufs=AHEAD + 1)
@@ -133,22 +129,14 @@ def tile_lambmlpbackwardstep_t_kernel(tc, x_bytes, x_scale, a, dy, w2, w1, m, v,
         def slots(i, e):
             return ge[i, 2][:].rearrange("p (q e t) -> p q e t", e=2, t=4)[:, :, e, :]
 
-        def gelu_third(i, whole):
+        def gelu_third(i):
             ge[i, 2] = pool.tile([P, 4 * F], F32, name=f"ge{i}_2", tag="ge2", bufs=2)
-            src = ac[i][:].rearrange("p (t q e) -> p t q e", t=4, e=2)
-            if whole:
-                nc.scalar.activation(
-                    out=ge[i, 2][:].rearrange("p (f t) -> p f t", t=4),
-                    in_=ac[i][:].rearrange("p (t f) -> p f t", t=4),
-                    func=ACT.Gelu,
-                    bias=offs[:, 2:3],
-                )
-            else:
-                odd[i] = pool.tile([P, 4, P], F32, name=f"odd{i}", tag="odd", bufs=1)
-                nc.scalar.activation(out=odd[i][:], in_=src[:, :, :, 1], func=ACT.Gelu, bias=offs[:, 2:3])
-                nc.scalar.activation(
-                    out=slots(i, 0), in_=src[:, :, :, 0].rearrange("p t q -> p q t"), func=ACT.Gelu, bias=offs[:, 2:3]
-                )
+            nc.scalar.activation(
+                out=ge[i, 2][:].rearrange("p (f t) -> p f t", t=4),
+                in_=ac[i][:].rearrange("p (t f) -> p f t", t=4),
+                func=ACT.Gelu,
+                bias=offs[:, 2:3],
+            )
 
         def w_gram(lo, hi):
             for k in range(lo, hi):
@@ -165,7 +153,7 @@ def tile_lambmlpbackwardstep_t_kernel(tc, x_bytes, x_scale, a, dy, w2, w1, m, v,
             nc.tensor.matmul(tot[:, 0:1], lhsT=ones[:], rhs=wall[:, 0:1], start=True, stop=True)
             return tot
 
-        def add_nodes(i, e, tag, closed=True):
+        def add_nodes(i, e, tag):
             sb[i, e] = psum.tile([P, 4, P], F32, name=f"sb{i}_{e}", tag=tag, bufs=1)
             for t in range(4):
                 for n in range(2):
@@ -173,8 +161,8 @@ def tile_lambmlpbackwardstep_t_kernel(tc, x_bytes, x_scale, a, dy, w2, w1, m, v,
                         sb[i, e][:, t, :],
                         lhsT=ge[i, n][:, t, e, :],
                         rhs=ident[:],
-                        start=(n == 0 if closed else (t, n) == (0, 0)),
-                        stop=(n == 1 and closed),
+                        start=(n == 0),
+                        stop=(n == 1),
                         is_transpose=True,
                     )
 
@@ -225,7 +213,7 @@ def tile_lambmlpbackwardstep_t_kernel(tc, x_bytes, x_scale, a, dy, w2, w1, m, v,
                     )
 
         def make_da(i, h):
-            if i not in da:
+            if h == 0:
                 da[i] = pool.tile([P, 4 * F], BF16, name=f"da{i}", tag="da", bufs=2, align_bytes=64)
             s = slice(BANK * h, BANK * (h + 1))
             if i == 0:
@@ -245,10 +233,8 @@ def tile_lambmlpbackwardstep_t_kernel(tc, x_bytes, x_scale, a, dy, w2, w1, m, v,
             nc.vector.quantize_mx(out=daq[:, i, :].bitcast(FP8X4), scales=daqs[:, i, :], in_=da[i][:])
 
         def widen_pairs(i, t, lo, hi):
-            if (i, t) not in xp:
-                if t == 0:
-                    xp[i] = pool.tile([P, 2, D, 2], BF16, name=f"xp{i}", tag="xp", bufs=2)
-                xp[i, t] = True
+            if t == 0:
+                xp[i] = pool.tile([P, 2, D, 2], BF16, name=f"xp{i}", tag="xp", bufs=2)
             nc.vector.tensor_scalar(
                 out=xp[i][:, t // 2, lo:hi, t % 2],
                 in0=x8[i][:, t, lo:hi].bitcast(FP8),
@@ -257,13 +243,12 @@ def tile_lambmlpbackwardstep_t_kernel(tc, x_bytes, x_scale, a, dy, w2, w1, m, v,
                 op0=MULT,
             )
 
-        def new_rows(i, lo, hi):
-            xr[i, lo] = pool.tile([P, 4, hi - lo], BF16, name=f"xr{i}_{lo}", tag="xr", bufs=3)
+        def new_rows(i):
+            xr[i] = pool.tile([P, 4, ROWS], BF16, name=f"xr{i}", tag="xr", bufs=3)
 
-        def row_vector(i, t, lo, hi, base=None):
-            base = lo if base is None else base
+        def row_vector(i, t, lo, hi):
             nc.vector.tensor_scalar(
-                out=xr[i, base][:, t, lo - base : hi - base],
+                out=xr[i][:, t, lo:hi],
                 in0=x8[i][:, t, lo:hi].bitcast(FP8),
                 scalar1=xs[i][:, t : t + 1],
                 scalar2=None,
@@ -272,45 +257,32 @@ def tile_lambmlpbackwardstep_t_kernel(tc, x_bytes, x_scale, a, dy, w2, w1, m, v,
 
         def row_scalar(i, t, lo, hi):
             nc.scalar.activation(
-                out=xr[i, lo][:, t, 0 : hi - lo], in_=x8[i][:, t, lo:hi].bitcast(FP8), func=ACT.Copy, scale=xs[i][:, t : t + 1]
+                out=xr[i][:, t, lo:hi], in_=x8[i][:, t, lo:hi].bitcast(FP8), func=ACT.Copy, scale=xs[i][:, t : t + 1]
             )
 
-        def weave(i, base, lo, hi):
+        def by_column(i, lo, hi):
+            return xr[i][:, :, lo:hi].rearrange("p t d -> p d t")
+
+        def words_of(i, lo, hi):
+            return xi[i][:, 4 * lo : 4 * hi].rearrange("p (d t) -> p d t", t=4)
+
+        def weave(i, lo, hi):
             nc.gpsimd.tensor_scalar(
-                out=xi[i][:, 4 * lo : 4 * hi].rearrange("p (d t) -> p d t", t=4),
-                in0=xr[i, base][:, :, lo - base : hi - base].rearrange("p t d -> p d t"),
-                scalar1=1.0,
-                scalar2=0.0,
-                op0=MULT,
-                op1=ADD,
+                out=words_of(i, lo, hi), in0=by_column(i, lo, hi), scalar1=1.0, scalar2=0.0, op0=MULT, op1=ADD
             )
 
-        def lace(i, base, lo, hi, tag):
-            xw[i, lo] = psum.tile([P, 4 * (hi - lo)], BF16, name=f"xw{i}_{lo}", tag=tag, bufs=1)
-            for c in range(lo, hi, P):
-                e = min(c + P, hi)
+        def lace(i, tag):
+            xw[i] = psum.tile([P, 4 * LACED], BF16, name=f"xw{i}", tag=tag, bufs=1)
+            for c in range(0, LACED, P):
                 nc.tensor.matmul(
-                    xw[i, lo][:, 4 * (c - lo) : 4 * (e - lo)],
-                    lhsT=ident_h[:],
-                    rhs=xr[i, base][:, :, c - base : e - base].rearrange("p t d -> p d t"),
-                    start=True,
-                    stop=True,
+                    xw[i][:, 4 * c : 4 * (c + P)], lhsT=ident_h[:], rhs=by_column(i, c, c + P), start=True, stop=True
                 )
 
-        def empty_lace(i, lo, hi, copy=nc.scalar.copy):
-            copy(out=xi[i][:, 4 * lo : 4 * hi], in_=xw[i, lo][:])
-
-        def join_part(i, base, lo, hi):
-            nc.scalar.copy(
-                out=xi[i][:, 4 * lo : 4 * hi].rearrange("p (d t) -> p d t", t=4),
-                in_=xr[i, base][:, :, lo - base : hi - base].rearrange("p t d -> p d t"),
-            )
+        def empty_lace(i):
+            nc.scalar.copy(out=xi[i][:, 0 : 4 * LACED], in_=xw[i][:])
 
         def join_rows(i, lo, hi):
-            nc.scalar.copy(
-                out=xi[i][:, 4 * lo : 4 * hi].rearrange("p (d t) -> p d t", t=4),
-                in_=xr[i, lo][:].rearrange("p t d -> p d t"),
-            )
+            nc.scalar.copy(out=words_of(i, lo, hi), in_=by_column(i, lo, hi))
 
         def new_xi(i):
             xi[i] = pool.tile([P, D * 4], BF16, name=f"xi{i}", tag="xi", bufs=2, align_bytes=64)
@@ -421,13 +393,12 @@ def tile_lambmlpbackwardstep_t_kernel(tc, x_bytes, x_scale, a, dy, w2, w1, m, v,
         mm1(0, 0, "a")
         mm1(0, 1, "d")
         q_x(0, 0, D)
-        new_rows(1, 0, ROWS)
-        row_vector(1, 1, 0, ROWS)
-        q_dy(1)
+        new_rows(1)
         row_scalar(1, 0, 0, ROWS)
-        gelu_third(1, True)
-        for t in range(2, 4):
+        gelu_third(1)
+        for t in range(1, 4):
             row_vector(1, t, 0, ROWS)
+        q_dy(1)
         add_nodes(1, 0, "b")
         add_nodes(1, 1, "c")
         gram = psum.tile([P, P], F32, name="gram", tag="g2", bufs=1)
@@ -435,7 +406,6 @@ def tile_lambmlpbackwardstep_t_kernel(tc, x_bytes, x_scale, a, dy, w2, w1, m, v,
 
         last = NG - 1
         for s in range(1, last):
-            end = D if s + 1 < last else D - REST
             if s + AHEAD + 1 < NG:
                 load_a(s + AHEAD + 1)
             if s + AHEAD < NG:
@@ -446,24 +416,25 @@ def tile_lambmlpbackwardstep_t_kernel(tc, x_bytes, x_scale, a, dy, w2, w1, m, v,
                 load_rows(mt, m)
                 load_rows(vt, v)
             new_xi(s)
-            weave(s, 0, LACED, ROWS)
+            weave(s, LACED, ROWS)
             make_da(s - 1, 0)
             make_da(s - 1, 1)
             diff(s, 0)
             diff(s, 1)
             gelu_turned(s + 1, 0)
             gelu_turned(s + 1, 1)
-            join_pairs(s, ROWS, D if s + 1 < last else D - 256, nc.scalar.copy)
+            if s + 1 < last:
+                join_pairs(s, ROWS, D, nc.scalar.copy)
             if s == 2:
                 nc.scalar.copy(out=wsum[:, 0:1], in_=tot[:, 0:1])
-            lace(s, 0, 0, LACED, "a")
+            lace(s, "a")
             turn(s + 1, 0, "d")
             turn(s + 1, 1, "b")
             if s == 1:
                 w_gram(GRAM_HEAD, 2 * NJ)
             turn(s + 1, 2, "c")
             turn(s + 1, 3, "x")
-            empty_lace(s, 0, LACED)
+            empty_lace(s)
             for t in range(4):
                 empty(s + 1, t)
             if s > 1:
@@ -471,25 +442,28 @@ def tile_lambmlpbackwardstep_t_kernel(tc, x_bytes, x_scale, a, dy, w2, w1, m, v,
             mm1(s, 0, "a")
             mm1(s, 1, "d")
             q_da(s - 1)
-            if s + 1 == last:
-                join_pairs(s, D - 256, D, nc.vector.tensor_copy)
-            if s + 2 < NG:
-                clamp(s + 2)
-            for t in range(4):
-                widen_pairs(s + 1, t, ROWS, end)
-            if s == 1:
-                w_trace()
-            new_rows(s + 1, 0, ROWS)
-            if s + 1 == last:
-                row_vector(s + 1, 0, 0, ROWS)
-            q_x(s, 0, D)
-            row_vector(s + 1, 1, 0, ROWS)
-            q_dy(s + 1)
             if s + 1 < last:
+                clamp(s + 2)
+                for t in range(4):
+                    widen_pairs(s + 1, t, ROWS, D)
+                if s == 1:
+                    w_trace()
+                new_rows(s + 1)
+                q_x(s, 0, D)
                 row_scalar(s + 1, 0, 0, ROWS)
-            gelu_third(s + 1, True)
-            for t in range(2, 4):
-                row_vector(s + 1, t, 0, ROWS)
+                gelu_third(s + 1)
+                for t in range(1, 4):
+                    row_vector(s + 1, t, 0, ROWS)
+            else:
+                join_pairs(s, ROWS, D, nc.vector.tensor_copy)
+                xr[last] = pool.tile([P, 4, D], BF16, name="xr_last", tag="xp", bufs=2)
+                row_vector(last, 3, 0, D)
+                q_x(s, 0, D)
+                row_scalar(last, 0, 0, D - REST)
+                gelu_third(last)
+                for t in range(1, 3):
+                    row_vector(last, t, 0, D - REST)
+            q_dy(s + 1)
             add_nodes(s + 1, 0, "b")
             if s + 2 < NG:
                 turn_a(s + 2, "x")
@@ -499,41 +473,34 @@ def tile_lambmlpbackwardstep_t_kernel(tc, x_bytes, x_scale, a, dy, w2, w1, m, v,
             mm2(s - 1, 0)
             mm2(s - 1, 1)
 
-        G3, SPARE = "x", ("b", "a", "c", "d")
-        gbank[LIVE] = psum.tile([P, BANK], F32, name="g3", tag=G3, bufs=1)
+        gbank[LIVE] = psum.tile([P, BANK], F32, name="g3", tag="x", bufs=1)
         new_xi(last)
-        weave(last, 0, LACED, ROWS)
+        weave(last, 0, D - REST)
         make_da(last - 1, 0)
-        make_da(last - 1, 1)
         diff(last, 0)
         diff(last, 1)
-        join_pairs(last, ROWS, D - REST, nc.scalar.copy)
-        new_rows(last, D - REST, D)
-        for t in range(4):
+        make_da(last - 1, 1)
+        for t in range(3):
             row_scalar(last, t, D - REST, D)
-        for i in range(EARLY):
-            mm2(i, LIVE)
         mm1(last, 0, "a")
-        mm1(last, 1, "d")
-        join_part(last, 0, 0, LACED)
+        mm1(last, 1, "b")
         join_rows(last, D - REST, D)
         nc.scalar.activation(out=winv[:, 0:1], in_=wsum[:, 0:1], func=ACT.Abs_reciprocal_sqrt)
-        q_da(last - 1)
-        mm2(last - 2, 2)
-        for i in range(EARLY, last - 1):
-            mm2(i, LIVE)
-        for b in range(NB):
-            mm2(last - 1, b)
         make_da(last, 0)
         make_da(last, 1)
-        q_x(last, 0, D // 2)
+        mm2(last - 2, 2)
+        for i in range(last - 1):
+            mm2(i, LIVE)
+        q_da(last - 1)
+        q_x(last, 0, F)
         q_da(last)
-        q_x(last, D // 2, D)
+        q_x(last, F, 2 * F)
+        q_x(last, 2 * F, D)
         sq = pool.tile([P, NJ * F], F32, name="sq", tag="dyg", bufs=2, align_bytes=64)
         mn = pool.tile([P, NJ * F], F32, name="mn", tag="dyg", bufs=2, align_bytes=64)
 
         vn, mb, rb = {}, {}, {}
-        spare = SPARE
+        spare = {1: "a", 2: "c", 3: "b"}
 
         def cols(b):
             return slice(BANK * b, BANK * (b + 1))
@@ -569,7 +536,7 @@ def tile_lambmlpbackwardstep_t_kernel(tc, x_bytes, x_scale, a, dy, w2, w1, m, v,
             )
 
         def turn_m(b):
-            mb[b] = psum.tile([P, 4, P], F32, name=f"mb{b}", tag=f"g{b}" if b < LIVE else G3, bufs=1)
+            mb[b] = psum.tile([P, 4, P], F32, name=f"mb{b}", tag=f"g{b}" if b < LIVE else "x", bufs=1)
             for k in range(4):
                 nc.tensor.transpose(mb[b][:, k, :], mn[:, block(b, k)], ident[:])
 
@@ -604,57 +571,57 @@ def tile_lambmlpbackwardstep_t_kernel(tc, x_bytes, x_scale, a, dy, w2, w1, m, v,
         def decay(b):
             nc.vector.tensor_tensor(out=mn[:, cols(b)], in0=mn[:, cols(b)], in1=w1t[:, cols(b)], op=SUB)
 
-        def r_norm_plain(b):
-            nc.scalar.activation(out=sq[:, cols(b)], in_=mn[:, cols(b)], func=ACT.Square, accum_out=rsum[:, b : b + 1])
+        def r_norm_vector(b):
+            nc.vector.scalar_tensor_tensor(
+                out=sq[:, cols(b)],
+                in0=mn[:, cols(b)],
+                scalar=1.0,
+                in1=mn[:, cols(b)],
+                op0=MULT,
+                op1=MULT,
+                accum_out=rsum[:, b : b + 1],
+            )
 
-        order = (0, 2, 1, 3)
-        mm2(last, 0)
-        mm2(last, 1)
-        mm2(last, 2)
-        mm2(last, 3)
-        open_v(0)
-        open_v(2)
+        for b in range(NB):
+            mm2(last - 1, b)
+            mm2(last, b)
         square(0)
         first_moment(1)
-        add_turned(vn[0], sq, 0)
+        add_v(0)
         square(2)
-        first_moment(3)
-        add_turned(vn[2], sq, 2)
-        open_v(1)
-        square(1)
         first_moment(0)
-        turn_m(0)
-        add_turned(vn[1], sq, 1)
-        square(3)
-        inv_root(0)
+        square(1)
         first_moment(2)
-        turn_m(2)
-        turn_m(1)
-        add_v(3)
-        open_r(0)
-        inv_root(2)
-        ratio(0)
-        inv_root(1)
-        add_turned(rb[0], mn, 0)
-        open_r(2)
-        inv_root_plain(3)
-        ratio(2)
+        square(3)
         nc.vector.tensor_tensor(out=winv2[:, 0:1], in0=winv[:, 0:1], in1=winv[:, 0:1], op=MULT)
+        first_moment(3)
+        for b in (2, 1):
+            open_v(b)
+            add_turned(vn[b], sq, b)
+        open_v(3)
+        turn_m(2)
+        add_turned(vn[3], sq, 3)
+        turn_m(1)
+        turn_m(3)
+        inv_root_plain(0)
+        inv_root(2)
+        inv_root(1)
+        inv_root(3)
+        ratio_plain(0)
+        ratio(2)
         ratio(1)
-        open_r(1)
-        add_turned(rb[2], mn, 2)
-        add_turned(rb[1], mn, 1)
-        ratio_plain(3)
-        decay(3)
+        ratio(3)
+        decay(0)
+        for b in (2, 1, 3):
+            open_r(b)
+            add_turned(rb[b], mn, b)
         rtot = psum.tile([P, 8], F32, name="rtot", tag="g0", bufs=1)
-        r_norm(0)
         r_norm(2)
         r_norm(1)
-        r_norm_plain(3)
-        nc.tensor.matmul(rtot[:, 0:1], lhsT=ones[:], rhs=rsum[:, order[0] : order[0] + 1], start=True, stop=False)
-        nc.tensor.matmul(rtot[:, 0:1], lhsT=ones[:], rhs=rsum[:, order[1] : order[1] + 1], start=False, stop=False)
-        nc.tensor.matmul(rtot[:, 0:1], lhsT=ones[:], rhs=rsum[:, order[2] : order[2] + 1], start=False, stop=False)
-        nc.tensor.matmul(rtot[:, 0:1], lhsT=ones[:], rhs=rsum[:, order[3] : order[3] + 1], start=False, stop=True)
+        r_norm_vector(0)
+        r_norm(3)
+        for k, b in enumerate((2, 1, 0, 3)):
+            nc.tensor.matmul(rtot[:, 0:1], lhsT=ones[:], rhs=rsum[:, b : b + 1], start=(k == 0), stop=(k == NB - 1))
         nc.scalar.activation(out=step[:, 0:1], in_=rtot[:, 0:1], func=ACT.Abs_reciprocal_sqrt, scale=winv2[:, 0:1])
         out_v = out.rearrange("(j p) f -> p j f", p=P)
         pieces = [(0, 1), (1, 2), (4, 6), (2, 4), (6, 7), (7, 8)]

@@ -36,7 +36,7 @@ CLAMP = 7.0
 G_SCALE = 1.0 / 64.0
 NEW_SHARE = 0.4 / 0.6
 
-WOVEN = 352
+WOVEN = 384
 LACED = 256
 ROWS = WOVEN + LACED
 REST = 384
@@ -122,21 +122,17 @@ def tile_lambmlpbackwardstep_t_kernel(tc, x_bytes, x_scale, a, dy, w2, w1, m, v,
             src = ta[i][:].rearrange("q k p -> q (k p)").bitcast(BF16).rearrange("q (k p e) -> q k e p", k=4, e=2)
             nc.scalar.activation(out=ge[i, n][:], in_=src, func=ACT.Gelu, bias=offs[:, n : n + 1])
 
-        def gelu_plain(i, n):
+        def gelu_slots(i, n):
             ge[i, n] = pool.tile([P, 4 * F], F32, name=f"ge{i}_{n}", tag=f"ge{n}", bufs=2)
-            nc.scalar.activation(out=ge[i, n][:], in_=ac[i][:], func=ACT.Gelu, bias=offs[:, n : n + 1])
+            nc.scalar.activation(
+                out=ge[i, n][:].rearrange("p (f t) -> p f t", t=4),
+                in_=ac[i][:].rearrange("p (t f) -> p f t", t=4),
+                func=ACT.Gelu,
+                bias=offs[:, n : n + 1],
+            )
 
         def slots(i, e):
             return ge[i, 2][:].rearrange("p (q e t) -> p q e t", e=2, t=4)[:, :, e, :]
-
-        def gelu_third(i):
-            ge[i, 2] = pool.tile([P, 4 * F], F32, name=f"ge{i}_2", tag="ge2", bufs=2)
-            nc.scalar.activation(
-                out=ge[i, 2][:].rearrange("p (f t) -> p f t", t=4),
-                in_=ac[i][:].rearrange("p (t f) -> p f t", t=4),
-                func=ACT.Gelu,
-                bias=offs[:, 2:3],
-            )
 
         def w_gram(lo, hi):
             for k in range(lo, hi):
@@ -216,10 +212,7 @@ def tile_lambmlpbackwardstep_t_kernel(tc, x_bytes, x_scale, a, dy, w2, w1, m, v,
             if h == 0:
                 da[i] = pool.tile([P, 4 * F], BF16, name=f"da{i}", tag="da", bufs=2, align_bytes=64)
             s = slice(BANK * h, BANK * (h + 1))
-            if i == 0:
-                slope = ge[i, 2][:].rearrange("p (t f) -> p f t", t=4)[:, P * h : P * (h + 1), :]
-            else:
-                slope = ge[i, 2][:, s].rearrange("p (f t) -> p f t", t=4)
+            slope = ge[i, 2][:, s].rearrange("p (f t) -> p f t", t=4)
             nc.vector.scalar_tensor_tensor(
                 out=da[i][:, s].rearrange("p (f t) -> p f t", t=4),
                 in0=slope,
@@ -348,21 +341,21 @@ def tile_lambmlpbackwardstep_t_kernel(tc, x_bytes, x_scale, a, dy, w2, w1, m, v,
             nc.vector.memset(offs[:, k : k + 1], n * GRID)
         nc.vector.memset(ones[:], 1.0)
         make_identity(nc, ident[:])
+        clamp(0)
         nc.vector.tensor_copy(out=ident_h[:], in_=ident[:])
         nc.vector.tensor_scalar(out=minus_h[:], in0=ident[:], scalar1=-1.0, scalar2=None, op0=MULT)
-        clamp(0)
         load_a(3)
         load_x(2)
         load_dy(2, 1)
-        gelu_plain(0, 0)
-        gelu_plain(0, 1)
+        gelu_slots(0, 0)
+        gelu_slots(0, 1)
         for t in range(2):
             widen_pairs(0, t, 0, D)
         turn(0, 0, "g0")
         turn(0, 1, "g1")
         turn(0, 2, "a")
         turn(0, 3, "b")
-        gelu_plain(0, 2)
+        gelu_slots(0, 2)
         for t in range(2, 4):
             widen_pairs(0, t, 0, D)
         new_xi(0)
@@ -385,17 +378,17 @@ def tile_lambmlpbackwardstep_t_kernel(tc, x_bytes, x_scale, a, dy, w2, w1, m, v,
         q_dy(0)
         for t in range(4):
             widen_pairs(1, t, ROWS, D)
-        clamp(2)
         q_w2()
+        clamp(2)
         for t in range(4):
             empty(1, t)
-        turn_a(2, "x")
         mm1(0, 0, "a")
         mm1(0, 1, "d")
+        turn_a(2, "x")
         q_x(0, 0, D)
         new_rows(1)
         row_scalar(1, 0, 0, ROWS)
-        gelu_third(1)
+        gelu_slots(1, 2)
         for t in range(1, 4):
             row_vector(1, t, 0, ROWS)
         q_dy(1)
@@ -451,7 +444,7 @@ def tile_lambmlpbackwardstep_t_kernel(tc, x_bytes, x_scale, a, dy, w2, w1, m, v,
                 new_rows(s + 1)
                 q_x(s, 0, D)
                 row_scalar(s + 1, 0, 0, ROWS)
-                gelu_third(s + 1)
+                gelu_slots(s + 1, 2)
                 for t in range(1, 4):
                     row_vector(s + 1, t, 0, ROWS)
             else:
@@ -460,7 +453,7 @@ def tile_lambmlpbackwardstep_t_kernel(tc, x_bytes, x_scale, a, dy, w2, w1, m, v,
                 row_vector(last, 3, 0, D)
                 q_x(s, 0, D)
                 row_scalar(last, 0, 0, D - REST)
-                gelu_third(last)
+                gelu_slots(last, 2)
                 for t in range(1, 3):
                     row_vector(last, t, 0, D - REST)
             q_dy(s + 1)
@@ -560,7 +553,7 @@ def tile_lambmlpbackwardstep_t_kernel(tc, x_bytes, x_scale, a, dy, w2, w1, m, v,
             )
 
         def add_v(b):
-            nc.vector.tensor_tensor(out=sq[:, cols(b)], in0=sq[:, cols(b)], in1=vt[:, cols(b)], op=ADD)
+            nc.gpsimd.tensor_tensor(out=sq[:, cols(b)], in0=sq[:, cols(b)], in1=vt[:, cols(b)], op=ADD)
 
         def inv_root_plain(b):
             nc.scalar.activation(out=sq[:, cols(b)], in_=sq[:, cols(b)], func=ACT.Abs_reciprocal_sqrt, scale=1.0 / 60.0)
@@ -585,42 +578,39 @@ def tile_lambmlpbackwardstep_t_kernel(tc, x_bytes, x_scale, a, dy, w2, w1, m, v,
         for b in range(NB):
             mm2(last - 1, b)
             mm2(last, b)
-        square(0)
-        first_moment(1)
-        add_v(0)
-        square(2)
-        first_moment(0)
-        square(1)
-        first_moment(2)
-        square(3)
-        nc.vector.tensor_tensor(out=winv2[:, 0:1], in0=winv[:, 0:1], in1=winv[:, 0:1], op=MULT)
-        first_moment(3)
-        for b in (2, 1):
-            open_v(b)
-            add_turned(vn[b], sq, b)
-        open_v(3)
-        turn_m(2)
-        add_turned(vn[3], sq, 3)
+        for b in range(NB):
+            square(b)
+            if b == 0:
+                add_v(b)
+            first_moment(b)
+        open_v(1)
+        add_turned(vn[1], sq, 1)
+        open_v(2)
+        add_turned(vn[2], sq, 2)
         turn_m(1)
+        open_v(3)
+        add_turned(vn[3], sq, 3)
+        turn_m(2)
         turn_m(3)
+        inv_root(1)
         inv_root_plain(0)
         inv_root(2)
-        inv_root(1)
         inv_root(3)
+        ratio(1)
         ratio_plain(0)
         ratio(2)
-        ratio(1)
         ratio(3)
         decay(0)
-        for b in (2, 1, 3):
+        nc.vector.tensor_tensor(out=winv2[:, 0:1], in0=winv[:, 0:1], in1=winv[:, 0:1], op=MULT)
+        for b in (1, 2, 3):
             open_r(b)
             add_turned(rb[b], mn, b)
         rtot = psum.tile([P, 8], F32, name="rtot", tag="g0", bufs=1)
-        r_norm(2)
         r_norm(1)
+        r_norm(2)
         r_norm_vector(0)
         r_norm(3)
-        for k, b in enumerate((2, 1, 0, 3)):
+        for k, b in enumerate((1, 2, 0, 3)):
             nc.tensor.matmul(rtot[:, 0:1], lhsT=ones[:], rhs=rsum[:, b : b + 1], start=(k == 0), stop=(k == NB - 1))
         nc.scalar.activation(out=step[:, 0:1], in_=rtot[:, 0:1], func=ACT.Abs_reciprocal_sqrt, scale=winv2[:, 0:1])
         out_v = out.rearrange("(j p) f -> p j f", p=P)

@@ -40,6 +40,8 @@ WOVEN = 384
 LACED = 256
 ROWS = WOVEN + LACED
 REST = 384
+LACED_0 = 128
+GATE = 128
 GRAM_HEAD = 8
 
 
@@ -94,13 +96,14 @@ def tile_lambmlpbackwardstep_t_kernel(tc, x_bytes, x_scale, a, dy, w2, w1, m, v,
             xs[i] = keep.tile([P, 4], F32, name=f"xs{i}")
             queue.dma_start(out=xs[i][:], in_=s_v[i])
 
-        def load_x(i, pieces=1):
-            if i > 0:
-                load_scale(i, nc.sync)
-            x8[i] = pool.tile([P, 4, D], U8, name=f"x8_{i}", tag="x8", bufs=AHEAD + 1)
-            n = 4 // pieces
-            for t in range(0, 4, n):
-                nc.sync.dma_start(out=x8[i][:, t : t + n, :], in_=x_v[i][:, t : t + n, :])
+        def load_slots(i, lo, hi):
+            if lo == 0:
+                x8[i] = pool.tile([P, 4, D], U8, name=f"x8_{i}", tag="x8", bufs=AHEAD + 1)
+            nc.sync.dma_start(out=x8[i][:, lo:hi, :], in_=x_v[i][:, lo:hi, :])
+
+        def load_x(i):
+            load_scale(i, nc.sync)
+            load_slots(i, 0, 4)
 
         def load_rows(dst, src):
             nc.sync.dma_start(out=dst[:].rearrange("p (j f) -> p j f", f=F), in_=src.rearrange("(j p) f -> p j f", p=P))
@@ -264,21 +267,21 @@ def tile_lambmlpbackwardstep_t_kernel(tc, x_bytes, x_scale, a, dy, w2, w1, m, v,
                 out=words_of(i, lo, hi), in0=by_column(i, lo, hi), scalar1=1.0, scalar2=0.0, op0=MULT, op1=ADD
             )
 
-        def lace(i, tag):
-            xw[i] = psum.tile([P, 4 * LACED], BF16, name=f"xw{i}", tag=tag, bufs=1)
-            for c in range(0, LACED, P):
-                nc.tensor.matmul(
-                    xw[i][:, 4 * c : 4 * (c + P)], lhsT=ident_h[:], rhs=by_column(i, c, c + P), start=True, stop=True
-                )
+        def lace(i, c, tag):
+            if c == 0:
+                xw[i] = psum.tile([P, 4 * LACED], BF16, name=f"xw{i}", tag=tag, bufs=1)
+            nc.tensor.matmul(
+                xw[i][:, 4 * c : 4 * (c + P)], lhsT=ident_h[:], rhs=by_column(i, c, c + P), start=True, stop=True
+            )
 
-        def empty_lace(i):
-            nc.scalar.copy(out=xi[i][:, 0 : 4 * LACED], in_=xw[i][:])
+        def empty_lace(i, width=LACED):
+            nc.scalar.copy(out=xi[i][:, 0 : 4 * width], in_=xw[i][:, 0 : 4 * width])
 
         def join_rows(i, lo, hi):
             nc.scalar.copy(out=words_of(i, lo, hi), in_=by_column(i, lo, hi))
 
         def new_xi(i):
-            xi[i] = pool.tile([P, D * 4], BF16, name=f"xi{i}", tag="xi", bufs=2, align_bytes=64)
+            xi[i] = pool.tile([P, D * 4], BF16, name=f"xi{i}", tag="xi", bufs=1, align_bytes=64)
 
         def join_pairs(i, lo, hi, copy):
             src = xp[i][:].rearrange("p a d e -> p (a d e)").bitcast(F32).rearrange("p (a d) -> p d a", a=2)
@@ -324,9 +327,11 @@ def tile_lambmlpbackwardstep_t_kernel(tc, x_bytes, x_scale, a, dy, w2, w1, m, v,
                 in_=w2g[:],
             )
 
-        load_a(0)
         load_scale(0, nc.scalar)
-        load_x(0, 2)
+        load_slots(0, 0, 1)
+        load_a(0)
+        load_slots(0, 1, 2)
+        load_slots(0, 2, 4)
         load_dy(0, 0)
         load_dy(0, 1)
         load_a(1)
@@ -341,64 +346,69 @@ def tile_lambmlpbackwardstep_t_kernel(tc, x_bytes, x_scale, a, dy, w2, w1, m, v,
             nc.vector.memset(offs[:, k : k + 1], n * GRID)
         nc.vector.memset(ones[:], 1.0)
         make_identity(nc, ident[:])
-        clamp(0)
         nc.vector.tensor_copy(out=ident_h[:], in_=ident[:])
         nc.vector.tensor_scalar(out=minus_h[:], in0=ident[:], scalar1=-1.0, scalar2=None, op0=MULT)
+        new_rows(0)
+        new_xi(0)
+        widen_pairs(0, 0, LACED_0, D)
+        clamp(0)
         load_a(3)
         load_x(2)
         load_dy(2, 1)
         gelu_slots(0, 0)
         gelu_slots(0, 1)
-        for t in range(2):
-            widen_pairs(0, t, 0, D)
+        for t in range(1, 4):
+            widen_pairs(0, t, LACED_0, D)
+        for t in range(4):
+            row_vector(0, t, 0, LACED_0)
         turn(0, 0, "g0")
         turn(0, 1, "g1")
         turn(0, 2, "a")
         turn(0, 3, "b")
         gelu_slots(0, 2)
-        for t in range(2, 4):
-            widen_pairs(0, t, 0, D)
-        new_xi(0)
         nc.vector.tensor_tensor(out=ge[0, 0][:], in0=ge[0, 0][:], in1=ge[0, 1][:], op=ADD)
         clamp(1)
         turn_a(1, "d")
         w2_banks = [turn_w2(h, "cx"[h]) for h in range(2)]
+        for c in range(0, LACED_0, P):
+            lace(0, c, "g2")
         nc.vector.scalar_tensor_tensor(out=ge[0, 2][:], in0=ge[0, 2][:], scalar=-2.0, in1=ge[0, 0][:], op0=MULT, op1=ADD)
         for t in range(4):
             empty(0, t)
         gelu_turned(1, 0)
-        gelu_turned(1, 1)
         empty_w2(0, w2_banks[0])
         empty_w2(1, w2_banks[1])
+        gelu_turned(1, 1)
         turn(1, 0, "g0")
         turn(1, 1, "g1")
         turn(1, 2, "b")
-        turn(1, 3, "g2")
-        join_pairs(0, 0, D, nc.vector.tensor_copy)
+        turn(1, 3, "c")
+        join_pairs(0, LACED_0, D, nc.vector.tensor_copy)
         q_dy(0)
         for t in range(4):
             widen_pairs(1, t, ROWS, D)
         q_w2()
-        clamp(2)
+        empty_lace(0, LACED_0)
         for t in range(4):
             empty(1, t)
         mm1(0, 0, "a")
         mm1(0, 1, "d")
-        turn_a(2, "x")
-        q_x(0, 0, D)
         new_rows(1)
         row_scalar(1, 0, 0, ROWS)
         gelu_slots(1, 2)
         for t in range(1, 4):
             row_vector(1, t, 0, ROWS)
+        clamp(2)
+        q_x(0, 0, D)
         q_dy(1)
+        turn_a(2, "x")
         add_nodes(1, 0, "b")
         add_nodes(1, 1, "c")
         gram = psum.tile([P, P], F32, name="gram", tag="g2", bufs=1)
         w_gram(0, GRAM_HEAD)
 
         last = NG - 1
-        for s in range(1, last):
+        for s in range(1, last - 1):
             if s + AHEAD + 1 < NG:
                 load_a(s + AHEAD + 1)
             if s + AHEAD < NG:
@@ -416,12 +426,12 @@ def tile_lambmlpbackwardstep_t_kernel(tc, x_bytes, x_scale, a, dy, w2, w1, m, v,
             diff(s, 1)
             gelu_turned(s + 1, 0)
             gelu_turned(s + 1, 1)
-            if s + 1 < last:
-                join_pairs(s, ROWS, D, nc.scalar.copy)
+            join_pairs(s, ROWS, D, nc.scalar.copy)
             if s == 2:
                 nc.scalar.copy(out=wsum[:, 0:1], in_=tot[:, 0:1])
-            lace(s, "a")
+            lace(s, 0, "a")
             turn(s + 1, 0, "d")
+            lace(s, P, "a")
             turn(s + 1, 1, "b")
             if s == 1:
                 w_gram(GRAM_HEAD, 2 * NJ)
@@ -435,39 +445,65 @@ def tile_lambmlpbackwardstep_t_kernel(tc, x_bytes, x_scale, a, dy, w2, w1, m, v,
             mm1(s, 0, "a")
             mm1(s, 1, "d")
             q_da(s - 1)
-            if s + 1 < last:
-                clamp(s + 2)
-                for t in range(4):
-                    widen_pairs(s + 1, t, ROWS, D)
-                if s == 1:
-                    w_trace()
-                new_rows(s + 1)
-                q_x(s, 0, D)
-                row_scalar(s + 1, 0, 0, ROWS)
-                gelu_slots(s + 1, 2)
-                for t in range(1, 4):
-                    row_vector(s + 1, t, 0, ROWS)
-            else:
-                join_pairs(s, ROWS, D, nc.vector.tensor_copy)
-                xr[last] = pool.tile([P, 4, D], BF16, name="xr_last", tag="xp", bufs=2)
-                row_vector(last, 3, 0, D)
-                q_x(s, 0, D)
-                row_scalar(last, 0, 0, D - REST)
-                gelu_slots(last, 2)
-                for t in range(1, 3):
-                    row_vector(last, t, 0, D - REST)
+            clamp(s + 2)
+            for t in range(4):
+                widen_pairs(s + 1, t, ROWS, D)
+            new_rows(s + 1)
+            row_scalar(s + 1, 0, 0, ROWS)
+            gelu_slots(s + 1, 2)
+            for t in range(1, 4):
+                row_vector(s + 1, t, 0, ROWS)
+            if s == 1:
+                w_trace()
+            q_x(s, 0, D)
             q_dy(s + 1)
             add_nodes(s + 1, 0, "b")
-            if s + 2 < NG:
-                turn_a(s + 2, "x")
+            turn_a(s + 2, "x")
             add_nodes(s + 1, 1, "c")
             if s == 1:
                 tot = w_total()
             mm2(s - 1, 0)
             mm2(s - 1, 1)
 
+        s = last - 1
+        new_xi(s)
+        weave(s, LACED, ROWS)
+        make_da(s - 1, 0)
+        make_da(s - 1, 1)
+        diff(s, 0)
+        diff(s, 1)
+        gelu_turned(last, 0)
+        gelu_turned(last, 1)
+        lace(s, 0, "a")
+        turn(last, 0, "d")
+        lace(s, P, "a")
+        turn(last, 1, "b")
+        turn(last, 2, "c")
+        turn(last, 3, "x")
+        empty(last, 0)
+        empty_lace(s)
+        for t in range(1, 4):
+            empty(last, t)
+        q_da(s - 1)
+        join_pairs(s, ROWS, D, nc.vector.tensor_copy)
+        xr[last] = pool.tile([P, 4, D], BF16, name="xr_last", tag="xp", bufs=2)
+        row_vector(last, 3, 0, D)
+        mm2(s - 2, 2)
+        mm1(s, 0, "a")
+        mm1(s, 1, "d")
+        row_scalar(last, 0, 0, GATE)
+        gelu_slots(last, 2)
+        row_vector(last, 0, GATE, D - REST)
+        for t in range(1, 3):
+            row_vector(last, t, 0, D - REST)
+        q_x(s, 0, 2 * F)
+        q_dy(last)
+        add_nodes(last, 0, "b")
+        add_nodes(last, 1, "c")
         gbank[LIVE] = psum.tile([P, BANK], F32, name="g3", tag="x", bufs=1)
-        new_xi(last)
+        mm2(s - 1, 0)
+
+        xi[last] = pool.tile([P, D * 4], BF16, name="xi_last", tag="xi_last", bufs=1, align_bytes=64)
         weave(last, 0, D - REST)
         make_da(last - 1, 0)
         diff(last, 0)
@@ -481,6 +517,7 @@ def tile_lambmlpbackwardstep_t_kernel(tc, x_bytes, x_scale, a, dy, w2, w1, m, v,
         nc.scalar.activation(out=winv[:, 0:1], in_=wsum[:, 0:1], func=ACT.Abs_reciprocal_sqrt)
         make_da(last, 0)
         make_da(last, 1)
+        mm2(s - 1, 1)
         mm2(last - 2, 2)
         for i in range(last - 1):
             mm2(i, LIVE)
@@ -488,7 +525,10 @@ def tile_lambmlpbackwardstep_t_kernel(tc, x_bytes, x_scale, a, dy, w2, w1, m, v,
         q_x(last, 0, F)
         q_da(last)
         q_x(last, F, 2 * F)
-        q_x(last, 2 * F, D)
+        q_x(last, 2 * F, 3 * F)
+        q_x(s, 2 * F, 3 * F)
+        q_x(last, 3 * F, D)
+        q_x(s, 3 * F, D)
         sq = pool.tile([P, NJ * F], F32, name="sq", tag="dyg", bufs=2, align_bytes=64)
         mn = pool.tile([P, NJ * F], F32, name="mn", tag="dyg", bufs=2, align_bytes=64)
 

@@ -30,10 +30,11 @@ WORDS = GROUP // 2
 AHEAD = 2
 LIVE = 3
 
-GRID = 2.0**-21
-NODES = (-9184.0, 3999.0, -7083.0)
+GRID = 2.0**-24
+NODES = (-67009.0, 29183.0, -51681.0)
+WIDTH = (NODES[0] + NODES[1] - 2 * NODES[2]) * GRID
 CLAMP = 7.0
-G_SCALE = 1.0 / 64.0
+G_SCALE = 1.0 / 64.0 / WIDTH
 NEW_SHARE = 0.4 / 0.6
 
 WOVEN = 384
@@ -215,14 +216,11 @@ def tile_lambmlpbackwardstep_t_kernel(tc, x_bytes, x_scale, a, dy, w2, w1, m, v,
             if h == 0:
                 da[i] = pool.tile([P, 4 * F], BF16, name=f"da{i}", tag="da", bufs=2, align_bytes=64)
             s = slice(BANK * h, BANK * (h + 1))
-            slope = ge[i, 2][:, s].rearrange("p (f t) -> p f t", t=4)
-            nc.vector.scalar_tensor_tensor(
-                out=da[i][:, s].rearrange("p (f t) -> p f t", t=4),
-                in0=slope,
-                scalar=1.0 / ((NODES[0] + NODES[1] - 2 * NODES[2]) * GRID),
-                in1=dh[i, h][:].rearrange("p t f -> p f t"),
-                op0=MULT,
-                op1=MULT,
+            nc.vector.tensor_tensor(
+                out=da[i][:, s].rearrange("p (c e t) -> p c t e", t=4, e=2),
+                in0=ge[i, 2][:, s].rearrange("p (c e t) -> p c t e", t=4, e=2),
+                in1=dh[i, h][:].rearrange("p t (c e) -> p c t e", e=2),
+                op=MULT,
             )
 
         def q_da(i):

@@ -43,6 +43,9 @@ ROWS = WOVEN + LACED
 REST = 384
 LACED_0 = 128
 GATE = 128
+RUN = 4
+FIRST = 512
+LATE = 448
 GRAM_HEAD = 8
 
 
@@ -83,7 +86,7 @@ def tile_lambmlpbackwardstep_t_kernel(tc, x_bytes, x_scale, a, dy, w2, w1, m, v,
         s_v = x_scale.rearrange("(g p t) o -> g p (t o)", p=P, t=4)
         x_v = x_bytes.rearrange("(g p t) d -> g p t d", p=P, t=4)
 
-        at, ac, ta, ge, sb, dyt, tp, dyg, dyq, dyqs, dh, da, xs, x8, xp, xr, xw, xi, gbank = ({} for k in range(19))
+        at, ac, ta, ge, sb, dyt, tp, dyg, dyq, dyqs, dh, da, xs, x8, xr, xw, xi, gbank = ({} for k in range(18))
 
         def load_a(i):
             at[i] = pool.tile([P, 4, F], BF16, name=f"a{i}", tag="a", bufs=AHEAD + 1)
@@ -112,7 +115,12 @@ def tile_lambmlpbackwardstep_t_kernel(tc, x_bytes, x_scale, a, dy, w2, w1, m, v,
         def clamp(i):
             ac[i] = pool.tile([P, 4 * F], BF16, name=f"ac{i}", tag="ac", bufs=3)
             nc.vector.tensor_scalar(
-                out=ac[i][:], in0=at[i][:].rearrange("p t f -> p (t f)"), scalar1=CLAMP, scalar2=-CLAMP, op0=MIN, op1=MAX
+                out=ac[i][:].rearrange("p (q t e) -> p q t e", t=4, e=2),
+                in0=at[i][:].rearrange("p t (q e) -> p q t e", e=2),
+                scalar1=CLAMP,
+                scalar2=-CLAMP,
+                op0=MIN,
+                op1=MAX,
             )
 
         def turn_a(i, tag):
@@ -129,8 +137,8 @@ def tile_lambmlpbackwardstep_t_kernel(tc, x_bytes, x_scale, a, dy, w2, w1, m, v,
         def gelu_slots(i, n):
             ge[i, n] = pool.tile([P, 4 * F], F32, name=f"ge{i}_{n}", tag=f"ge{n}", bufs=2)
             nc.scalar.activation(
-                out=ge[i, n][:].rearrange("p (f t) -> p f t", t=4),
-                in_=ac[i][:].rearrange("p (t f) -> p f t", t=4),
+                out=ge[i, n][:].rearrange("p (q e t) -> p q e t", e=2, t=4),
+                in_=ac[i][:].rearrange("p (q t e) -> p q e t", t=4, e=2),
                 func=ACT.Gelu,
                 bias=offs[:, n : n + 1],
             )
@@ -171,7 +179,7 @@ def tile_lambmlpbackwardstep_t_kernel(tc, x_bytes, x_scale, a, dy, w2, w1, m, v,
                 out=slots(i, e),
                 in0=slots(i, e),
                 scalar=-2.0,
-                in1=sb[i, e][:].rearrange("p t q -> p q t"),
+                in1=sb[i, e][:].rearrange("p k (q t) -> p (k q) t", t=4),
                 op0=MULT,
                 op1=ADD,
             )
@@ -226,19 +234,8 @@ def tile_lambmlpbackwardstep_t_kernel(tc, x_bytes, x_scale, a, dy, w2, w1, m, v,
         def q_da(i):
             nc.vector.quantize_mx(out=daq[:, i, :].bitcast(FP8X4), scales=daqs[:, i, :], in_=da[i][:])
 
-        def widen_pairs(i, t, lo, hi):
-            if t == 0:
-                xp[i] = pool.tile([P, 2, D, 2], BF16, name=f"xp{i}", tag="xp", bufs=2)
-            nc.vector.tensor_scalar(
-                out=xp[i][:, t // 2, lo:hi, t % 2],
-                in0=x8[i][:, t, lo:hi].bitcast(FP8),
-                scalar1=xs[i][:, t : t + 1],
-                scalar2=None,
-                op0=MULT,
-            )
-
         def new_rows(i):
-            xr[i] = pool.tile([P, 4, ROWS], BF16, name=f"xr{i}", tag="xr", bufs=3)
+            xr[i] = pool.tile([P, 4, D], BF16, name=f"xr{i}", tag="xr", bufs=3)
 
         def row_vector(i, t, lo, hi):
             nc.vector.tensor_scalar(
@@ -281,10 +278,11 @@ def tile_lambmlpbackwardstep_t_kernel(tc, x_bytes, x_scale, a, dy, w2, w1, m, v,
         def new_xi(i):
             xi[i] = pool.tile([P, D * 4], BF16, name=f"xi{i}", tag="xi", bufs=1, align_bytes=64)
 
-        def join_pairs(i, lo, hi, copy):
-            src = xp[i][:].rearrange("p a d e -> p (a d e)").bitcast(F32).rearrange("p (a d) -> p d a", a=2)
-            dst = xi[i][:].bitcast(F32).rearrange("p (d a) -> p d a", a=2)
-            copy(out=dst[:, lo:hi, :], in_=src[:, lo:hi, :])
+        def braid(i, lo, hi):
+            nc.vector.tensor_copy(
+                out=xi[i][:, 4 * lo : 4 * hi].rearrange("p (c e t) -> p c t e", e=RUN, t=4),
+                in_=xr[i][:, :, lo:hi].rearrange("p t (c e) -> p c t e", e=RUN),
+            )
 
         def q_x(i, lo, hi):
             s = slice(lo, hi)
@@ -348,7 +346,7 @@ def tile_lambmlpbackwardstep_t_kernel(tc, x_bytes, x_scale, a, dy, w2, w1, m, v,
         nc.vector.tensor_scalar(out=minus_h[:], in0=ident[:], scalar1=-1.0, scalar2=None, op0=MULT)
         new_rows(0)
         new_xi(0)
-        widen_pairs(0, 0, LACED_0, D)
+        row_vector(0, 0, 0, D)
         clamp(0)
         load_a(3)
         load_x(2)
@@ -356,9 +354,8 @@ def tile_lambmlpbackwardstep_t_kernel(tc, x_bytes, x_scale, a, dy, w2, w1, m, v,
         gelu_slots(0, 0)
         gelu_slots(0, 1)
         for t in range(1, 4):
-            widen_pairs(0, t, LACED_0, D)
-        for t in range(4):
-            row_vector(0, t, 0, LACED_0)
+            row_vector(0, t, 0, D)
+        braid(0, LACED_0, FIRST)
         turn(0, 0, "g0")
         turn(0, 1, "g1")
         turn(0, 2, "a")
@@ -381,21 +378,21 @@ def tile_lambmlpbackwardstep_t_kernel(tc, x_bytes, x_scale, a, dy, w2, w1, m, v,
         turn(1, 1, "g1")
         turn(1, 2, "b")
         turn(1, 3, "c")
-        join_pairs(0, LACED_0, D, nc.vector.tensor_copy)
+        braid(0, FIRST, D)
         q_dy(0)
-        for t in range(4):
-            widen_pairs(1, t, ROWS, D)
+        new_rows(1)
+        row_vector(1, 3, 0, D)
+        row_vector(1, 2, 0, D)
         q_w2()
         empty_lace(0, LACED_0)
         for t in range(4):
             empty(1, t)
         mm1(0, 0, "a")
         mm1(0, 1, "d")
-        new_rows(1)
         row_scalar(1, 0, 0, ROWS)
         gelu_slots(1, 2)
-        for t in range(1, 4):
-            row_vector(1, t, 0, ROWS)
+        row_vector(1, 0, ROWS, D)
+        row_vector(1, 1, 0, D)
         clamp(2)
         q_x(0, 0, D)
         q_dy(1)
@@ -424,7 +421,8 @@ def tile_lambmlpbackwardstep_t_kernel(tc, x_bytes, x_scale, a, dy, w2, w1, m, v,
             diff(s, 1)
             gelu_turned(s + 1, 0)
             gelu_turned(s + 1, 1)
-            join_pairs(s, ROWS, D, nc.scalar.copy)
+            new_rows(s + 1)
+            row_scalar(s + 1, 1, 0, D)
             if s == 2:
                 nc.scalar.copy(out=wsum[:, 0:1], in_=tot[:, 0:1])
             lace(s, 0, "a")
@@ -444,13 +442,12 @@ def tile_lambmlpbackwardstep_t_kernel(tc, x_bytes, x_scale, a, dy, w2, w1, m, v,
             mm1(s, 1, "d")
             q_da(s - 1)
             clamp(s + 2)
-            for t in range(4):
-                widen_pairs(s + 1, t, ROWS, D)
-            new_rows(s + 1)
-            row_scalar(s + 1, 0, 0, ROWS)
+            braid(s, ROWS, D)
+            row_scalar(s + 1, 0, 0, LATE)
             gelu_slots(s + 1, 2)
-            for t in range(1, 4):
-                row_vector(s + 1, t, 0, ROWS)
+            row_vector(s + 1, 0, LATE, D)
+            for t in range(2, 4):
+                row_vector(s + 1, t, 0, D)
             if s == 1:
                 w_trace()
             q_x(s, 0, D)
@@ -483,8 +480,8 @@ def tile_lambmlpbackwardstep_t_kernel(tc, x_bytes, x_scale, a, dy, w2, w1, m, v,
         for t in range(1, 4):
             empty(last, t)
         q_da(s - 1)
-        join_pairs(s, ROWS, D, nc.vector.tensor_copy)
-        xr[last] = pool.tile([P, 4, D], BF16, name="xr_last", tag="xp", bufs=2)
+        braid(s, ROWS, D)
+        new_rows(last)
         row_vector(last, 3, 0, D)
         mm2(s - 2, 2)
         mm1(s, 0, "a")

@@ -46,6 +46,7 @@ GATE = 128
 RUN = 4
 FIRST = 512
 LATE = 448
+WARM = 256
 GRAM_HEAD = 8
 
 
@@ -323,6 +324,11 @@ def tile_lambmlpbackwardstep_t_kernel(tc, x_bytes, x_scale, a, dy, w2, w1, m, v,
                 in_=w2g[:],
             )
 
+        def warm_up(columns, tag, name):
+            idle = psum.tile([P, BANK], F32, name=name, tag=tag, bufs=1)
+            words = ac[0][:].bitcast(F32)
+            nc.tensor.matmul(idle[:, 0:columns], lhsT=ident[:], rhs=words[:, 0:columns], start=True, stop=True)
+
         load_scale(0, nc.scalar)
         load_slots(0, 0, 1)
         load_a(0)
@@ -356,8 +362,10 @@ def tile_lambmlpbackwardstep_t_kernel(tc, x_bytes, x_scale, a, dy, w2, w1, m, v,
         for t in range(1, 4):
             row_vector(0, t, 0, D)
         braid(0, LACED_0, FIRST)
+        warm_up(2 * WARM, "g2", "idle0")
         turn(0, 0, "g0")
         turn(0, 1, "g1")
+        warm_up(WARM, "g2", "idle1")
         turn(0, 2, "a")
         turn(0, 3, "b")
         gelu_slots(0, 2)
@@ -374,8 +382,10 @@ def tile_lambmlpbackwardstep_t_kernel(tc, x_bytes, x_scale, a, dy, w2, w1, m, v,
         empty_w2(0, w2_banks[0])
         empty_w2(1, w2_banks[1])
         gelu_turned(1, 1)
+        warm_up(WARM, "a", "idle2")
         turn(1, 0, "g0")
         turn(1, 1, "g1")
+        warm_up(WARM, "x", "idle3")
         turn(1, 2, "b")
         turn(1, 3, "c")
         braid(0, FIRST, D)

@@ -37,7 +37,7 @@ CLAMP = 7.0
 G_SCALE = 1.0 / 64.0 / WIDTH
 NEW_SHARE = 0.4 / 0.6
 
-WOVEN = 384
+WOVEN = 480
 LACED = 256
 ROWS = WOVEN + LACED
 REST = 384
@@ -255,12 +255,15 @@ def tile_lambmlpbackwardstep_t_kernel(tc, x_bytes, x_scale, a, dy, w2, w1, m, v,
         def by_column(i, lo, hi):
             return xr[i][:, :, lo:hi].rearrange("p t d -> p d t")
 
-        def words_of(i, lo, hi):
-            return xi[i][:, 4 * lo : 4 * hi].rearrange("p (d t) -> p d t", t=4)
+        def runs_in(i, lo, hi):
+            return xr[i][:, :, lo:hi].rearrange("p t (c e) -> p c t e", e=RUN)
+
+        def runs_out(i, lo, hi):
+            return xi[i][:, 4 * lo : 4 * hi].rearrange("p (c e t) -> p c t e", e=RUN, t=4)
 
         def weave(i, lo, hi):
             nc.gpsimd.tensor_scalar(
-                out=words_of(i, lo, hi), in0=by_column(i, lo, hi), scalar1=1.0, scalar2=0.0, op0=MULT, op1=ADD
+                out=runs_out(i, lo, hi), in0=runs_in(i, lo, hi), scalar1=1.0, scalar2=0.0, op0=MULT, op1=ADD
             )
 
         def lace(i, c, tag):
@@ -274,16 +277,13 @@ def tile_lambmlpbackwardstep_t_kernel(tc, x_bytes, x_scale, a, dy, w2, w1, m, v,
             nc.scalar.copy(out=xi[i][:, 0 : 4 * width], in_=xw[i][:, 0 : 4 * width])
 
         def join_rows(i, lo, hi):
-            nc.scalar.copy(out=words_of(i, lo, hi), in_=by_column(i, lo, hi))
+            nc.scalar.copy(out=runs_out(i, lo, hi), in_=runs_in(i, lo, hi))
 
         def new_xi(i):
             xi[i] = pool.tile([P, D * 4], BF16, name=f"xi{i}", tag="xi", bufs=1, align_bytes=64)
 
         def braid(i, lo, hi):
-            nc.vector.tensor_copy(
-                out=xi[i][:, 4 * lo : 4 * hi].rearrange("p (c e t) -> p c t e", e=RUN, t=4),
-                in_=xr[i][:, :, lo:hi].rearrange("p t (c e) -> p c t e", e=RUN),
-            )
+            nc.vector.tensor_copy(out=runs_out(i, lo, hi), in_=runs_in(i, lo, hi))
 
         def q_x(i, lo, hi):
             s = slice(lo, hi)
@@ -399,9 +399,9 @@ def tile_lambmlpbackwardstep_t_kernel(tc, x_bytes, x_scale, a, dy, w2, w1, m, v,
             empty(1, t)
         mm1(0, 0, "a")
         mm1(0, 1, "d")
-        row_scalar(1, 0, 0, ROWS)
+        row_scalar(1, 0, 0, D - REST)
         gelu_slots(1, 2)
-        row_vector(1, 0, ROWS, D)
+        row_vector(1, 0, D - REST, D)
         row_vector(1, 1, 0, D)
         clamp(2)
         q_x(0, 0, D)

@@ -37,7 +37,7 @@ CLAMP = 7.0
 G_SCALE = 1.0 / 64.0 / WIDTH
 NEW_SHARE = 0.4 / 0.6
 
-WOVEN = 480
+WOVEN = 512
 LACED = 256
 ROWS = WOVEN + LACED
 REST = 384
@@ -45,7 +45,7 @@ LACED_0 = 128
 GATE = 128
 RUN = 4
 FIRST = 512
-LATE = 448
+LATE = 320
 WARM = 256
 GRAM_HEAD = 8
 
@@ -266,15 +266,15 @@ def tile_lambmlpbackwardstep_t_kernel(tc, x_bytes, x_scale, a, dy, w2, w1, m, v,
                 out=runs_out(i, lo, hi), in0=runs_in(i, lo, hi), scalar1=1.0, scalar2=0.0, op0=MULT, op1=ADD
             )
 
-        def lace(i, c, tag):
+        def lace(i, lo, c, tag):
             if c == 0:
                 xw[i] = psum.tile([P, 4 * LACED], BF16, name=f"xw{i}", tag=tag, bufs=1)
             nc.tensor.matmul(
-                xw[i][:, 4 * c : 4 * (c + P)], lhsT=ident_h[:], rhs=by_column(i, c, c + P), start=True, stop=True
+                xw[i][:, 4 * c : 4 * (c + P)], lhsT=ident_h[:], rhs=by_column(i, lo + c, lo + c + P), start=True, stop=True
             )
 
-        def empty_lace(i, width=LACED):
-            nc.scalar.copy(out=xi[i][:, 0 : 4 * width], in_=xw[i][:, 0 : 4 * width])
+        def empty_lace(i, lo, width=LACED):
+            nc.scalar.copy(out=xi[i][:, 4 * lo : 4 * (lo + width)], in_=xw[i][:, 0 : 4 * width])
 
         def join_rows(i, lo, hi):
             nc.scalar.copy(out=runs_out(i, lo, hi), in_=runs_in(i, lo, hi))
@@ -374,7 +374,7 @@ def tile_lambmlpbackwardstep_t_kernel(tc, x_bytes, x_scale, a, dy, w2, w1, m, v,
         turn_a(1, "d")
         w2_banks = [turn_w2(h, "cx"[h]) for h in range(2)]
         for c in range(0, LACED_0, P):
-            lace(0, c, "g2")
+            lace(0, 0, c, "g2")
         nc.vector.scalar_tensor_tensor(out=ge[0, 2][:], in0=ge[0, 2][:], scalar=-2.0, in1=ge[0, 0][:], op0=MULT, op1=ADD)
         for t in range(4):
             empty(0, t)
@@ -394,7 +394,7 @@ def tile_lambmlpbackwardstep_t_kernel(tc, x_bytes, x_scale, a, dy, w2, w1, m, v,
         row_vector(1, 3, 0, D)
         row_vector(1, 2, 0, D)
         q_w2()
-        empty_lace(0, LACED_0)
+        empty_lace(0, 0, LACED_0)
         for t in range(4):
             empty(1, t)
         mm1(0, 0, "a")
@@ -424,7 +424,7 @@ def tile_lambmlpbackwardstep_t_kernel(tc, x_bytes, x_scale, a, dy, w2, w1, m, v,
                 load_rows(mt, m)
                 load_rows(vt, v)
             new_xi(s)
-            weave(s, LACED, ROWS)
+            weave(s, 0, WOVEN)
             make_da(s - 1, 0)
             make_da(s - 1, 1)
             diff(s, 0)
@@ -435,15 +435,15 @@ def tile_lambmlpbackwardstep_t_kernel(tc, x_bytes, x_scale, a, dy, w2, w1, m, v,
             row_scalar(s + 1, 1, 0, D)
             if s == 2:
                 nc.scalar.copy(out=wsum[:, 0:1], in_=tot[:, 0:1])
-            lace(s, 0, "a")
+            lace(s, WOVEN, 0, "a")
             turn(s + 1, 0, "d")
-            lace(s, P, "a")
+            lace(s, WOVEN, P, "a")
             turn(s + 1, 1, "b")
             if s == 1:
                 w_gram(GRAM_HEAD, 2 * NJ)
             turn(s + 1, 2, "c")
             turn(s + 1, 3, "x")
-            empty_lace(s)
+            empty_lace(s, WOVEN)
             for t in range(4):
                 empty(s + 1, t)
             if s > 1:
@@ -472,21 +472,21 @@ def tile_lambmlpbackwardstep_t_kernel(tc, x_bytes, x_scale, a, dy, w2, w1, m, v,
 
         s = last - 1
         new_xi(s)
-        weave(s, LACED, ROWS)
+        weave(s, 0, WOVEN)
         make_da(s - 1, 0)
         make_da(s - 1, 1)
         diff(s, 0)
         diff(s, 1)
         gelu_turned(last, 0)
         gelu_turned(last, 1)
-        lace(s, 0, "a")
+        lace(s, WOVEN, 0, "a")
         turn(last, 0, "d")
-        lace(s, P, "a")
+        lace(s, WOVEN, P, "a")
         turn(last, 1, "b")
         turn(last, 2, "c")
         turn(last, 3, "x")
         empty(last, 0)
-        empty_lace(s)
+        empty_lace(s, WOVEN)
         for t in range(1, 4):
             empty(last, t)
         q_da(s - 1)

@@ -37,15 +37,16 @@ CLAMP = 7.0
 G_SCALE = 1.0 / 64.0 / WIDTH
 NEW_SHARE = 0.4 / 0.6
 
-WOVEN = 512
+WOVEN = 464
 LACED = 256
 ROWS = WOVEN + LACED
 REST = 384
 LACED_0 = 128
 GATE = 128
-RUN = 4
+FETCH = 4
+LINE = 8
 FIRST = 512
-LATE = 320
+LATE = 384
 WARM = 256
 GRAM_HEAD = 8
 
@@ -255,15 +256,20 @@ def tile_lambmlpbackwardstep_t_kernel(tc, x_bytes, x_scale, a, dy, w2, w1, m, v,
         def by_column(i, lo, hi):
             return xr[i][:, :, lo:hi].rearrange("p t d -> p d t")
 
-        def runs_in(i, lo, hi):
-            return xr[i][:, :, lo:hi].rearrange("p t (c e) -> p c t e", e=RUN)
+        def runs_in(i, lo, hi, run):
+            return xr[i][:, :, lo:hi].rearrange("p t (c e) -> p c t e", e=run)
 
-        def runs_out(i, lo, hi):
-            return xi[i][:, 4 * lo : 4 * hi].rearrange("p (c e t) -> p c t e", e=RUN, t=4)
+        def runs_out(i, lo, hi, run):
+            return xi[i][:, 4 * lo : 4 * hi].rearrange("p (c e t) -> p c t e", e=run, t=4)
 
         def weave(i, lo, hi):
             nc.gpsimd.tensor_scalar(
-                out=runs_out(i, lo, hi), in0=runs_in(i, lo, hi), scalar1=1.0, scalar2=0.0, op0=MULT, op1=ADD
+                out=runs_out(i, lo, hi, FETCH),
+                in0=runs_in(i, lo, hi, FETCH),
+                scalar1=1.0,
+                scalar2=0.0,
+                op0=MULT,
+                op1=ADD,
             )
 
         def lace(i, lo, c, tag):
@@ -277,13 +283,13 @@ def tile_lambmlpbackwardstep_t_kernel(tc, x_bytes, x_scale, a, dy, w2, w1, m, v,
             nc.scalar.copy(out=xi[i][:, 4 * lo : 4 * (lo + width)], in_=xw[i][:, 0 : 4 * width])
 
         def join_rows(i, lo, hi):
-            nc.scalar.copy(out=runs_out(i, lo, hi), in_=runs_in(i, lo, hi))
+            nc.scalar.copy(out=runs_out(i, lo, hi, LINE), in_=runs_in(i, lo, hi, LINE))
 
         def new_xi(i):
             xi[i] = pool.tile([P, D * 4], BF16, name=f"xi{i}", tag="xi", bufs=1, align_bytes=64)
 
         def braid(i, lo, hi):
-            nc.vector.tensor_copy(out=runs_out(i, lo, hi), in_=runs_in(i, lo, hi))
+            nc.vector.tensor_copy(out=runs_out(i, lo, hi, LINE), in_=runs_in(i, lo, hi, LINE))
 
         def q_x(i, lo, hi):
             s = slice(lo, hi)

from contextlib import ExitStack

import concourse.mybir as mybir
from concourse.masks import make_identity

F32 = mybir.dt.float32
BF16 = mybir.dt.bfloat16
U32 = mybir.dt.uint32
U8 = mybir.dt.uint8
FP8 = mybir.dt.float8_e4m3fn
FP8X4 = mybir.dt.float8_e4m3fn_x4
MULT = mybir.AluOpType.mult
ADD = mybir.AluOpType.add
SUB = mybir.AluOpType.subtract
MAX = mybir.AluOpType.max
MIN = mybir.AluOpType.min
ACT = mybir.ActivationFunctionType

T, D, F = 4096, 1024, 256
FLOPS = 4 * T * D * F

P = 128
GROUP = 4 * P
NG = T // GROUP
NC = D // GROUP
NJ = D // P
NB = NJ // 2
BANK = 2 * F
WORDS = GROUP // 2
AHEAD = 2
LIVE = 3

GRID = 2.0**-24
NODES = (-67009.0, 29183.0, -51681.0)
WIDTH = (NODES[0] + NODES[1] - 2 * NODES[2]) * GRID
CLAMP = 7.0
G_SCALE = 1.0 / 64.0 / WIDTH
NEW_SHARE = 0.4 / 0.6

WOVEN = 464
LACED = 256
ROWS = WOVEN + LACED
REST = 384
LACED_0 = 128
GATE = 128
FETCH = 4
LINE = 8
FIRST = 512
LATE = 384
WARM = 256
GRAM_HEAD = 8


def tile_lambmlpbackwardstep_t_kernel(tc, x_bytes, x_scale, a, dy, w2, w1, m, v, out):
    nc = tc.nc
    with ExitStack() as ctx:
        keep = ctx.enter_context(tc.tile_pool(name="keep", bufs=1))
        pool = ctx.enter_context(tc.tile_pool(name="work", bufs=2))
        psum = ctx.enter_context(tc.psum_pool(name="psum", bufs=1))
        ctx.enter_context(tc.manual_schedule())

        ident = keep.tile([P, P], F32, name="ident")
        ones = keep.tile([P, P], F32, name="ones")
        ident_h = keep.tile([P, P], BF16, name="ident_h")
        minus_h = keep.tile([P, P], BF16, name="minus_h")
        offs = keep.tile([P, 4], F32, name="offs")
        xq = keep.tile([P, NG, D], U32, name="xq", align_bytes=64)
        xqs = keep.tile([P, NG, D], U8, name="xqs", align_bytes=64)
        daq = keep.tile([P, NG, F], U32, name="daq", align_bytes=64)
        daqs = keep.tile([P, NG, F], U8, name="daqs", align_bytes=64)
        w2r = keep.tile([P, 2, D], BF16, name="w2r", align_bytes=64)
        w2g = keep.tile([P, NC * F * 4], BF16, name="w2g", align_bytes=64)
        w2q = keep.tile([P, NC, F], U32, name="w2q", align_bytes=64)
        w2qs = keep.tile([P, NC, F], U8, name="w2qs", align_bytes=64)
        w1t = keep.tile([P, NJ * F], BF16, name="w1t")
        mt = keep.tile([P, NJ * F], BF16, name="mt")
        vt = keep.tile([P, NJ * F], BF16, name="vt")
        diag = keep.tile([P, P], F32, name="diag")
        rsum = keep.tile([P, 8], F32, name="rsum")
        wall = keep.tile([P, 8], F32, name="wall")
        wsum = keep.tile([P, 8], F32, name="wsum")
        winv = keep.tile([P, 8], F32, name="winv")
        winv2 = keep.tile([P, 8], F32, name="winv2")
        step = keep.tile([P, 8], F32, name="step")

        a_v = a.rearrange("(g p t) f -> g p t f", p=P, t=4)
        dy_v = dy.rearrange("(g p t) d -> g p t d", p=P, t=4)
        s_v = x_scale.rearrange("(g p t) o -> g p (t o)", p=P, t=4)
        x_v = x_bytes.rearrange("(g p t) d -> g p t d", p=P, t=4)

        at, ac, ta, ge, sb, dyt, tp, dyg, dyq, dyqs, dh, da, xs, x8, xr, xw, xi, gbank = ({} for k in range(18))

        def load_a(i):
            at[i] = pool.tile([P, 4, F], BF16, name=f"a{i}", tag="a", bufs=AHEAD + 1)
            nc.sync.dma_start(out=at[i][:], in_=a_v[i])

        def load_dy(i, u):
            dyt[i, u] = pool.tile([P, 2, D], BF16, name=f"dy{i}_{u}", tag="dy", bufs=2 * (AHEAD + 1))
            nc.sync.dma_start(out=dyt[i, u][:], in_=dy_v[i][:, 2 * u : 2 * u + 2, :])

        def load_scale(i, queue):
            xs[i] = keep.tile([P, 4], F32, name=f"xs{i}")
            queue.dma_start(out=xs[i][:], in_=s_v[i])

        def load_slots(i, lo, hi):
            if lo == 0:
                x8[i] = pool.tile([P, 4, D], U8, name=f"x8_{i}", tag="x8", bufs=AHEAD + 1)
            nc.sync.dma_start(out=x8[i][:, lo:hi, :], in_=x_v[i][:, lo:hi, :])

        def load_x(i):
            load_scale(i, nc.sync)
            load_slots(i, 0, 4)

        def load_rows(dst, src):
            nc.sync.dma_start(out=dst[:].rearrange("p (j f) -> p j f", f=F), in_=src.rearrange("(j p) f -> p j f", p=P))

        def clamp(i):
            ac[i] = pool.tile([P, 4 * F], BF16, name=f"ac{i}", tag="ac", bufs=3)
            nc.vector.tensor_scalar(
                out=ac[i][:].rearrange("p (q t e) -> p q t e", t=4, e=2),
                in0=at[i][:].rearrange("p t (q e) -> p q t e", e=2),
                scalar1=CLAMP,
                scalar2=-CLAMP,
                op0=MIN,
                op1=MAX,
            )

        def turn_a(i, tag):
            ta[i] = psum.tile([P, 4, P], F32, name=f"ta{i}", tag=tag, bufs=1)
            words = ac[i][:].bitcast(F32)
            for k in range(4):
                nc.tensor.transpose(ta[i][:, k, :], words[:, P * k : P * (k + 1)], ident[:])

        def gelu_turned(i, n):
            ge[i, n] = pool.tile([P, 4, 2, P], F32, name=f"ge{i}_{n}", tag=f"ge{n}", bufs=2)
            src = ta[i][:].rearrange("q k p -> q (k p)").bitcast(BF16).rearrange("q (k p e) -> q k e p", k=4, e=2)
            nc.scalar.activation(out=ge[i, n][:], in_=src, func=ACT.Gelu, bias=offs[:, n : n + 1])

        def gelu_slots(i, n):
            ge[i, n] = pool.tile([P, 4 * F], F32, name=f"ge{i}_{n}", tag=f"ge{n}", bufs=2)
            nc.scalar.activation(
                out=ge[i, n][:].rearrange("p (q e t) -> p q e t", e=2, t=4),
                in_=ac[i][:].rearrange("p (q t e) -> p q e t", t=4, e=2),
                func=ACT.Gelu,
                bias=offs[:, n : n + 1],
            )

        def slots(i, e):
            return ge[i, 2][:].rearrange("p (q e t) -> p q e t", e=2, t=4)[:, :, e, :]

        def w_gram(lo, hi):
            for k in range(lo, hi):
                block = w1t[:, P * k : P * (k + 1)]
                nc.tensor.matmul(gram[:], lhsT=block, rhs=block, start=(k == 0), stop=(k == 2 * NJ - 1))

        def w_trace():
            nc.vector.scalar_tensor_tensor(
                out=diag[:], in0=gram[:], scalar=0.25, in1=ident[:], op0=MULT, op1=MULT, accum_out=wall[:, 0:1]
            )

        def w_total():
            tot = psum.tile([P, 8], F32, name="tot", tag="g2", bufs=1)
            nc.tensor.matmul(tot[:, 0:1], lhsT=ones[:], rhs=wall[:, 0:1], start=True, stop=True)
            return tot

        def add_nodes(i, e, tag):
            sb[i, e] = psum.tile([P, 4, P], F32, name=f"sb{i}_{e}", tag=tag, bufs=1)
            for t in range(4):
                for n in range(2):
                    nc.tensor.matmul(
                        sb[i, e][:, t, :],
                        lhsT=ge[i, n][:, t, e, :],
                        rhs=ident[:],
                        start=(n == 0),
                        stop=(n == 1),
                        is_transpose=True,
                    )

        def diff(i, e):
            nc.vector.scalar_tensor_tensor(
                out=slots(i, e),
                in0=slots(i, e),
                scalar=-2.0,
                in1=sb[i, e][:].rearrange("p k (q t) -> p (k q) t", t=4),
                op0=MULT,
                op1=ADD,
            )

        def turn(i, t, tag):
            tp[i, t] = psum.tile([P, NC, 2, P], F32, name=f"tp{i}_{t}", tag=tag, bufs=1)
            words = dyt[i, t // 2][:, t % 2, :].bitcast(F32)
            for c in range(NC):
                for u in range(2):
                    nc.tensor.transpose(tp[i, t][:, c, u, :], words[:, WORDS * c + u : WORDS * (c + 1) : 2], ident[:])

        def empty(i, t):
            if t == 0:
                dyg[i] = pool.tile([P, 4, D], BF16, name=f"dyg{i}", tag="dyg", bufs=2, align_bytes=64)
            dst = dyg[i][:, t, :].bitcast(F32).rearrange("q (c r u) -> q c r u", c=NC, u=2)
            nc.scalar.copy(out=dst, in_=tp[i, t][:].rearrange("q c u r -> q c r u"))

        def q_dy(i):
            dyq[i] = pool.tile([P, 4, NC, P], U32, name=f"dyq{i}", tag="dyq", bufs=2, align_bytes=64)
            dyqs[i] = pool.tile([P, 4, NC, P], U8, name=f"dyqs{i}", tag="dyqs", bufs=2, align_bytes=64)
            nc.vector.quantize_mx(
                out=dyq[i][:].rearrange("p t c r -> p (t c r)").bitcast(FP8X4),
                scales=dyqs[i][:].rearrange("p t c r -> p (t c r)"),
                in_=dyg[i][:].rearrange("p t k -> p (t k)"),
            )

        def mm1(i, h, tag):
            dh[i, h] = psum.tile([P, 4, P], F32, name=f"dh{i}_{h}", tag=tag, bufs=1)
            for t in range(4):
                for c in range(NC):
                    nc.tensor.matmul_mx(
                        out=dh[i, h][:, t, :],
                        lhsT=dyq[i][:, t, c, :].bitcast(FP8X4),
                        lhsT_scale=dyqs[i][:, t, c, :],
                        rhs=w2q[:, c, P * h : P * (h + 1)].bitcast(FP8X4),
                        rhs_scale=w2qs[:, c, P * h : P * (h + 1)],
                        start=(c == 0),
                        stop=(c == NC - 1),
                    )

        def make_da(i, h):
            if h == 0:
                da[i] = pool.tile([P, 4 * F], BF16, name=f"da{i}", tag="da", bufs=2, align_bytes=64)
            s = slice(BANK * h, BANK * (h + 1))
            nc.vector.tensor_tensor(
                out=da[i][:, s].rearrange("p (c e t) -> p c t e", t=4, e=2),
                in0=ge[i, 2][:, s].rearrange("p (c e t) -> p c t e", t=4, e=2),
                in1=dh[i, h][:].rearrange("p t (c e) -> p c t e", e=2),
                op=MULT,
            )

        def q_da(i):
            nc.vector.quantize_mx(out=daq[:, i, :].bitcast(FP8X4), scales=daqs[:, i, :], in_=da[i][:])

        def new_rows(i):
            xr[i] = pool.tile([P, 4, D], BF16, name=f"xr{i}", tag="xr", bufs=3)

        def row_vector(i, t, lo, hi):
            nc.vector.tensor_scalar(
                out=xr[i][:, t, lo:hi],
                in0=x8[i][:, t, lo:hi].bitcast(FP8),
                scalar1=xs[i][:, t : t + 1],
                scalar2=None,
                op0=MULT,
            )

        def row_scalar(i, t, lo, hi):
            nc.scalar.activation(
                out=xr[i][:, t, lo:hi], in_=x8[i][:, t, lo:hi].bitcast(FP8), func=ACT.Copy, scale=xs[i][:, t : t + 1]
            )

        def by_column(i, lo, hi):
            return xr[i][:, :, lo:hi].rearrange("p t d -> p d t")

        def runs_in(i, lo, hi, run):
            return xr[i][:, :, lo:hi].rearrange("p t (c e) -> p c t e", e=run)

        def runs_out(i, lo, hi, run):
            return xi[i][:, 4 * lo : 4 * hi].rearrange("p (c e t) -> p c t e", e=run, t=4)

        def weave(i, lo, hi):
            nc.gpsimd.tensor_scalar(
                out=runs_out(i, lo, hi, FETCH),
                in0=runs_in(i, lo, hi, FETCH),
                scalar1=1.0,
                scalar2=0.0,
                op0=MULT,
                op1=ADD,
            )

        def lace(i, lo, c, tag):
            if c == 0:
                xw[i] = psum.tile([P, 4 * LACED], BF16, name=f"xw{i}", tag=tag, bufs=1)
            nc.tensor.matmul(
                xw[i][:, 4 * c : 4 * (c + P)], lhsT=ident_h[:], rhs=by_column(i, lo + c, lo + c + P), start=True, stop=True
            )

        def empty_lace(i, lo, width=LACED):
            nc.scalar.copy(out=xi[i][:, 4 * lo : 4 * (lo + width)], in_=xw[i][:, 0 : 4 * width])

        def join_rows(i, lo, hi):
            nc.scalar.copy(out=runs_out(i, lo, hi, LINE), in_=runs_in(i, lo, hi, LINE))

        def new_xi(i):
            xi[i] = pool.tile([P, D * 4], BF16, name=f"xi{i}", tag="xi", bufs=1, align_bytes=64)

        def braid(i, lo, hi):
            nc.vector.tensor_copy(out=runs_out(i, lo, hi, LINE), in_=runs_in(i, lo, hi, LINE))

        def q_x(i, lo, hi):
            s = slice(lo, hi)
            nc.vector.quantize_mx(
                out=xq[:, i, s].bitcast(FP8X4), scales=xqs[:, i, s], in_=xi[i][:, 4 * lo : 4 * hi]
            )

        def mm2(i, b):
            if i == 0 and b < LIVE:
                gbank[b] = psum.tile([P, BANK], F32, name=f"g{b}", tag=f"g{b}", bufs=1)
            for j in (2 * b, 2 * b + 1):
                nc.tensor.matmul_mx(
                    out=gbank[b][:, F * (j % 2) : F * (j % 2 + 1)],
                    lhsT=xq[:, i, P * j : P * (j + 1)].bitcast(FP8X4),
                    lhsT_scale=xqs[:, i, P * j : P * (j + 1)],
                    rhs=daq[:, i, :].bitcast(FP8X4),
                    rhs_scale=daqs[:, i, :],
                    start=(i == 0 and j % 2 == 0),
                    stop=(i == NG - 1 and j % 2 == 1),
                )

        def turn_w2(h, tag):
            bank = psum.tile([P, NC, 2, P], F32, name=f"w2_{h}", tag=tag, bufs=1)
            words = w2r[:, h, :].bitcast(F32)
            for c in range(NC):
                for u in range(2):
                    nc.tensor.transpose(bank[:, c, u, :], words[:, WORDS * c + u : WORDS * (c + 1) : 2], ident[:])
            return bank

        def empty_w2(h, bank):
            dst = w2g[:].bitcast(F32).rearrange("q (c f u) -> q c f u", c=NC, u=2)
            nc.scalar.copy(out=dst[:, :, P * h : P * (h + 1), :], in_=bank[:].rearrange("q c u r -> q c r u"))

        def q_w2():
            nc.vector.quantize_mx(
                out=w2q[:].rearrange("p c f -> p (c f)").bitcast(FP8X4),
                scales=w2qs[:].rearrange("p c f -> p (c f)"),
                in_=w2g[:],
            )

        def warm_up(columns, tag, name):
            idle = psum.tile([P, BANK], F32, name=name, tag=tag, bufs=1)
            words = ac[0][:].bitcast(F32)
            nc.tensor.matmul(idle[:, 0:columns], lhsT=ident[:], rhs=words[:, 0:columns], start=True, stop=True)

        load_scale(0, nc.scalar)
        load_slots(0, 0, 1)
        load_a(0)
        load_slots(0, 1, 2)
        load_slots(0, 2, 4)
        load_dy(0, 0)
        load_dy(0, 1)
        load_a(1)
        nc.sync.dma_start(out=w2r[:], in_=w2.rearrange("(h p) d -> p h d", p=P))
        load_x(1)
        load_dy(1, 0)
        load_dy(1, 1)
        load_a(2)
        load_rows(w1t, w1)
        load_dy(2, 0)
        for k, n in enumerate(NODES):
            nc.vector.memset(offs[:, k : k + 1], n * GRID)
        nc.vector.memset(ones[:], 1.0)
        make_identity(nc, ident[:])
        nc.vector.tensor_copy(out=ident_h[:], in_=ident[:])
        nc.vector.tensor_scalar(out=minus_h[:], in0=ident[:], scalar1=-1.0, scalar2=None, op0=MULT)
        new_rows(0)
        new_xi(0)
        row_vector(0, 0, 0, D)
        clamp(0)
        load_a(3)
        load_x(2)
        load_dy(2, 1)
        gelu_slots(0, 0)
        gelu_slots(0, 1)
        for t in range(1, 4):
            row_vector(0, t, 0, D)
        braid(0, LACED_0, FIRST)
        warm_up(2 * WARM, "g2", "idle0")
        turn(0, 0, "g0")
        turn(0, 1, "g1")
        warm_up(WARM, "g2", "idle1")
        turn(0, 2, "a")
        turn(0, 3, "b")
        gelu_slots(0, 2)
        nc.vector.tensor_tensor(out=ge[0, 0][:], in0=ge[0, 0][:], in1=ge[0, 1][:], op=ADD)
        clamp(1)
        turn_a(1, "d")
        w2_banks = [turn_w2(h, "cx"[h]) for h in range(2)]
        for c in range(0, LACED_0, P):
            lace(0, 0, c, "g2")
        nc.vector.scalar_tensor_tensor(out=ge[0, 2][:], in0=ge[0, 2][:], scalar=-2.0, in1=ge[0, 0][:], op0=MULT, op1=ADD)
        for t in range(4):
            empty(0, t)
        gelu_turned(1, 0)
        empty_w2(0, w2_banks[0])
        empty_w2(1, w2_banks[1])
        gelu_turned(1, 1)
        warm_up(WARM, "a", "idle2")
        turn(1, 0, "g0")
        turn(1, 1, "g1")
        warm_up(WARM, "x", "idle3")
        turn(1, 2, "b")
        turn(1, 3, "c")
        braid(0, FIRST, D)
        q_dy(0)
        new_rows(1)
        row_vector(1, 3, 0, D)
        row_vector(1, 2, 0, D)
        q_w2()
        empty_lace(0, 0, LACED_0)
        for t in range(4):
            empty(1, t)
        mm1(0, 0, "a")
        mm1(0, 1, "d")
        row_scalar(1, 0, 0, D - REST)
        gelu_slots(1, 2)
        row_vector(1, 0, D - REST, D)
        row_vector(1, 1, 0, D)
        clamp(2)
        q_x(0, 0, D)
        q_dy(1)
        turn_a(2, "x")
        add_nodes(1, 0, "b")
        add_nodes(1, 1, "c")
        gram = psum.tile([P, P], F32, name="gram", tag="g2", bufs=1)
        w_gram(0, GRAM_HEAD)

        last = NG - 1
        for s in range(1, last - 1):
            if s + AHEAD + 1 < NG:
                load_a(s + AHEAD + 1)
            if s + AHEAD < NG:
                load_dy(s + AHEAD, 0)
                load_x(s + AHEAD)
                load_dy(s + AHEAD, 1)
            if s + AHEAD == last:
                load_rows(mt, m)
                load_rows(vt, v)
            new_xi(s)
            weave(s, 0, WOVEN)
            make_da(s - 1, 0)
            make_da(s - 1, 1)
            diff(s, 0)
            diff(s, 1)
            gelu_turned(s + 1, 0)
            gelu_turned(s + 1, 1)
            new_rows(s + 1)
            row_scalar(s + 1, 1, 0, D)
            if s == 2:
                nc.scalar.copy(out=wsum[:, 0:1], in_=tot[:, 0:1])
            lace(s, WOVEN, 0, "a")
            turn(s + 1, 0, "d")
            lace(s, WOVEN, P, "a")
            turn(s + 1, 1, "b")
            if s == 1:
                w_gram(GRAM_HEAD, 2 * NJ)
            turn(s + 1, 2, "c")
            turn(s + 1, 3, "x")
            empty_lace(s, WOVEN)
            for t in range(4):
                empty(s + 1, t)
            if s > 1:
                mm2(s - 2, 2)
            mm1(s, 0, "a")
            mm1(s, 1, "d")
            q_da(s - 1)
            clamp(s + 2)
            braid(s, ROWS, D)
            row_scalar(s + 1, 0, 0, LATE)
            gelu_slots(s + 1, 2)
            row_vector(s + 1, 0, LATE, D)
            for t in range(2, 4):
                row_vector(s + 1, t, 0, D)
            if s == 1:
                w_trace()
            q_x(s, 0, D)
            q_dy(s + 1)
            add_nodes(s + 1, 0, "b")
            turn_a(s + 2, "x")
            add_nodes(s + 1, 1, "c")
            if s == 1:
                tot = w_total()
            mm2(s - 1, 0)
            mm2(s - 1, 1)

        s = last - 1
        new_xi(s)
        weave(s, 0, WOVEN)
        make_da(s - 1, 0)
        make_da(s - 1, 1)
        diff(s, 0)
        diff(s, 1)
        gelu_turned(last, 0)
        gelu_turned(last, 1)
        lace(s, WOVEN, 0, "a")
        turn(last, 0, "d")
        lace(s, WOVEN, P, "a")
        turn(last, 1, "b")
        turn(last, 2, "c")
        turn(last, 3, "x")
        empty(last, 0)
        empty_lace(s, WOVEN)
        for t in range(1, 4):
            empty(last, t)
        q_da(s - 1)
        braid(s, ROWS, D)
        new_rows(last)
        row_vector(last, 3, 0, D)
        mm2(s - 2, 2)
        mm1(s, 0, "a")
        mm1(s, 1, "d")
        row_scalar(last, 0, 0, GATE)
        gelu_slots(last, 2)
        row_vector(last, 0, GATE, D - REST)
        for t in range(1, 3):
            row_vector(last, t, 0, D - REST)
        q_x(s, 0, 2 * F)
        q_dy(last)
        add_nodes(last, 0, "b")
        add_nodes(last, 1, "c")
        gbank[LIVE] = psum.tile([P, BANK], F32, name="g3", tag="x", bufs=1)
        mm2(s - 1, 0)

        xi[last] = pool.tile([P, D * 4], BF16, name="xi_last", tag="xi_last", bufs=1, align_bytes=64)
        weave(last, 0, D - REST)
        make_da(last - 1, 0)
        diff(last, 0)
        diff(last, 1)
        make_da(last - 1, 1)
        for t in range(3):
            row_scalar(last, t, D - REST, D)
        mm1(last, 0, "a")
        mm1(last, 1, "b")
        join_rows(last, D - REST, D)
        nc.scalar.activation(out=winv[:, 0:1], in_=wsum[:, 0:1], func=ACT.Abs_reciprocal_sqrt)
        make_da(last, 0)
        make_da(last, 1)
        mm2(s - 1, 1)
        mm2(last - 2, 2)
        for i in range(last - 1):
            mm2(i, LIVE)
        q_da(last - 1)
        q_x(last, 0, F)
        q_da(last)
        q_x(last, F, 2 * F)
        q_x(last, 2 * F, 3 * F)
        q_x(s, 2 * F, 3 * F)
        q_x(last, 3 * F, D)
        q_x(s, 3 * F, D)
        sq = pool.tile([P, NJ * F], F32, name="sq", tag="dyg", bufs=2, align_bytes=64)
        mn = pool.tile([P, NJ * F], F32, name="mn", tag="dyg", bufs=2, align_bytes=64)

        vn, mb, rb = {}, {}, {}
        spare = {1: "a", 2: "c", 3: "b"}

        def cols(b):
            return slice(BANK * b, BANK * (b + 1))

        def block(b, k):
            return slice(BANK * b + P * k, BANK * b + P * (k + 1))

        def square(b):
            nc.scalar.activation(out=sq[:, cols(b)], in_=gbank[b][:], func=ACT.Square, scale=NEW_SHARE**0.5 * G_SCALE)

        def first_moment(b):
            nc.vector.scalar_tensor_tensor(
                out=mn[:, cols(b)], in0=gbank[b][:], scalar=-NEW_SHARE * G_SCALE, in1=mt[:, cols(b)], op0=MULT, op1=SUB
            )

        def open_v(b):
            vn[b] = psum.tile([P, 4, P], F32, name=f"vn{b}", tag=spare[b], bufs=1)
            for k in range(4):
                nc.tensor.matmul(vn[b][:, k, :], lhsT=vt[:, block(b, k)], rhs=ident_h[:], start=(k == 0), stop=False)

        def add_turned(bank, src, b):
            for k in range(4):
                nc.tensor.matmul(
                    bank[:, k, :], lhsT=src[:, block(b, k)], rhs=ident[:], start=False, stop=(k == 3), is_transpose=True
                )

        def inv_root(b):
            nc.scalar.activation(
                out=sq[:, cols(b)],
                in_=vn[b][:].rearrange("p k q -> p (k q)"),
                func=ACT.Abs_reciprocal_sqrt,
                scale=1.0 / 60.0,
            )

        def turn_m(b):
            mb[b] = psum.tile([P, 4, P], F32, name=f"mb{b}", tag=f"g{b}" if b < LIVE else "x", bufs=1)
            for k in range(4):
                nc.tensor.transpose(mb[b][:, k, :], mn[:, block(b, k)], ident[:])

        def ratio(b):
            nc.vector.tensor_tensor(
                out=mn[:, cols(b)], in0=mb[b][:].rearrange("p k q -> p (k q)"), in1=sq[:, cols(b)], op=MULT
            )

        def open_r(b):
            rb[b] = psum.tile([P, 4, P], F32, name=f"rb{b}", tag=spare[b], bufs=1)
            nc.tensor.matmul(
                rb[b][:].rearrange("p k q -> p (k q)"), lhsT=minus_h[:], rhs=w1t[:, cols(b)], start=True, stop=False
            )

        def r_norm(b):
            nc.scalar.activation(
                out=sq[:, cols(b)],
                in_=rb[b][:].rearrange("p k q -> p (k q)"),
                func=ACT.Square,
                accum_out=rsum[:, b : b + 1],
            )

        def add_v(b):
            nc.gpsimd.tensor_tensor(out=sq[:, cols(b)], in0=sq[:, cols(b)], in1=vt[:, cols(b)], op=ADD)

        def inv_root_plain(b):
            nc.scalar.activation(out=sq[:, cols(b)], in_=sq[:, cols(b)], func=ACT.Abs_reciprocal_sqrt, scale=1.0 / 60.0)

        def ratio_plain(b):
            nc.vector.tensor_tensor(out=mn[:, cols(b)], in0=mn[:, cols(b)], in1=sq[:, cols(b)], op=MULT)

        def decay(b):
            nc.vector.tensor_tensor(out=mn[:, cols(b)], in0=mn[:, cols(b)], in1=w1t[:, cols(b)], op=SUB)

        def r_norm_vector(b):
            nc.vector.scalar_tensor_tensor(
                out=sq[:, cols(b)],
                in0=mn[:, cols(b)],
                scalar=1.0,
                in1=mn[:, cols(b)],
                op0=MULT,
                op1=MULT,
                accum_out=rsum[:, b : b + 1],
            )

        for b in range(NB):
            mm2(last - 1, b)
            mm2(last, b)
        for b in range(NB):
            square(b)
            if b == 0:
                add_v(b)
            first_moment(b)
        open_v(1)
        add_turned(vn[1], sq, 1)
        open_v(2)
        add_turned(vn[2], sq, 2)
        turn_m(1)
        open_v(3)
        add_turned(vn[3], sq, 3)
        turn_m(2)
        turn_m(3)
        inv_root(1)
        inv_root_plain(0)
        inv_root(2)
        inv_root(3)
        ratio(1)
        ratio_plain(0)
        ratio(2)
        ratio(3)
        decay(0)
        nc.vector.tensor_tensor(out=winv2[:, 0:1], in0=winv[:, 0:1], in1=winv[:, 0:1], op=MULT)
        for b in (1, 2, 3):
            open_r(b)
            add_turned(rb[b], mn, b)
        rtot = psum.tile([P, 8], F32, name="rtot", tag="g0", bufs=1)
        r_norm(1)
        r_norm(2)
        r_norm_vector(0)
        r_norm(3)
        for k, b in enumerate((1, 2, 0, 3)):
            nc.tensor.matmul(rtot[:, 0:1], lhsT=ones[:], rhs=rsum[:, b : b + 1], start=(k == 0), stop=(k == NB - 1))
        nc.scalar.activation(out=step[:, 0:1], in_=rtot[:, 0:1], func=ACT.Abs_reciprocal_sqrt, scale=winv2[:, 0:1])
        out_v = out.rearrange("(j p) f -> p j f", p=P)
        pieces = [(0, 1), (1, 2), (4, 6), (2, 4), (6, 7), (7, 8)]
        for lo, hi in pieces:
            c = slice(F * lo, F * hi)
            if lo // 2 in rb:
                src = rb[lo // 2][:].rearrange("p k q -> p (k q)")[:, F * (lo % 2) : F * (lo % 2 + hi - lo)]
            else:
                src = mn[:, c]
            res = pool.tile([P, (hi - lo) * F], F32, name=f"res{lo}", tag="dy", bufs=2 * (AHEAD + 1))
            nc.vector.scalar_tensor_tensor(out=res[:], in0=src, scalar=step[:, 0:1], in1=w1t[:, c], op0=MULT, op1=ADD)
            nc.sync.dma_start(out=out_v[:, lo:hi, :], in_=res[:].rearrange("p (j f) -> p j f", f=F))
